import numpy as np, ml_dtypes
CORES = [10,34,74,98]
N = 4
import mx_ref
BF = ml_dtypes.bfloat16
def gentries(a):
    return np.ascontiguousarray(a.reshape(8, 16, -1).transpose(0, 2, 1)).reshape(8, -1)
def gtable(e):
    e = np.asarray(e); return np.ascontiguousarray(e.reshape(8, -1, 16).transpose(0, 2, 1)).reshape(128, -1).astype(np.int32)
def gcols(t, e):
    v = np.concatenate([t.reshape(8, 16, -1, 4), np.zeros((8, 16, 1, 4), BF)], axis=2)
    return np.ascontiguousarray(np.stack([v[g][:, e[g]] for g in range(8)])).reshape(128, -1)
def tile(rs):
    return np.stack(rs, axis=2).reshape(128, -1).astype(BF)
def pick(q, e):
    c = np.concatenate([q[0].reshape(128, -1, 4), np.zeros((128, 1, 4), np.uint8)], axis=1); s = np.concatenate([q[1], np.ones((16, 1), np.uint8)], axis=1)
    return (np.ascontiguousarray(c[:, e].reshape(128, -1)), np.ascontiguousarray(s[:, e]))
def join(*qs):
    return (np.concatenate([q[0] for q in qs], axis=1), np.concatenate([q[1] for q in qs], axis=1))
def put(q, e, v):
    c, s = q[0].reshape(128, -1, 4).copy(), q[1].copy(); c[:, e] = v[0].reshape(128, -1, 4); s[:, e] = v[1]
    return (c.reshape(128, -1), s)
def pk(c, s):
    return (np.ascontiguousarray(c), mx_ref.live(s))
def emit(q):
    return q[0], q[1]
def packed(v, rng):
    q = [mx_ref.quantize(np.ascontiguousarray(v[r])) for r in range(N)]
    return np.stack([a for a, b in q]), np.stack([mx_ref.plane(b, rng) for a, b in q])
def values_of_codes():
    e, c = np.zeros((128, 128, 4), np.float32), np.zeros((128, 2, 4), np.uint8)
    e[np.arange(128), np.arange(128), 0] = 1
    c[:127, :, 0] = np.arange(256).reshape(2, 128).T[:127]
    return mx_ref.matmul(mx_ref.quantize(e.reshape(128, 512).astype(BF)), (c.reshape(128, 8), np.full((16, 2), 127, np.uint8))).T.reshape(-1).astype(np.float64)
CODE_VALUE, SCALE_VALUE = values_of_codes(), 2.0 ** (np.arange(256) - 127.0)
def decode(q):
    return (CODE_VALUE[q[0]].reshape(16, 8, -1, 4) * SCALE_VALUE[q[1]][:, None, :, None] + 0.0).reshape(128, -1).astype(np.float32)
def f(rng, *shape):
    return mx_ref.flush((rng.standard_normal(shape, dtype=np.float32) * np.exp2(rng.integers(-2, 3, shape[:-1] + (1,)))).astype(BF))
def wide(rng, *shape, cols=0):
    v = rng.standard_normal(shape, dtype=np.float32) * np.exp2(rng.integers(-12, 13, shape)).astype(np.float32)
    if cols: v *= np.repeat(np.exp2(rng.integers(-cols, cols + 1, shape[:-2] + (1, shape[-1] // 4))) * (rng.random(shape[:-2] + (1, shape[-1] // 4)) > 0.0625), 4, axis=-1).astype(np.float32)
    return mx_ref.flush(v.astype(BF))
C = 416
MASK = [1, 2, 3]
def numbers_of(rng):
    return {"x": np.array(f(rng, N, 128, 4 * C)), "u": np.array(f(rng, N, 128, 512)), "v": np.array(f(rng, N, 128, 512))}
def following(o):
    e = np.zeros_like(o)
    np.put_along_axis(e, o, np.roll(o, -1, axis=-1), axis=-1)
    return e
def rings(rng):
    return following(rng.permuted(np.tile(np.arange(C), (N, 8, 1)), axis=2))
def runs(rng, when, same=False):
    o, go = np.zeros((N, 8, C), np.int64), np.zeros((N, 8, C), bool)
    for r in range(N):
        k = rng.permutation(C)
        for g in range(8):
            p = r ^ MASK[when[g]]
            if p < r: continue
            if not same: k = rng.permutation(C)
            for i, m in ((r, [1, 0, 3, 2]), (p, [2, 0, 3, 1])):
                q = rng.permuted(k.reshape(4, -1), axis=1)[m]
                o[i, g] = np.concatenate([q[:2].T.reshape(-1), q[2:].T.reshape(-1)])
                go[i, g, q[:2].reshape(-1)] = True
    return following(o), go
def stored(e):
    return {"nx": np.stack([gtable(e[r]) for r in range(N)])}
def layers(rng, still=[]):
    w = np.array(f(rng, N, 128, 2048)).reshape(N, 8, 16, 4, 8, 16, 4)
    for i in still:
        w[:, :, i] = 0
        w[:, :, :, :, :, i] = 0
    return w
def weights(rng, w):
    c, s = packed(np.ascontiguousarray(w).reshape(N, 128, 2048), rng)
    return {"wc": c, "ws": s}
def setup_inputs(rng):
    return {**numbers_of(rng), **stored(rings(rng)), **weights(rng, layers(rng))}
def setup_inputs_ties(rng):
    d = numbers_of(rng)
    o = rng.permutation(N)
    k = rng.integers(-1, 2, (N, 8, C)).astype(np.float32)
    k[o[1]] = 1
    x = d["x"].reshape(N, 8, 16, C, 4)
    x[:, :, 0] = 0
    x[:, :, 0, :, 0] = k.astype(BF)
    c = np.ones(N, np.float32)
    c[o[0]] = 0
    c[o[2]] = -1
    u = d["u"].reshape(N, 128, 128, 4)
    u[:, :, ::16] = 0
    for h in range(0, 128, 16): u[:, h, h, 0] = c.astype(BF)
    e, i = rings(rng), np.arange(C)
    for r in range(N):
        p, h = r ^ MASK[0], rng.permutation(8)
        if p < r: continue
        e[p, h[0]] = e[r, h[0]]
        e[p, h[1]] = np.argsort(e[r, h[1]])
        e[r, h[2]], e[p, h[2]] = (i + 1) % C, (i - 1) % C
        e[r, h[3]] = e[p, h[3]] = (i + 1) % C
    w = layers(rng)
    w[:, :, :, :, :, :8] = 0
    return {"x": x.reshape(N, 128, 4 * C), "u": u.reshape(N, 128, 512), "v": d["v"], **stored(e), **weights(rng, w)}
def setup_inputs_near(rng):
    d = numbers_of(rng)
    o = rng.permutation(N) % 4
    k = np.where(o % 2 == 0, 1.0, 2.0 ** -30)
    x = np.zeros((N, 8, 16, C, 4))
    s = rng.integers(-1, 2, (N, 8, C)) * k[:, None, None]
    x[:, :, 0, :, 0] = 1.125 * s
    x[:, :, 1, :, 0] = -1.25 * s
    x[:, :, 8, :, 0] = rng.integers(-1, 2, (N, 8, C)) * 2.0 ** -27
    x[:, :, 8, :, 1] = 2.0 ** -27
    x[:, :, 9:] = (1.0 + rng.integers(0, 128, (N, 8, 7, C, 4)) * 2.0 ** -7) * 2.0 ** -27 * rng.choice([-1.0, 1.0], (N, 8, 7, C, 4))
    w = layers(rng, list(range(9)))
    for r in range(N):
        if o[r] % 2 == 1: x[r, :, 7, :, 0] = 2.0 ** -26
        if o[r] == 3:
            x[r, :, :2] = 0
            x[r, :, 7, :, 0] = 2.0 ** -27
            for g in range(8):
                w[r, g, 8, 0, g, 0, 0] = 2.0 ** -10
                w[r, g, 8, 0, g, 0, 1] = 2.0 ** -8
                w[r, g, 8, 0, g, 1, 0] = -2.0 ** -10
                w[r, g, 8, 0, g, 1, 1] = -1.125 * 2.0 ** -8
        else:
            at = [0, C - 1, int(rng.integers(C)), int(rng.integers(C))]
            for g, j in zip(rng.permutation(8)[:4], at): x[r, g, 0, j, 0] = 2.0 ** 30 * rng.choice([-1.0, 1.0])
    u = d["u"].reshape(N, 128, 128, 4)
    u[:, :, ::16] = 0
    for h in range(0, 128, 16):
        u[:, h, h, 0] = (1.125 * k).astype(np.float32).astype(BF)
        u[:, h + 1, h, 0] = k.astype(np.float32).astype(BF)
    return {"x": x.astype(np.float32).reshape(N, 128, 4 * C).astype(BF), "u": u.reshape(N, 128, 512), "v": d["v"], **stored(rings(rng)), **weights(rng, w)}
def setup_inputs_runs(rng):
    d = numbers_of(rng)
    o = rng.permutation(8)
    when = np.zeros(8, np.int64)
    when[o[4:6]] = 1
    when[o[6:]] = 2
    e, go = runs(rng, when)
    low = -rng.integers(0, 2, (N, 8, C))
    t = np.where(go, 1, low)
    for r in range(N):
        h = rng.permutation(o[:4])
        t[r, h[0]] = 1
        t[r, h[1]] = low[r, h[1]]
    for g in o[4:]:
        for i in range(when[g]): t[:, g] = np.take_along_axis(t[:, g], e[:, g], axis=1)
    x = (1.0 + (2 * rng.integers(0, 64, (N, 16, 8, C, 4)) + 1) * 2.0 ** -7) * np.exp2(-rng.integers(0, 7, (N, 16, 8, C, 4)).astype(np.float64)) * rng.choice([-1.0, 1.0], (N, 16, 8, C, 4))
    c = rng.choice([-1.0, 1.0], (N, 16, 1))
    k = np.exp2(when - 8.0)[:, None]
    x[:, :, 0, :, 0] = np.where(rng.random((N, 16, C)) < 0.5, 1.96875, 1.875) * 2.0 ** 8 * c
    x[:, :, 3, :, 0] = 1.875 * 2.0 ** 7
    x[:, ::2, 1, :, 0] = (8 + t) * k
    x[:, ::2, 2, :, 0] = 8 * k
    u = d["u"].reshape(N, 128, 128, 4)
    u[:, :, ::16] = 0
    for h in range(0, 128, 16):
        u[:, h + 1, h, 0] = 1
        u[:, h + 2, h, 0] = -1
    w = layers(rng, [0, 3, 8, 11])
    for g in range(8):
        for i in (0, 1):
            w[:, g, 8 * i + 3, 0, g, 8 * i, 0] = (64 * c[:, 2 * g + i, 0]).astype(np.float32).astype(BF)
            w[:, g, 8 * i + 3, 0, g, 8 * i + 3, 0] = 32
    for g in o[4:]:
        x[:, 2 * g, 4, :, 0] = -1.0
        x[:, 2 * g, 5, :, 0] = 1.0 - when[g]
        u[:, 16 * g + 4, 16 * g, 0] = 1
        for i in (1, 2, 4, 5): w[:, :, :, :, g, i] = 0
        w[:, g, 4, 0, g, 4, 0] = -32
        w[:, g, 5, 0, g, 4, 0] = 64
        w[:, g, 5, 0, g, 5, 0] = -32
    return {"x": x.astype(np.float32).reshape(N, 128, 4 * C).astype(BF), "u": u.reshape(N, 128, 512), "v": d["v"], **stored(e), **weights(rng, w)}
def setup_inputs_ends(rng):
    d = numbers_of(rng)
    e, go = runs(rng, np.zeros(8, np.int64), True)
    o = rng.permutation(N) % 4
    s = go[:, 0] * 2.0 - 1.0
    small = (1.0 + 0.125 * rng.integers(0, 8, (N, 8, 16, C, 4))) * 2.0 ** -20
    x = (0.9 + 0.1 * rng.random((N, 8, 16, C, 4))) * 2.0 ** 30
    u = d["u"].astype(np.float32).reshape(N, 128, 128, 4)
    v = np.zeros((N, 128, 512), np.float32)
    w = np.zeros((N, 128, 4, 128, 4), np.float32)
    i = np.arange(128)
    for r in range(N):
        if o[r] == 0: x[r] *= s[r][:, None]
        if o[r] == 1: x[r] *= -1
        if o[r] == 2: x[r] *= rng.choice([-1.0, 1.0], (8, 1, C, 1))
        if o[r] == 3: x[r] = small[r] * s[r][:, None]
        x[r, 7, 8:] = small[r, 7, 8:] * rng.choice([-1.0, 1.0], (8, C, 4))
        c = np.array([0.0, 1, 1, 1, -1, -1, -1, -1])[rng.permutation(8)][None, :, None]
        if o[r] < 3: u[r, :, ::16] = c * (0.9 + 0.1 * rng.random((128, 8, 4))) * 2.0 ** 30
        else: u[r, :, ::16] = c * (1.0 + 0.125 * rng.integers(0, 8, (128, 8, 4))) * 2.0 ** -30
        if o[r] < 2: v[r] = (0.9 + 0.1 * rng.random((128, 512))) * 2.0 ** 30
        else: v[r] = (1.0 + 0.125 * rng.integers(0, 8, (128, 512))) * 2.0 ** -30
        v[r] *= rng.choice([-1.0, 1.0], (128, 512))
        k = np.full(128, 32.0)
        if o[r] == 3: k = np.where(i < 120, 2.0 ** -8, 2.0 ** 8)
        for b in range(4): w[r, i, b, i, b] = k
    return {"x": x.astype(np.float32).reshape(N, 128, 4 * C).astype(BF), "u": u.reshape(N, 128, 512).astype(BF), "v": v.astype(BF), **stored(e), **weights(rng, w.astype(BF))}
def setup_inputs_spread(rng):
    d = setup_inputs(rng)
    d["x"] = wide(rng, N, 128, 4 * C, cols=6)
    return d
def check_inputs(d):
    b = []
    for k in ("x", "u", "v"):
        a = np.abs(d[k].astype(np.float32))
        if not (np.isfinite(a).all() and ((a == 0) | (a >= 2.0 ** -30) & (a <= 2.0 ** 30)).all()): b.append("a value of " + k)
    if not ((d["nx"] >= 0) & (d["nx"] < C)).all(): b.append("an entry of nx")
    else:
        e = np.concatenate([gentries(d["nx"][r]) for r in range(N)])
        at, back = np.zeros(8 * N, np.int64), np.zeros(8 * N, np.int64)
        for i in range(1, C + 1):
            at = e[np.arange(8 * N), at]
            back = np.where((at == 0) & (back == 0), i, back)
        if not (back == C).all(): b.append("a ring of nx")
    none, least, most = [emit(mx_ref.quantize(np.full((128, 16), k, np.float32).astype(BF)))[1][0, 0] for k in (0.0, 2.0 ** -8, 2.0 ** 8)]
    for r in range(N):
        if ((d["wc"][r] == 0x7F) | (d["wc"][r] == 0xFF)).any(): b.append("wc: a code that is no number")
        s = mx_ref.live(d["ws"][r])
        if ((s != none) & ((s < least) | (s > most))).any(): b.append("ws: a scale out of range")
    return b
def at(a, e):
    return np.take_along_axis(a, e, axis=1)
def mean(a, b):
    return ((a.astype(np.float32) + b.astype(np.float32)) * np.float32(0.5)).astype(BF)
def reference(x, u, v, nx, wc, ws):
    qu = [mx_ref.quantize(u[r]) for r in range(N)]
    lay = [pk(wc[r], ws[r]) for r in range(N)]
    ring = [gentries(nx[r]).astype(np.int64) for r in range(N)]
    now = [x[r] for r in range(N)]
    for m in MASK:
        t, new, back, z = [], [], [], []
        for r in range(N):
            q = mx_ref.quantize(now[r])
            t.append(decode(q).astype(BF))
            up = mx_ref.matmul(qu[r], q)[::16] > 0
            guest = ring[r ^ m]
            host = np.argsort(guest, axis=1)
            leave = up & ~at(up, host)
            a = ring[r]
            for i in range(8):
                a = np.where(at(leave, a), at(a, a), a)
            new.append(np.where(leave, at(a, host), np.where(at(leave, guest), guest, a)))
            back.append(np.argsort(new[r], axis=1))
            z.append(mx_ref.quantize(mean(gcols(t[r], new[r]), gcols(t[r], back[r]))))
        for r in range(N):
            h = tile([mx_ref.matmul(pick(lay[r], np.arange(128 * b, 128 * b + 128)), z[r ^ m]) * np.float32(0.03125) for b in range(4)])
            now[r] = mean(gcols(t[r], back[r]), gcols(h, new[r]))
        ring = new
    y, nr = np.zeros((N, 128, C), np.float32), np.zeros((N, 8, C), np.float32)
    oc, osc = np.zeros((N, 128, 4 * C), np.uint8), np.zeros((N, 16, C), np.uint8)
    for r in range(N):
        q = mx_ref.quantize(now[r])
        y[r] = mx_ref.matmul(mx_ref.quantize(v[r]), q)
        nr[r] = ring[r]
        oc[r], osc[r] = emit(q)
    return {"y": y, "nr": nr, "oc": oc, "osc": osc}

@@ -1,0 +1,496 @@
+from concourse.mybir import dt, AluOpType, AxisListType, ActivationFunctionType
+
+ADD, SUB, MUL, MAX = AluOpType.add, AluOpType.subtract, AluOpType.mult, AluOpType.max
+GT, EQ, NE = AluOpType.is_gt, AluOpType.is_equal, AluOpType.not_equal
+COPY, IDENT = ActivationFunctionType.Copy, ActivationFunctionType.Identity
+C = 416
+K = C // 16
+MASKS = [1, 2, 3]
+HALF = [(0, 288), (288, 416)]
+CHUNK = [(4, 0, 16, 16), (5, 0, 32, 32), (6, 0, 64, 64), (7, 0, 128, 128), (7, 128, 256, 256), (7, 256, 288, 384)]
+
+
+def layout(items):
+    at, n = {}, 0
+    for name, w in items:
+        at[name] = (n, w)
+        n += (w + 15) // 16 * 16
+    return at, n
+
+
+_rb = [(k, C) for k in ("mask", "hm", "cx", "one", "two", "iota", "t16", "om", "os", "W0")]
+_rb += [("%s%d" % (k, s), C) for s in range(1, 8) for k in "WMS"]
+_rb += [("mb%d" % s, 16) for s in range(4)] + [("og%d" % s, 16) for s in range(4)] + [("ds%d" % s, 16) for s in range(4)] + [("cp", 16)]
+_rb += [("%s_%d" % (k, r), 432) for r in (1, 2, 3) for k in ("up", "sg", "g", "l", "ls", "so", "go", "PB", "pm", "ps", "OB", "am", "as", "rR", "hm", "hs")]
+RB, NRB = layout(_rb)
+_ru = [("G%d" % s, K) for s in range(1, 8)] + [("OG0", K), ("pick", 8)] + [("q%d" % s, 1) for s in range(5)]
+_ru += [("%s_%d" % (k, r), K) for r in (1, 2, 3) for k in ("x", "sc", "ai", "bi", "og")]
+RU, NRU = layout(_ru)
+_rf = [(k, C) for k in ("i1024", "w0", "w0s", "rr", "rrs", "hf", "hfs", "nr")]
+_rf += [("p16", 1), ("pw", 16), ("bit", 4), ("f0", 1), ("rG0", K), ("hd", K)] + [("fo%d" % s, 16) for s in range(4)]
+_rf += [("%s_%d" % (k, r), C) for r in (1, 2, 3) for k in ("bf", "bs", "of", "os")]
+_rf += [("%s_%d" % (k, r), K) for r in (1, 2, 3) for k in ("t2", "t3", "lG", "rG", "rH", "dG")]
+RF, NRF = layout(_rf)
+RI, NRI = layout([("nx", K), ("p", 1), ("p16", 1), ("bit", 4), ("pick", 8)])
+WHERE = {"rb": RB, "ru": RU, "rf": RF, "ri": RI}
+
+X4, U8, BF = "float8_e4m3fn_x4", "uint8", "bfloat16"
+SCRATCH = {
+    "rb": ("sbuf", [128, NRB], BF), "ru": ("sbuf", [128, NRU], "uint16"), "rf": ("sbuf", [128, NRF], "float32"), "ri": ("sbuf", [128, NRI], "int32"),
+    "et": ("sbuf", [128, 528], BF), "qe": ("sbuf", [128, 512], X4), "se": ("sbuf", [128, 512], U8),
+    "uin": ("sbuf", [128, 512], BF), "qu": ("sbuf", [128, 128], X4), "su": ("sbuf", [128, 128], U8),
+    "u2": ("sbuf", [128, 128], X4), "s2": ("sbuf", [128, 128], U8),
+    "vin": ("sbuf", [128, 512], BF), "qv": ("sbuf", [128, 128], X4), "sv": ("sbuf", [128, 128], U8),
+    "wq": ("sbuf", [128, 512], X4), "wp": ("sbuf", [128, 512], U8),
+    "yo": ("sbuf", [128, C], "float32"),
+    "psA": ("psum", [128, 2048], "float32"), "psB": ("psum", [128, 2048], "float32"),
+    "L0": ("sbuf", [128, 2 * K], "uint16"),
+    "xt0": ("sbuf", [128, 4 * C], BF), "xq0": ("sbuf", [128, C], X4), "xs0": ("sbuf", [128, C], U8),
+}
+for _r in (1, 2, 3):
+    for _n in ("th", "tp", "za", "zt", "hh", "tb", "xt"):
+        SCRATCH["%s%d" % (_n, _r)] = ("sbuf", [128, 4 * C], BF)
+    for _n in ("xq", "lq", "zq"):
+        SCRATCH["%s%d" % (_n, _r)] = ("sbuf", [128, C], X4)
+    for _n in ("xs", "lp", "zs"):
+        SCRATCH["%s%d" % (_n, _r)] = ("sbuf", [128, C], U8)
+    for _n in ("L", "LN", "LZ"):
+        SCRATCH["%s%d" % (_n, _r)] = ("sbuf", [128, 2 * K], "uint16")
+SEMAPHORES = ["cv", "cs", "ct", "cg", "dnx", "dx", "du", "dv", "dwc", "dws", "dout", "lsem"] + ["%s%d" % (k, r) for r in (1, 2, 3) for k in ("aN", "aZ", "aQ")]
+
+
+def rank_program(g, core, T, topo):
+    rank = T.rank_of(core)
+    if rank is None:
+        return
+    eng = {"v": g.vector, "s": g.scalar, "t": g.tensor, "g": g, "y": g.sync}
+    known = {q: {} for q in eng}
+    count = {q: 0 for q in eng}
+    clocks, wr, rd, total = {}, {}, {}, {}
+
+    def over(a, b):
+        return a[1] < b[2] and b[1] < a[2]
+
+    def learn(q, sem, n):
+        for k, v in list(clocks.get((sem, n), {}).items()) + [(sem, n)]:
+            if known[q].get(k, 0) < v:
+                known[q][k] = v
+
+    def sync(q, reads, writes):
+        need = {}
+        for r in reads:
+            for reg, ev in wr.get(r[0], []):
+                if over(reg, r):
+                    need[ev] = 1
+            if r[0][:2] == "ps":
+                for reg, ev in rd.get(r[0], []):
+                    if over(reg, r) and ev[0] != "c" + q:
+                        need[ev] = 1
+        for w in writes:
+            for reg, ev in wr.get(w[0], []) + rd.get(w[0], []):
+                if over(reg, w):
+                    need[ev] = 1
+        for sem, n in sorted(need, key=lambda e: -len(clocks.get(e, {})) * 100000 - e[1]):
+            if known[q].get(sem, 0) < n:
+                eng[q].wait_ge(T.sem[sem], n)
+                learn(q, sem, n)
+
+    def mark(ev, q, reads, writes):
+        clocks[ev] = dict(known[q]) if q else {}
+        for w in writes:
+            wr[w[0]] = [e for e in wr.get(w[0], []) if not (w[1] <= e[0][1] and e[0][2] <= w[2])] + [(w, ev)]
+            rd[w[0]] = [e for e in rd.get(w[0], []) if not (w[1] <= e[0][1] and e[0][2] <= w[2])]
+        for r in reads:
+            rd.setdefault(r[0], []).append((r, ev))
+
+    def op(q, f, reads, writes):
+        sync(q, reads, writes)
+        count[q] += 1
+        sem = "c" + q
+        f().then_inc(T.sem[sem], 1)
+        total[sem] = count[q]
+        mark((sem, count[q]), q, reads, writes)
+
+    def dma(q, sem, out, in_, reads, writes):
+        sync(q, reads, writes)
+        eng[q].dma_start(out, in_).then_inc(T.sem[sem], 16)
+        total[sem] = total.get(sem, 0) + 16
+        mark((sem, total[sem]), q, reads, writes)
+
+    def A(buf, a, b, step=1):
+        return (T[buf][:, a:b] if step == 1 else T[buf][:, a:b:step], [(buf, a, b)])
+
+    def N(buf, name, a=0, b=None):
+        o, w = WHERE[buf][name]
+        return A(buf, o + a, o + (w if b is None else b))
+
+    def ends(buf, name, n=C):
+        o = WHERE[buf][name][0]
+        return A(buf, o + 15, o + n, 16)
+
+    def ind(w, o):
+        return (w[0].indirect(o[0]), w[1] + o[1])
+
+    def P(buf, bank, n):
+        return (T[buf][:, 512 * bank:512 * bank + n], [(buf, 512 * bank, 512 * bank + 512)])
+
+    def plane(buf, b, a=0, e=C):
+        return A(buf, C * b + a, C * b + e)
+
+    def strip(buf, b, a, e):
+        return (T[buf][:, 4 * a + b:4 * e:4], [("%s#%d" % (buf, b), a, e)])
+
+    def tt(out, a, b, o):
+        op("v", lambda: g.vector.tensor_tensor(out[0], a[0], b[0], o), a[1] + b[1], out[1])
+
+    def ts(out, a, s1, o1, s2=None, o2=None):
+        regs = list(a[1])
+        if isinstance(s1, tuple):
+            regs += s1[1]
+            s1 = s1[0]
+        if isinstance(s2, tuple):
+            regs += s2[1]
+            s2 = s2[0]
+        if o2 is None:
+            op("v", lambda: g.vector.tensor_scalar(out[0], a[0], s1, None, o1), regs, out[1])
+        else:
+            op("v", lambda: g.vector.tensor_scalar(out[0], a[0], s1, s2, o1, o2), regs, out[1])
+
+    def vcopy(out, a):
+        op("v", lambda: g.vector.tensor_copy(out[0], a[0]), a[1], out[1])
+
+    def act(out, a, scale=1.0, bias=0.0):
+        if bias == 0.0 and scale == 1.0:
+            op("s", lambda: g.scalar.activation(out[0], a[0], COPY), a[1], out[1])
+        else:
+            op("s", lambda: g.scalar.activation(out[0], a[0], IDENT, bias=bias, scale=scale), a[1], out[1])
+
+    def scan(out, a, b, init, o1, o2):
+        regs = a[1] + b[1]
+        if isinstance(init, tuple):
+            regs = regs + init[1]
+            init = init[0]
+        op("v", lambda: g.vector.tensor_tensor_scan(out[0], a[0], b[0], init, o1, o2), regs, out[1])
+
+    def memset(out, v):
+        op("v", lambda: g.vector.memset(out[0], v), [], out[1])
+
+    def iota(out, pattern, base, cm):
+        op("g", lambda: g.iota(out[0], pattern, base, cm, allow_small_or_imprecise_dtypes=True), [], out[1])
+
+    def quant(q, s, tile, a, e, t0=None):
+        regs = [("%s#%d" % (tile, b), a, e) for b in range(4)] if t0 is None else [(tile, t0, t0 + 4 * (e - a))]
+        i0 = 4 * a if t0 is None else t0
+        op("v", lambda: g.vector.quantize_mx(T[q][:, a:e], T[s][:, a:e], T[tile][:, i0:i0 + 4 * (e - a)]), regs, [(q, a, e), (s, a, e)])
+
+    def mm(out, lq, ls, la, rq, rs, a, e):
+        op("t", lambda: g.tensor.matmul_mx(out[0], T[lq][:, la:la + 128], T[ls][:, la:la + 128], T[rq][:, a:e], T[rs][:, a:e], True, True),
+           [(lq, la, la + 128), (ls, la, la + 128), (rq, a, e), (rs, a, e)], out[1])
+
+    def peer(m):
+        return T.cores[rank ^ m]
+
+    def send(dst, sem, pairs, regs):
+        rid, pid = topo.addr(dst)[:2]
+        mask = topo.mask(core, dst)
+        n = len(topo.engines(core, dst))
+        sync("g", regs, [])
+        for out, in_ in pairs:
+            g.remote_dma(out, in_, T.sem[sem], T.sem.lsem, pid, rid, mask)
+            total["lsem"] = total.get("lsem", 0) + n
+
+    def arrives(src, sem, k, regs):
+        n = k * len(topo.engines(src, core))
+        total[sem] = n
+        mark((sem, n), None, [], regs)
+
+    def send_lists(src, dst_buf, sem, m):
+        send(peer(m), sem, [(T[dst_buf][:, 0:2 * K], T[src][:, 0:2 * K])], [(src, 0, 2 * K)])
+        arrives(peer(m), sem, 1, [(dst_buf, 0, 2 * K)])
+
+    def send_state(r, m):
+        xq, xs, lq, lp = "xq%d" % (r - 1), "xs%d" % (r - 1), "lq%d" % r, "lp%d" % r
+        send(peer(m), "aQ%d" % r, [(T[lq][:, 0:C].bitcast(dt.uint8), T[xq][:, 0:C].bitcast(dt.uint8)), (T[lp][:, 0:C], T[xs][:, 0:C])], [(xq, 0, C), (xs, 0, C)])
+        arrives(peer(m), "aQ%d" % r, 2, [(lq, 0, C), (lp, 0, C)])
+
+    def scores(r):
+        for i, (a, e) in enumerate(HALF):
+            for k in (0, 2):
+                mm(P("psB", i + k, e - a), "u2", "s2", 0, "xq%d" % (r - 1), "xs%d" % (r - 1), a, e)
+
+    def unpack(ps, q, s):
+        for b in range(4):
+            mm(P(ps, b, C), "qe", "se", 128 * b, q, s, 0, C)
+
+    def halves(ps, dst):
+        for b in range(4):
+            act(plane(dst, b), P(ps, b, C), scale=0.5)
+
+    mask, hm, io = N("rb", "mask"), N("rb", "hm"), N("rb", "iota")
+
+    def settle(m, s, n=C):
+        scan(N("rb", s, 0, n), N("rb", "hm", 0, n), N("rb", m, 0, n), 0.0, MUL, ADD)
+
+    def settle_max(*jobs):
+        for buf, src, dst, out, shift in jobs:
+            hold(buf, src, dst)
+        for buf, src, dst, out, shift in jobs:
+            ts(out, ends(buf, dst), N("rf", "pw", 15, 16), MUL, shift, ADD)
+
+    def hold(buf, src, dst):
+        scan(N(buf, dst, 0, C), N("rb", "cx"), N(buf, src, 0, C), 0.0, MUL, MAX)
+
+    dma("y", "dnx", N("ri", "nx")[0], T.nx[:], [], N("ri", "nx")[1])
+    dma("s", "dx", T.xt0[:], T.x[:], [], [("xt0", 0, 4 * C)])
+    dma("y", "du", T.uin[:], T.u[:], [], [("uin", 0, 512)])
+    dma("y", "dwc", T.wq[:].bitcast(dt.uint8), T.wc[:], [], [("wq", 0, 512)])
+    dma("y", "dws", T.wp[:], T.ws[:], [], [("wp", 0, 512)])
+    dma("y", "dv", T.vin[:], T.v[:], [], [("vin", 0, 512)])
+
+    op("g", lambda: g.iota(N("ri", "p")[0], [[0, 1]], 0, 1), [], N("ri", "p")[1])
+    iota(N("rb", "t16"), [[0, K], [1, 16]], 0, 0)
+    op("g", lambda: g.iota(N("ri", "pick")[0], [[16, 8]], 0, 0), [], N("ri", "pick")[1])
+    memset(N("rb", "one"), 1.0)
+    memset(N("rf", "f0"), -208.0)
+    memset(N("ru", "q0"), 0)
+    scan(N("rf", "i1024"), N("rb", "one"), N("rb", "one"), 1023.0, MUL, ADD)
+    act(io, N("rf", "i1024"), bias=-1232.0)
+    act(N("rb", "two"), N("rb", "one"), scale=2.0)
+    ts(N("ri", "p16"), N("ri", "p"), 15, AluOpType.bitwise_and)
+    for s in range(4):
+        ts(N("ri", "bit", s, s + 1), N("ri", "p"), s, AluOpType.logical_shift_right, 1, AluOpType.bitwise_and)
+    vcopy(N("rf", "p16"), N("ri", "p16"))
+    vcopy(N("rf", "bit"), N("ri", "bit"))
+    vcopy(N("ru", "pick"), N("ri", "pick"))
+    ts(N("rb", "mask"), N("rb", "t16"), N("rf", "p16"), EQ)
+    ts(N("rb", "cp"), N("rb", "t16", 0, 16), N("rf", "p16"), GT, 0.5, MUL)
+    act(hm, N("rb", "mask"), scale=-1.0, bias=1.0)
+    ts(N("rb", "cx"), N("rb", "t16"), N("rf", "p16"), GT, 2.0, MUL)
+    scan(N("rf", "pw"), N("rb", "cp"), N("rb", "mask", 0, 16), 0.0, MUL, ADD)
+    for s in range(4):
+        act(N("rb", "ds%d" % s), N("rb", "one", 0, 16))
+
+    vcopy(A("L0", 0, K), N("ri", "nx"))
+    w0 = N("rf", "w0")
+    op("v", lambda: g.vector.tensor_copy(w0[0].indirect(T.L0[:, 0:K]), N("rf", "i1024")[0]), N("rf", "i1024")[1] + [("L0", 0, K)], w0[1])
+    act(N("rb", "W0"), w0, bias=-1232.0)
+    hold("rf", "w0", "w0s")
+    for s in range(4):
+        ts(N("rb", "mb%d" % s), N("rb", "mask", 0, 16), N("rf", "bit", s, s + 1), MUL)
+    ts(A("L0", K, 2 * K), ends("rf", "w0s"), N("rf", "pw", 15, 16), MUL, -1024.0, ADD)
+    for s in range(4):
+        ts(N("rb", "ds%d" % s, 0, 1), N("rf", "bit", s, s + 1), -1.0, MUL, 1.0, ADD)
+    memset(A("et", 0, 515), 1.0)
+    op("g", lambda: g.affine_select(T.et[:, 0:515], T.et[:, 0:515], [[1, 515]], EQ, 0.0, -3, -4), [("et", 0, 515)], [("et", 0, 515)])
+    send_lists("L0", "LN1", "aN1", MASKS[0])
+
+    def first_x():
+        quant("xq0", "xs0", "xt0", 0, C, 0)
+        send_state(1, MASKS[0])
+
+    def first_u():
+        quant("qu", "su", "uin", 0, 128, 0)
+        pk = N("ru", "pick")
+        op("v", lambda: g.vector.tensor_copy(T.u2[:, 0:128].bitcast(dt.uint32), T.qu[:, 0:128].bitcast(dt.uint32).indirect(pk[0])), [("qu", 0, 128)] + pk[1], [("u2", 0, 128)])
+        op("s", lambda: g.scalar.activation(T.s2[:, 0:128], T.su[:, 0:128].indirect(pk[0]), COPY), [("su", 0, 128)] + pk[1], [("s2", 0, 128)])
+
+    def constant(b):
+        op("v", lambda: g.vector.quantize_mx(T.qe[:, 128 * b:128 * b + 128], T.se[:, 128 * b:128 * b + 128], T.et[:, 3 - b:515 - b]), [("et", 0, 515)], [("qe", 128 * b, 128 * b + 128), ("se", 128 * b, 128 * b + 128)])
+
+    def up(r, i):
+        a, e = HALF[i]
+        ts(N("rb", "up_%d" % r, a, e), P("psB", i + 2, e - a), 0.0, GT)
+        out, ps = N("rb", "sg_%d" % r, a, e), P("psB", i, e - a)
+        op("s", lambda: g.scalar.activation(out[0], ps[0], ActivationFunctionType.Sign), ps[1], out[1])
+
+    def chunk(c, part):
+        s, a, e, to = CHUNK[c]
+        n = e - a
+        if part == 0:
+            tt(N("rb", "om", to, to + n), ind(N("rb", "W%d" % s), N("ru", "OG0", a // 16, e // 16) if c else N("ru", "q4")), N("rb", "mask", 0, n), MUL)
+        if part == 1:
+            scan(N("rb", "os", to, to + n), N("rb", "hm", 0, n), N("rb", "om", to, to + n), 0.0, MUL, ADD)
+        if part == 2:
+            o = RB["os"][0]
+            ts(N("ru", "OG0", to // 16, to // 16 + n // 16), A("rb", o + to + 15, o + to + n, 16), 208.0, ADD)
+
+    for s in range(5):
+        src = A("L0", K, 2 * K) if s == 0 else N("ru", "G%d" % s)
+        w = N("rb", "W%d" % s)
+        small = s < 4
+        act(N("rb", "W%d" % (s + 1)), ind(w, src))
+        tt(N("rb", "M%d" % s if s else "om"), ind(w, src), mask, MUL)
+        if small:
+            tt(N("rb", "og%d" % s), ind(w, N("ru", "q%d" % s)), N("rb", "mb%d" % s), MUL)
+        else:
+            chunk(s - 4, 0)
+        if s:
+            settle("M%d" % s, "S%d" % s)
+        else:
+            settle("om", "os")
+        if small:
+            scan(N("rf", "fo%d" % s), N("rb", "ds%d" % s), N("rb", "og%d" % s), N("rf", "fo%d" % (s - 1), 15, 16) if s else N("rf", "f0"), MUL, ADD)
+        else:
+            chunk(s - 4, 1)
+        ts(N("ru", "G%d" % (s + 1)), ends("rb", "S%d" % s if s else "os"), 208.0, ADD)
+        if small:
+            ts(N("ru", "q%d" % (s + 1)), N("rf", "fo%d" % s, 15, 16), 208.0, ADD)
+            if s == 3:
+                vcopy(N("ru", "OG0", 0, 1), N("ru", "q4"))
+        else:
+            chunk(s - 4, 2)
+    act(N("rb", "W6"), ind(N("rb", "W5"), N("ru", "G5")))
+    act(N("rb", "M7"), ind(N("rb", "W6"), N("ru", "G5")))
+    act(N("rb", "W7"), ind(N("rb", "M7"), N("ru", "G5")))
+    for part in range(3):
+        chunk(1, part)
+    first_x()
+    for part in range(3):
+        chunk(2, part)
+    first_u()
+    scores(1)
+    for c in (3, 4, 5):
+        for part in range(3):
+            chunk(c, part)
+            if c < 5 and part < 2:
+                constant(2 * c - 6 + part)
+            if c == 5 and part < 2:
+                up(1, part)
+    unpack("psA", "xq0", "xs0")
+    rr = N("rf", "rr")
+    order = N("ru", "OG0")
+    op("v", lambda: g.vector.tensor_copy(rr[0].indirect(order[0]), N("rf", "i1024")[0]), N("rf", "i1024")[1] + order[1], rr[1])
+    act(N("rf", "hf"), ind(rr, A("LN1", K, 2 * K)))
+    rG = N("rf", "rG0")
+    hold("rf", "rr", "rrs")
+
+
+    for r in (1, 2, 3):
+        m = MASKS[r - 1]
+        L, LN, LZ = "L%d" % r, "LN%d" % r, "LZ%d" % r
+        nb = lambda k, a=0, b=C: N("rb", "%s_%d" % (k, r), a, b)
+        nu = lambda k: N("ru", "%s_%d" % (k, r))
+        nf = lambda k: N("rf", "%s_%d" % (k, r))
+        if r > 1:
+            up(r, 0)
+            up(r, 1)
+        tt(nb("g"), ind(nb("sg"), A(LN, 0, K)), nb("up"), GT)
+        act(nb("go"), ind(nb("g"), order))
+        if r == 1:
+            ts(rG, ends("rf", "rrs"), N("rf", "pw", 15, 16), MUL, -1231.0, ADD)
+        tt(nb("l"), ind(nb("g"), A(LN, K, 2 * K)), N("rb", "two"), ADD)
+        act(nb("so"), ind(nb("l"), order), scale=-1.0, bias=3.0)
+        lG = nf("lG")
+        left = ("rb", "l_%d" % r, "ls_%d" % r, lG, -2.0)
+        if r == 1:
+            settle_max(left, ("rf", "hf", "hfs", N("rf", "hd"), -1231.0))
+            tt(nf("dG"), N("rf", "hd"), rG, SUB)
+        else:
+            settle_max(left)
+        tt(nf("t2"), lG, nf("dG"), MUL)
+        tt(nf("t3"), nf("t2"), rG, ADD)
+        ts(nu("x"), nf("t3"), 207.0, ADD)
+        scan(nb("PB", 0, C), nb("so"), nb("go"), -208.0, ADD, ADD)
+        halves("psA", "th%d" % r)
+        if r == 1:
+            unpack("psB", "lq1", "lp1")
+            halves("psB", "tp1")
+        tt(nb("pm"), ind(nb("PB"), nu("x")), mask, MUL)
+        settle("pm_%d" % r, "ps_%d" % r)
+        tt(nf("rG"), ends("rb", "ps_%d" % r), lG, SUB)
+        rG = nf("rG")
+        ts(nu("sc"), rG, 208.0, ADD)
+        ts(nu("ai"), rG, 207.0, ADD)
+        ts(nu("bi"), rG, 209.0, ADD)
+        ob = nb("OB", 0, 417)
+        op("v", lambda: g.vector.tensor_copy(ob[0].indirect(nu("sc")[0]), io[0]), io[1] + nu("sc")[1], ob[1])
+        vcopy(nb("OB", 0, 1), nb("OB", 416, 417))
+        act(nb("OB", 417, 418), nb("OB", 1, 2))
+        tt(nb("am"), ind(nb("OB"), nu("ai")), mask, MUL)
+        act(nf("bf"), ind(nb("OB", 0, 418), nu("bi")), bias=1232.0)
+        settle("am_%d" % r, "as_%d" % r)
+        hold("rf", "bf_%d" % r, "bs_%d" % r)
+        ts(A(L, 0, K), ends("rb", "as_%d" % r), 208.0, ADD)
+        ts(A(L, K, 2 * K), ends("rf", "bs_%d" % r), N("rf", "pw", 15, 16), MUL, -1024.0, ADD)
+        send_lists(L, LZ, "aZ%d" % r, m)
+        if r < 3:
+            send_lists(L, "LN%d" % (r + 1), "aN%d" % (r + 1), MASKS[r])
+            act(nf("of"), nb("OB", 1, 417), bias=1232.0)
+            rr = nb("rR")
+            tt(rr, ind(nb("PB"), nu("x")), nb("l", 0, C), SUB)
+            ts(nf("rH"), rG, -2.0, ADD)
+            settle_max(("rf", "of_%d" % r, "os_%d" % r, nu("og"), -1024.0))
+            order = nu("og")
+        if r == 1:
+            quant("qv", "sv", "vin", 0, 128, 0)
+        else:
+            unpack("psB", "lq%d" % r, "lp%d" % r)
+            halves("psB", "tp%d" % r)
+        th, tp, tb, za, zt, hh, xt = ["%s%d" % (k, r) for k in ("th", "tp", "tb", "za", "zt", "hh", "xt")]
+        zq, zs, xq, xs = ["%s%d" % (k, r) for k in ("zq", "zs", "xq", "xs")]
+
+        for b in range(4):
+            if b in ((3,), (1, 2), (1, 2, 3))[r - 1]:
+                vcopy(plane(tb, b), ind(plane(th, b), A(L, K, 2 * K)))
+            elif (r, b) != (2, 3):
+                act(plane(tb, b), ind(plane(th, b), A(L, K, 2 * K)))
+        def pack_z(i):
+            a, e = HALF[i]
+            quant(zq, zs, zt, a, e)
+            for b in range(4):
+                mm(P("psB" if i else "psA", b, e - a), "wq", "wp", 128 * b, zq, zs, a, e)
+
+        for i, (a, e) in enumerate(HALF):
+            for b in range(4):
+                for a1, e1 in ((a, a + 96), (a + 96, e)) if (i, b) == (0, 0) else ((a, e),):
+                    act(plane(za, b, a1, e1), ind(plane(tp, b), A(LZ, a1 // 16, e1 // 16)))
+                    tt(strip(zt, b, a1, e1), ind(plane(tp, b), A(LZ, K + a1 // 16, K + e1 // 16)), plane(za, b, a1, e1), ADD)
+                if (i, b) == (1, 0):
+                    pack_z(0)
+        pack_z(1)
+        if r < 3:
+            tt(N("rb", "hm_%d" % (r + 1), 0, C), ind(rr, A("LN%d" % (r + 1), K, 2 * K)), mask, MUL)
+        a, e = HALF[0]
+        for b in range(4):
+            act(plane(hh, b, a, e), P("psA", b, e - a), scale=0.015625)
+        a, e = HALF[1]
+        for b in range(4):
+            if b % 2:
+                act(plane(hh, b, a, e), P("psB", b, e - a), scale=0.015625)
+            else:
+                ts(plane(hh, b, a, e), P("psB", b, e - a), 0.015625, MUL)
+        if r == 2:
+            act(plane(tb, 3), ind(plane(th, 3), A(L, K, 2 * K)))
+        if r == 3:
+            act(N("rf", "nr"), ind(nb("OB"), nu("ai")), bias=208.0)
+            dma("y", "dout", T.nr[:, :], T.rf[0:128:16, RF["nr"][0]:RF["nr"][0] + C], N("rf", "nr")[1], [])
+        def pack_x(i):
+            a, e = HALF[i]
+            quant(xq, xs, xt, a, e)
+            if r == 3:
+                mm(P("psA", i, e - a), "qv", "sv", 0, xq, xs, a, e)
+                dma("y", "dout", T.oc[:, 4 * a:4 * e], T[xq][:, a:e].bitcast(dt.uint8), [(xq, a, e)], [])
+                for k in range(4):
+                    dma("s" if i and k > 1 else "y", "dout", T.osc[4 * k:4 * k + 4, a:e], T[xs][32 * k:32 * k + 4, a:e], [(xs, a, e)], [])
+                if i:
+                    vcopy(A("yo", a, e), P("psA", i, e - a))
+                else:
+                    act(A("yo", a, e), P("psA", i, e - a))
+                dma("s", "dout", T.y[:, a:e], T.yo[:, a:e], [("yo", a, e)], [])
+
+        for i, (a, e) in enumerate(HALF):
+            for b in range(4):
+                tt(strip(xt, b, a, e), ind(plane(hh, b), A(L, a // 16, e // 16)), plane(tb, b, a, e), ADD)
+                if (i, b) == (1, 0):
+                    pack_x(0)
+        if r < 3:
+            settle("hm_%d" % (r + 1), "hs_%d" % (r + 1))
+        pack_x(1)
+        if r < 3:
+            send_state(r + 1, MASKS[r])
+            scores(r + 1)
+            unpack("psA", xq, xs)
+            tt(N("rf", "dG_%d" % (r + 1)), ends("rb", "hs_%d" % (r + 1)), nf("rH"), SUB)
+
+    for sem in sorted(total):
+        g.wait_ge(T.sem[sem], total[sem])

@@ -1,13 +1,16 @@
 from concourse.mybir import dt, AluOpType, AxisListType, ActivationFunctionType
 
 ADD, SUB, MUL, MAX = AluOpType.add, AluOpType.subtract, AluOpType.mult, AluOpType.max
-GT, EQ, NE = AluOpType.is_gt, AluOpType.is_equal, AluOpType.not_equal
-COPY, IDENT = ActivationFunctionType.Copy, ActivationFunctionType.Identity
+GT, LT, EQ = AluOpType.is_gt, AluOpType.is_lt, AluOpType.is_equal
+COPY, IDENT, SIGN = ActivationFunctionType.Copy, ActivationFunctionType.Identity, ActivationFunctionType.Sign
 C = 416
 K = C // 16
 MASKS = [1, 2, 3]
 HALF = [(0, 288), (288, 416)]
-CHUNK = [(4, 0, 16, 16), (5, 0, 32, 32), (6, 0, 64, 64), (7, 0, 128, 128), (7, 128, 256, 256), (7, 256, 288, 384)]
+CUT = 160
+TINY = 2.0 ** -93
+OWN_TB = {1: (2, 3), 2: (2, 3), 3: (1, 2, 3)}
+LATE_TB = {1: (), 2: (1,), 3: ()}
 
 
 def layout(items):
@@ -18,18 +21,21 @@ def layout(items):
     return at, n
 
 
-_rb = [(k, C) for k in ("mask", "hm", "cx", "one", "two", "iota", "t16", "om", "os", "W0")]
-_rb += [("%s%d" % (k, s), C) for s in range(1, 8) for k in "WMS"]
-_rb += [("mb%d" % s, 16) for s in range(4)] + [("og%d" % s, 16) for s in range(4)] + [("ds%d" % s, 16) for s in range(4)] + [("cp", 16)]
-_rb += [("%s_%d" % (k, r), 432) for r in (1, 2, 3) for k in ("up", "sg", "g", "l", "ls", "so", "go", "PB", "pm", "ps", "OB", "am", "as", "rR", "hm", "hs")]
+_rb = [(k, C) for k in ("mask", "hm", "cx", "c4", "iota", "t16", "PE")] + [("cp", 16)]
+_rb += [("%s%d" % (k, s), 16) for s in (1, 2, 3) for k in ("mb", "ds")]
+_rb += [("%s_%d" % (k, r), 432) for r in (1, 2, 3) for k in ("sg", "sh", "g", "l", "ls", "so", "go", "OB", "am", "as")]
+_rb += [("PW_%d" % r, 2 * C) for r in (1, 2, 3)]
 RB, NRB = layout(_rb)
-_ru = [("G%d" % s, K) for s in range(1, 8)] + [("OG0", K), ("pick", 8)] + [("q%d" % s, 1) for s in range(5)]
+_ru = [("G%d" % s, K) for s in (2, 8, 32)] + [("OG0", K), ("pick", 8)] + [("q%d" % s, 1) for s in (1, 2, 3)]
 _ru += [("%s_%d" % (k, r), K) for r in (1, 2, 3) for k in ("x", "sc", "ai", "bi", "og")]
 RU, NRU = layout(_ru)
-_rf = [(k, C) for k in ("i1024", "w0", "w0s", "rr", "rrs", "hf", "hfs", "nr")]
-_rf += [("p16", 1), ("pw", 16), ("bit", 4), ("f0", 1), ("rG0", K), ("hd", K)] + [("fo%d" % s, 16) for s in range(4)]
-_rf += [("%s_%d" % (k, r), C) for r in (1, 2, 3) for k in ("bf", "bs", "of", "os")]
-_rf += [("%s_%d" % (k, r), K) for r in (1, 2, 3) for k in ("t2", "t3", "lG", "rG", "rH", "dG")]
+POWERS = (1, 2, 4, 6, 8, 16, 24, 32, 64, 96, 128, 160)
+_rf = [(k, C) for k in ("i1024", "w0", "w0s", "or", "os", "nr", "S2", "S8", "S32")] + [("W%d" % s, C) for s in POWERS]
+_rf += [("p16", 1), ("pw", 16), ("p4", 16), ("thr", 1), ("bit", 4), ("nb", 1), ("fo0", 1), ("h1", K), ("j16", K)]
+_rf += [("%s%d" % (k, s), 16) for s in (1, 2, 3) for k in ("fo", "og")]
+_rf += [("%s_%d" % (k, r), C) for r in (1, 2, 3) for k in ("PR", "Ps", "bf", "bs")]
+_rf += [("%s_%d" % (k, r), C) for r in (1, 2) for k in ("of", "os", "hf", "hs")]
+_rf += [("%s_%d" % (k, r), 2 * K) for r in (1, 2, 3) for k in ("fd", "fe", "fx")] + [("hd_%d" % r, K) for r in (1, 2)]
 RF, NRF = layout(_rf)
 RI, NRI = layout([("nx", K), ("p", 1), ("p16", 1), ("bit", 4), ("pick", 8)])
 WHERE = {"rb": RB, "ru": RU, "rf": RF, "ri": RI}
@@ -37,7 +43,7 @@ WHERE = {"rb": RB, "ru": RU, "rf": RF, "ri": RI}
 X4, U8, BF = "float8_e4m3fn_x4", "uint8", "bfloat16"
 SCRATCH = {
     "rb": ("sbuf", [128, NRB], BF), "ru": ("sbuf", [128, NRU], "uint16"), "rf": ("sbuf", [128, NRF], "float32"), "ri": ("sbuf", [128, NRI], "int32"),
-    "et": ("sbuf", [128, 528], BF), "qe": ("sbuf", [128, 512], X4), "se": ("sbuf", [128, 512], U8),
+    "one": ("sbuf", [128, 528], BF), "et": ("sbuf", [128, 528], BF), "qe": ("sbuf", [128, 512], X4), "se": ("sbuf", [128, 512], U8),
     "uin": ("sbuf", [128, 512], BF), "qu": ("sbuf", [128, 128], X4), "su": ("sbuf", [128, 128], U8),
     "u2": ("sbuf", [128, 128], X4), "s2": ("sbuf", [128, 128], U8),
     "vin": ("sbuf", [128, 512], BF), "qv": ("sbuf", [128, 128], X4), "sv": ("sbuf", [128, 128], U8),
@@ -46,17 +52,20 @@ SCRATCH = {
     "psA": ("psum", [128, 2048], "float32"), "psB": ("psum", [128, 2048], "float32"),
     "L0": ("sbuf", [128, 2 * K], "uint16"),
     "xt0": ("sbuf", [128, 4 * C], BF), "xq0": ("sbuf", [128, C], X4), "xs0": ("sbuf", [128, C], U8),
+    "za": ("sbuf", [128, 4 * C], BF), "hh": ("sbuf", [128, 4 * C], BF), "tb": ("sbuf", [128, 4 * C], BF),
 }
 for _r in (1, 2, 3):
-    for _n in ("th", "tp", "za", "zt", "hh", "tb", "xt"):
+    for _n in ("th", "tp", "zt", "xt"):
         SCRATCH["%s%d" % (_n, _r)] = ("sbuf", [128, 4 * C], BF)
     for _n in ("xq", "lq", "zq"):
         SCRATCH["%s%d" % (_n, _r)] = ("sbuf", [128, C], X4)
     for _n in ("xs", "lp", "zs"):
         SCRATCH["%s%d" % (_n, _r)] = ("sbuf", [128, C], U8)
-    for _n in ("L", "LN", "LZ"):
+    for _n in ("L", "LN"):
         SCRATCH["%s%d" % (_n, _r)] = ("sbuf", [128, 2 * K], "uint16")
-SEMAPHORES = ["cv", "cs", "ct", "cg", "dnx", "dx", "du", "dv", "dwc", "dws", "dout", "lsem"] + ["%s%d" % (k, r) for r in (1, 2, 3) for k in ("aN", "aZ", "aQ")]
+    for _n in ("LA", "LB"):
+        SCRATCH["%s%d" % (_n, _r)] = ("sbuf", [128, K], "uint16")
+SEMAPHORES = ["cv", "cs", "ct", "cg", "dnx", "dx", "du", "dv", "dwc", "dws", "dout", "lsem"] + ["%s%d" % (k, r) for r in (1, 2, 3) for k in ("aN", "aA", "aB", "aQ")]
 
 
 def rank_program(g, core, T, topo):
@@ -124,9 +133,16 @@ def rank_program(g, core, T, topo):
         o, w = WHERE[buf][name]
         return A(buf, o + a, o + (w if b is None else b))
 
-    def ends(buf, name, n=C):
+    def ends(buf, name, a=0, e=C):
         o = WHERE[buf][name][0]
-        return A(buf, o + 15, o + n, 16)
+        return A(buf, o + a + 15, o + e, 16)
+
+    def lane(name, k):
+        o = RF[name][0]
+        return (T.rf[:, o + k:o + 2 * K:2], [("%s#%d" % (name, k), 0, K)])
+
+    def lanes(name):
+        return (N("rf", name)[0], lane(name, 0)[1] + lane(name, 1)[1])
 
     def ind(w, o):
         return (w[0].indirect(o[0]), w[1] + o[1])
@@ -159,11 +175,17 @@ def rank_program(g, core, T, topo):
     def vcopy(out, a):
         op("v", lambda: g.vector.tensor_copy(out[0], a[0]), a[1], out[1])
 
-    def act(out, a, scale=1.0, bias=0.0):
-        if bias == 0.0 and scale == 1.0:
-            op("s", lambda: g.scalar.activation(out[0], a[0], COPY), a[1], out[1])
-        else:
-            op("s", lambda: g.scalar.activation(out[0], a[0], IDENT, bias=bias, scale=scale), a[1], out[1])
+    def scatter(win, o, a):
+        op("v", lambda: g.vector.tensor_copy(win[0].indirect(o[0]), a[0]), a[1] + o[1], win[1])
+
+    def act(out, a, scale=1.0, bias=0.0, func=IDENT):
+        regs = list(a[1])
+        if isinstance(scale, tuple):
+            regs += scale[1]
+            scale = scale[0]
+        elif bias == 0.0 and scale == 1.0 and func == IDENT:
+            return op("s", lambda: g.scalar.activation(out[0], a[0], COPY), regs, out[1])
+        op("s", lambda: g.scalar.activation(out[0], a[0], func, bias=bias, scale=scale), regs, out[1])
 
     def scan(out, a, b, init, o1, o2):
         regs = a[1] + b[1]
@@ -204,236 +226,279 @@ def rank_program(g, core, T, topo):
         total[sem] = n
         mark((sem, n), None, [], regs)
 
-    def send_lists(src, dst_buf, sem, m):
-        send(peer(m), sem, [(T[dst_buf][:, 0:2 * K], T[src][:, 0:2 * K])], [(src, 0, 2 * K)])
-        arrives(peer(m), sem, 1, [(dst_buf, 0, 2 * K)])
+    def send_list(src, a, e, dst, sem, m):
+        send(peer(m), sem, [(T[dst][:, 0:e - a], T[src][:, a:e])], [(src, a, e)])
+        arrives(peer(m), sem, 1, [(dst, 0, e - a)])
 
     def send_state(r, m):
         xq, xs, lq, lp = "xq%d" % (r - 1), "xs%d" % (r - 1), "lq%d" % r, "lp%d" % r
         send(peer(m), "aQ%d" % r, [(T[lq][:, 0:C].bitcast(dt.uint8), T[xq][:, 0:C].bitcast(dt.uint8)), (T[lp][:, 0:C], T[xs][:, 0:C])], [(xq, 0, C), (xs, 0, C)])
         arrives(peer(m), "aQ%d" % r, 2, [(lq, 0, C), (lp, 0, C)])
 
-    def scores(r):
-        for i, (a, e) in enumerate(HALF):
-            for k in (0, 2):
-                mm(P("psB", i + k, e - a), "u2", "s2", 0, "xq%d" % (r - 1), "xs%d" % (r - 1), a, e)
+    def signs(r, i):
+        a, e = HALF[i]
+        mm(P("psB", i, e - a), "u2", "s2", 0, "xq%d" % (r - 1), "xs%d" % (r - 1), a, e)
+        for k in ("sg", "sh"):
+            act(N("rb", "%s_%d" % (k, r), a, e), P("psB", i, e - a), bias=-TINY, func=SIGN)
 
     def unpack(ps, q, s):
         for b in range(4):
             mm(P(ps, b, C), "qe", "se", 128 * b, q, s, 0, C)
 
-    def halves(ps, dst):
-        for b in range(4):
+    def halves(ps, dst, planes=range(4)):
+        for b in planes:
             act(plane(dst, b), P(ps, b, C), scale=0.5)
 
-    mask, hm, io = N("rb", "mask"), N("rb", "hm"), N("rb", "iota")
+    mask, hm, io, pw = N("rb", "mask"), N("rb", "hm"), N("rb", "iota"), N("rf", "pw", 15, 16)
 
-    def settle(m, s, n=C):
-        scan(N("rb", s, 0, n), N("rb", "hm", 0, n), N("rb", m, 0, n), 0.0, MUL, ADD)
+    def hold(src, dst, a=0, e=C):
+        scan(N("rf", dst, a, e), N("rb", "cx", 0, e - a), N("rf", src, a, e), 0.0, MUL, MAX)
 
-    def settle_max(*jobs):
-        for buf, src, dst, out, shift in jobs:
-            hold(buf, src, dst)
-        for buf, src, dst, out, shift in jobs:
-            ts(out, ends(buf, dst), N("rf", "pw", 15, 16), MUL, shift, ADD)
+    def listed(out, held, shift, a=0, e=C):
+        ts(out, ends("rf", held, a, e), pw, MUL, shift, ADD)
 
-    def hold(buf, src, dst):
-        scan(N(buf, dst, 0, C), N("rb", "cx"), N(buf, src, 0, C), 0.0, MUL, MAX)
+    def shared(dst, win, buf, at, cut=CUT, bias=0.0):
+        if cut:
+            o = ind(win, A(buf, at, at + cut // 16))
+            if bias:
+                ts(N("rf", dst, 0, cut), o, bias, ADD)
+            else:
+                vcopy(N("rf", dst, 0, cut), o)
+        act(N("rf", dst, cut, C), ind(win, A(buf, at + cut // 16, at + K)), bias=bias)
 
     dma("y", "dnx", N("ri", "nx")[0], T.nx[:], [], N("ri", "nx")[1])
-    dma("s", "dx", T.xt0[:], T.x[:], [], [("xt0", 0, 4 * C)])
+    dma("y", "dx", T.xt0[:], T.x[:], [], [("xt0", 0, 4 * C)])
     dma("y", "du", T.uin[:], T.u[:], [], [("uin", 0, 512)])
     dma("y", "dwc", T.wq[:].bitcast(dt.uint8), T.wc[:], [], [("wq", 0, 512)])
     dma("y", "dws", T.wp[:], T.ws[:], [], [("wp", 0, 512)])
     dma("y", "dv", T.vin[:], T.v[:], [], [("vin", 0, 512)])
 
+    one = lambda n: A("one", 0, n)
+    memset(one(528), 1.0)
     op("g", lambda: g.iota(N("ri", "p")[0], [[0, 1]], 0, 1), [], N("ri", "p")[1])
     iota(N("rb", "t16"), [[0, K], [1, 16]], 0, 0)
     op("g", lambda: g.iota(N("ri", "pick")[0], [[16, 8]], 0, 0), [], N("ri", "pick")[1])
-    memset(N("rb", "one"), 1.0)
-    memset(N("rf", "f0"), -208.0)
-    memset(N("ru", "q0"), 0)
-    scan(N("rf", "i1024"), N("rb", "one"), N("rb", "one"), 1023.0, MUL, ADD)
+    iota(N("rf", "j16"), [[16, K]], 0, 0)
+    op("g", lambda: g.affine_select(T.et[:, 0:515], one(515)[0], [[1, 515]], EQ, 0.0, -3, -4), one(515)[1], [("et", 0, 515)])
+    scan(N("rf", "i1024"), one(C), one(C), 1023.0, MUL, ADD)
     act(io, N("rf", "i1024"), bias=-1232.0)
-    act(N("rb", "two"), N("rb", "one"), scale=2.0)
     ts(N("ri", "p16"), N("ri", "p"), 15, AluOpType.bitwise_and)
     for s in range(4):
         ts(N("ri", "bit", s, s + 1), N("ri", "p"), s, AluOpType.logical_shift_right, 1, AluOpType.bitwise_and)
     vcopy(N("rf", "p16"), N("ri", "p16"))
     vcopy(N("rf", "bit"), N("ri", "bit"))
+    for r in (1, 2, 3):
+        memset(lane("fd_%d" % r, 0), 0.0)
+    memset(N("rb", "PE", 0, 1), -208.0)
+    for r in (2, 3):
+        memset(N("rb", "PW_%d" % r, 0, 1), -208.0)
+        memset(N("rb", "PW_%d" % r, C, C + 1), -207.0)
+    ts(mask, N("rb", "t16"), N("rf", "p16"), EQ)
     vcopy(N("ru", "pick"), N("ri", "pick"))
-    ts(N("rb", "mask"), N("rb", "t16"), N("rf", "p16"), EQ)
-    ts(N("rb", "cp"), N("rb", "t16", 0, 16), N("rf", "p16"), GT, 0.5, MUL)
-    act(hm, N("rb", "mask"), scale=-1.0, bias=1.0)
-    ts(N("rb", "cx"), N("rb", "t16"), N("rf", "p16"), GT, 2.0, MUL)
+    act(N("rb", "cx"), mask, scale=-2.0, bias=2.0)
+    act(N("rb", "cp"), N("rb", "mask", 0, 16), scale=-0.5, bias=0.5)
+    act(N("rf", "nb"), N("rf", "bit", 0, 1), scale=-1024.0, bias=1024.0)
+    ts(lane("fe_1", 1), N("rf", "j16"), N("rf", "p16"), ADD)
     scan(N("rf", "pw"), N("rb", "cp"), N("rb", "mask", 0, 16), 0.0, MUL, ADD)
-    for s in range(4):
-        act(N("rb", "ds%d" % s), N("rb", "one", 0, 16))
 
+    W = lambda s, a=0, e=C: N("rf", "W%d" % s, a, e)
     vcopy(A("L0", 0, K), N("ri", "nx"))
-    w0 = N("rf", "w0")
-    op("v", lambda: g.vector.tensor_copy(w0[0].indirect(T.L0[:, 0:K]), N("rf", "i1024")[0]), N("rf", "i1024")[1] + [("L0", 0, K)], w0[1])
-    act(N("rb", "W0"), w0, bias=-1232.0)
-    hold("rf", "w0", "w0s")
-    for s in range(4):
-        ts(N("rb", "mb%d" % s), N("rb", "mask", 0, 16), N("rf", "bit", s, s + 1), MUL)
-    ts(A("L0", K, 2 * K), ends("rf", "w0s"), N("rf", "pw", 15, 16), MUL, -1024.0, ADD)
-    for s in range(4):
-        ts(N("rb", "ds%d" % s, 0, 1), N("rf", "bit", s, s + 1), -1.0, MUL, 1.0, ADD)
-    memset(A("et", 0, 515), 1.0)
-    op("g", lambda: g.affine_select(T.et[:, 0:515], T.et[:, 0:515], [[1, 515]], EQ, 0.0, -3, -4), [("et", 0, 515)], [("et", 0, 515)])
-    send_lists("L0", "LN1", "aN1", MASKS[0])
+    shared("W1", N("rf", "i1024"), "L0", 0, 0)
+    shared("W2", W(1), "L0", 0, 0)
+    scatter(N("rf", "w0"), A("L0", 0, K), N("rf", "i1024"))
+    for s in (1, 2, 3):
+        act(N("rb", "mb%d" % s), N("rb", "mask", 0, 16), scale=N("rf", "bit", s, s + 1))
+        act(N("rb", "ds%d" % s, 1, 16), one(15))
+        act(N("rb", "ds%d" % s, 0, 1), N("rf", "bit", s, s + 1), scale=-1.0, bias=1.0)
+    hold("w0", "w0s")
+    hold("W2", "S2")
+    listed(A("L0", K, 2 * K), "w0s", -1024.0)
+    listed(N("ru", "G2"), "S2", -1024.0)
+    send_list("L0", 0, 2 * K, "LN1", "aN1", MASKS[0])
+    ts(N("ru", "q1"), W(1, 0, 1), -1024.0, ADD, N("rf", "bit", 0, 1), MUL)
+    ts(N("rf", "fo0"), W(1, 0, 1), N("rf", "bit", 0, 1), MUL, N("rf", "nb"), ADD)
 
-    def first_x():
-        quant("xq0", "xs0", "xt0", 0, C, 0)
-        send_state(1, MASKS[0])
+    def power(s, k, cut=CUT):
+        shared("W%d" % s, W(s - k), "ru", RU["G%d" % k][0], cut)
 
-    def first_u():
-        quant("qu", "su", "uin", 0, 128, 0)
-        pk = N("ru", "pick")
-        op("v", lambda: g.vector.tensor_copy(T.u2[:, 0:128].bitcast(dt.uint32), T.qu[:, 0:128].bitcast(dt.uint32).indirect(pk[0])), [("qu", 0, 128)] + pk[1], [("u2", 0, 128)])
-        op("s", lambda: g.scalar.activation(T.s2[:, 0:128], T.su[:, 0:128].indirect(pk[0]), COPY), [("su", 0, 128)] + pk[1], [("s2", 0, 128)])
+    def as_list(s, *between, cut=CUT):
+        if cut:
+            hold("W%d" % s, "S%d" % s, 0, cut)
+        hold("W%d" % s, "S%d" % s, cut, C)
+        for f in between:
+            f()
+        listed(N("ru", "G%d" % s), "S%d" % s, -1024.0)
+
+    def bit(s, part):
+        if part == 0:
+            tt(N("rf", "og%d" % s), ind(W(2 ** s), N("ru", "q%d" % s)), N("rb", "mb%d" % s), MUL)
+        if part == 1:
+            scan(N("rf", "fo%d" % s), N("rb", "ds%d" % s), N("rf", "og%d" % s), N("rf", "fo%d" % (s - 1), 15, 16) if s > 1 else N("rf", "fo0"), MUL, ADD)
+        if part == 2:
+            ts(N("ru", "q%d" % (s + 1)) if s < 3 else N("ru", "OG0", 0, 1), N("rf", "fo%d" % s, 15, 16), -1024.0, ADD)
+
+    def more(s, a, e, part):
+        if part == 0:
+            vcopy(N("rf", "or", a + s, e + s), ind(W(s), N("ru", "OG0", a // 16, e // 16)))
+        if part == 1:
+            hold("or", "os", a + s, e + s)
+        if part == 2:
+            listed(N("ru", "OG0", (a + s) // 16, (e + s) // 16), "os", -1024.0, a + s, e + s)
 
     def constant(b):
         op("v", lambda: g.vector.quantize_mx(T.qe[:, 128 * b:128 * b + 128], T.se[:, 128 * b:128 * b + 128], T.et[:, 3 - b:515 - b]), [("et", 0, 515)], [("qe", 128 * b, 128 * b + 128), ("se", 128 * b, 128 * b + 128)])
 
-    def up(r, i):
-        a, e = HALF[i]
-        ts(N("rb", "up_%d" % r, a, e), P("psB", i + 2, e - a), 0.0, GT)
-        out, ps = N("rb", "sg_%d" % r, a, e), P("psB", i, e - a)
-        op("s", lambda: g.scalar.activation(out[0], ps[0], ActivationFunctionType.Sign), ps[1], out[1])
+    def pick_u():
+        pk = N("ru", "pick")
+        op("v", lambda: g.vector.tensor_copy(T.u2[:, 0:128].bitcast(dt.uint32), T.qu[:, 0:128].bitcast(dt.uint32).indirect(pk[0])), [("qu", 0, 128)] + pk[1], [("u2", 0, 128)])
+        op("s", lambda: g.scalar.activation(T.s2[:, 0:128], T.su[:, 0:128].indirect(pk[0]), COPY), [("su", 0, 128)] + pk[1], [("s2", 0, 128)])
 
-    def chunk(c, part):
-        s, a, e, to = CHUNK[c]
-        n = e - a
+    def guests(r):
+        tt(N("rb", "g_%d" % r, 0, C), ind(N("rb", "sg_%d" % r, 0, C), A("LN%d" % r, 0, K)), N("rb", "sh_%d" % r, 0, C), GT)
+
+    def leavers(r):
+        tt(N("rb", "l_%d" % r, 0, C), ind(N("rb", "sg_%d" % r, 0, C), A("LN%d" % r, K, 2 * K)), N("rb", "sh_%d" % r, 0, C), LT)
+
+    def slots(r, part):
         if part == 0:
-            tt(N("rb", "om", to, to + n), ind(N("rb", "W%d" % s), N("ru", "OG0", a // 16, e // 16) if c else N("ru", "q4")), N("rb", "mask", 0, n), MUL)
+            scan(N("rb", "ls_%d" % r, 0, C), N("rb", "c4"), N("rb", "l_%d" % r, 0, C), 0.0, MUL, ADD)
         if part == 1:
-            scan(N("rb", "os", to, to + n), N("rb", "hm", 0, n), N("rb", "om", to, to + n), 0.0, MUL, ADD)
+            ts(lane("fe_%d" % r, 0), ends("rb", "ls_%d" % r), N("rf", "thr"), GT)
         if part == 2:
-            o = RB["os"][0]
-            ts(N("ru", "OG0", to // 16, to // 16 + n // 16), A("rb", o + to + 15, o + to + n, 16), 208.0, ADD)
+            scan(N("rf", "fx_%d" % r), lanes("fd_%d" % r), lanes("fe_%d" % r), 0.0, MUL, ADD)
+        if part == 3:
+            o = RF["fx_%d" % r][0]
+            vcopy(N("ru", "x_%d" % r), A("rf", o + 1, o + 2 * K, 2))
 
-    for s in range(5):
-        src = A("L0", K, 2 * K) if s == 0 else N("ru", "G%d" % s)
-        w = N("rb", "W%d" % s)
-        small = s < 4
-        act(N("rb", "W%d" % (s + 1)), ind(w, src))
-        tt(N("rb", "M%d" % s if s else "om"), ind(w, src), mask, MUL)
-        if small:
-            tt(N("rb", "og%d" % s), ind(w, N("ru", "q%d" % s)), N("rb", "mb%d" % s), MUL)
-        else:
-            chunk(s - 4, 0)
-        if s:
-            settle("M%d" % s, "S%d" % s)
-        else:
-            settle("om", "os")
-        if small:
-            scan(N("rf", "fo%d" % s), N("rb", "ds%d" % s), N("rb", "og%d" % s), N("rf", "fo%d" % (s - 1), 15, 16) if s else N("rf", "f0"), MUL, ADD)
-        else:
-            chunk(s - 4, 1)
-        ts(N("ru", "G%d" % (s + 1)), ends("rb", "S%d" % s if s else "os"), 208.0, ADD)
-        if small:
-            ts(N("ru", "q%d" % (s + 1)), N("rf", "fo%d" % s, 15, 16), 208.0, ADD)
-            if s == 3:
-                vcopy(N("ru", "OG0", 0, 1), N("ru", "q4"))
-        else:
-            chunk(s - 4, 2)
-    act(N("rb", "W6"), ind(N("rb", "W5"), N("ru", "G5")))
-    act(N("rb", "M7"), ind(N("rb", "W6"), N("ru", "G5")))
-    act(N("rb", "W7"), ind(N("rb", "M7"), N("ru", "G5")))
-    for part in range(3):
-        chunk(1, part)
-    first_x()
-    for part in range(3):
-        chunk(2, part)
-    first_u()
-    scores(1)
-    for c in (3, 4, 5):
-        for part in range(3):
-            chunk(c, part)
-            if c < 5 and part < 2:
-                constant(2 * c - 6 + part)
-            if c == 5 and part < 2:
-                up(1, part)
-    unpack("psA", "xq0", "xs0")
-    rr = N("rf", "rr")
-    order = N("ru", "OG0")
-    op("v", lambda: g.vector.tensor_copy(rr[0].indirect(order[0]), N("rf", "i1024")[0]), N("rf", "i1024")[1] + order[1], rr[1])
-    act(N("rf", "hf"), ind(rr, A("LN1", K, 2 * K)))
-    rG = N("rf", "rG0")
-    hold("rf", "rr", "rrs")
-
+    power(4, 2)
+    bit(1, 0)
+    power(6, 2)
+    bit(1, 1)
+    act(hm, mask, scale=-1.0, bias=1.0)
+    power(8, 2)
+    bit(1, 2)
+    as_list(8, lambda: bit(2, 0))
+    bit(2, 1)
+    power(16, 8, 0)
+    bit(2, 2)
+    quant("xq0", "xs0", "xt0", 0, C, 0)
+    send_state(1, MASKS[0])
+    bit(3, 0)
+    power(24, 8, 0)
+    quant("qu", "su", "uin", 0, 128, 0)
+    bit(3, 1)
+    pick_u()
+    bit(3, 2)
+    power(32, 8)
+    more(16, 0, 16, 0)
+    signs(1, 0)
+    signs(1, 1)
+    as_list(32, lambda: more(16, 0, 16, 1))
+    more(16, 0, 16, 2)
+    power(64, 32, 0)
+    more(32, 0, 32, 0)
+    guests(1)
+    more(32, 0, 32, 1)
+    power(96, 32, 0)
+    act(N("rb", "c4"), mask, scale=-4.0, bias=4.0)
+    more(32, 0, 32, 2)
+    leavers(1)
+    more(64, 0, 64, 0)
+    power(128, 32)
+    more(64, 0, 64, 1)
+    vcopy(N("rf", "h1"), A("LN1", K, 2 * K))
+    more(64, 0, 64, 2)
+    scan(N("rf", "p4"), N("rb", "c4", 0, 16), N("rb", "mask", 0, 16), 0.0, MUL, ADD)
+    power(160, 32, 0)
+    more(128, 0, 128, 0)
+    ts(N("rf", "thr"), N("rf", "p4", 15, 16), 0.5, MUL)
+    more(128, 0, 128, 1)
+    tt(N("rf", "hd_1"), N("rf", "h1"), lane("fe_1", 1), SUB)
+    more(128, 0, 128, 2)
+    slots(1, 0)
+    more(160, 96, 256, 0)
+    l1, g1 = N("rb", "l_1", 0, C), N("rb", "g_1", 0, C)
+    so1, go1 = lambda a, e: N("rb", "so_1", a, e), lambda a, e: N("rb", "go_1", a, e)
+    act(so1(0, 256), ind(l1, N("ru", "OG0", 0, 16)), scale=-1.0, bias=1.0)
+    act(go1(0, 256), ind(g1, N("ru", "OG0", 0, 16)))
+    ts(lane("fd_1", 1), N("rf", "hd_1"), float(C), ADD)
+    more(160, 96, 256, 1)
+    slots(1, 1)
+    more(160, 96, 256, 2)
+    slots(1, 2)
+    vcopy(go1(256, C), ind(g1, N("ru", "OG0", 16, K)))
+    act(so1(256, C), ind(l1, N("ru", "OG0", 16, K)), scale=-1.0, bias=1.0)
+    scan(N("rb", "PE", 1, 257), so1(0, 256), go1(0, 256), -208.0, ADD, ADD)
+    scan(N("rb", "PE", 257, C), so1(256, C - 1), go1(256, C - 1), N("rb", "PE", 256, 257), ADD, ADD)
+    slots(1, 3)
+    scatter(N("rb", "PW_1", 0, C), N("ru", "OG0"), N("rb", "PE"))
+    constant(0)
+    ts(N("rb", "PW_1", C, 2 * C), N("rb", "PW_1", 0, C), 1.0, ADD)
+    constant(1)
 
     for r in (1, 2, 3):
         m = MASKS[r - 1]
-        L, LN, LZ = "L%d" % r, "LN%d" % r, "LZ%d" % r
+        L, LN, LA, LB = "L%d" % r, "LN%d" % r, "LA%d" % r, "LB%d" % r
         nb = lambda k, a=0, b=C: N("rb", "%s_%d" % (k, r), a, b)
         nu = lambda k: N("ru", "%s_%d" % (k, r))
-        nf = lambda k: N("rf", "%s_%d" % (k, r))
+        th, tp, zt, xt = ["%s%d" % (k, r) for k in ("th", "tp", "zt", "xt")]
+        zq, zs, xq, xs = ["%s%d" % (k, r) for k in ("zq", "zs", "xq", "xs")]
+        PR, Ps = "PR_%d" % r, "Ps_%d" % r
         if r > 1:
-            up(r, 0)
-            up(r, 1)
-        tt(nb("g"), ind(nb("sg"), A(LN, 0, K)), nb("up"), GT)
-        act(nb("go"), ind(nb("g"), order))
+            leavers(r)
+            act(nb("so"), ind(nb("l"), N("ru", "og_%d" % (r - 1))), scale=-1.0, bias=1.0)
+            guests(r)
+            act(nb("go"), ind(nb("g"), N("ru", "og_%d" % (r - 1))))
+            slots(r, 0)
+            tt(lane("fd_%d" % r, 1), N("rf", "hd_%d" % (r - 1)), lane("fe_%d" % r, 1), SUB)
+            slots(r, 1)
+            slots(r, 2)
+            slots(r, 3)
+            scan(nb("PW", 1, C), nb("so", 0, C - 1), nb("go", 0, C - 1), -208.0, ADD, ADD)
+            scan(nb("PW", C + 1, 2 * C), nb("so", 0, C - 1), nb("go", 0, C - 1), -207.0, ADD, ADD)
+        shared(PR, nb("PW", 0, 2 * C), "ru", RU["x_%d" % r][0], bias=1232.0)
         if r == 1:
-            ts(rG, ends("rf", "rrs"), N("rf", "pw", 15, 16), MUL, -1231.0, ADD)
-        tt(nb("l"), ind(nb("g"), A(LN, K, 2 * K)), N("rb", "two"), ADD)
-        act(nb("so"), ind(nb("l"), order), scale=-1.0, bias=3.0)
-        lG = nf("lG")
-        left = ("rb", "l_%d" % r, "ls_%d" % r, lG, -2.0)
+            constant(2)
+        hold(PR, Ps, 0, CUT)
+        hold(PR, Ps, CUT, C)
         if r == 1:
-            settle_max(left, ("rf", "hf", "hfs", N("rf", "hd"), -1231.0))
-            tt(nf("dG"), N("rf", "hd"), rG, SUB)
-        else:
-            settle_max(left)
-        tt(nf("t2"), lG, nf("dG"), MUL)
-        tt(nf("t3"), nf("t2"), rG, ADD)
-        ts(nu("x"), nf("t3"), 207.0, ADD)
-        scan(nb("PB", 0, C), nb("so"), nb("go"), -208.0, ADD, ADD)
-        halves("psA", "th%d" % r)
-        if r == 1:
+            constant(3)
+            unpack("psA", "xq0", "xs0")
             unpack("psB", "lq1", "lp1")
-            halves("psB", "tp1")
-        tt(nb("pm"), ind(nb("PB"), nu("x")), mask, MUL)
-        settle("pm_%d" % r, "ps_%d" % r)
-        tt(nf("rG"), ends("rb", "ps_%d" % r), lG, SUB)
-        rG = nf("rG")
-        ts(nu("sc"), rG, 208.0, ADD)
-        ts(nu("ai"), rG, 207.0, ADD)
-        ts(nu("bi"), rG, 209.0, ADD)
-        ob = nb("OB", 0, 417)
-        op("v", lambda: g.vector.tensor_copy(ob[0].indirect(nu("sc")[0]), io[0]), io[1] + nu("sc")[1], ob[1])
-        vcopy(nb("OB", 0, 1), nb("OB", 416, 417))
-        act(nb("OB", 417, 418), nb("OB", 1, 2))
-        tt(nb("am"), ind(nb("OB"), nu("ai")), mask, MUL)
-        act(nf("bf"), ind(nb("OB", 0, 418), nu("bi")), bias=1232.0)
-        settle("am_%d" % r, "as_%d" % r)
-        hold("rf", "bf_%d" % r, "bs_%d" % r)
-        ts(A(L, 0, K), ends("rb", "as_%d" % r), 208.0, ADD)
-        ts(A(L, K, 2 * K), ends("rf", "bs_%d" % r), N("rf", "pw", 15, 16), MUL, -1024.0, ADD)
-        send_lists(L, LZ, "aZ%d" % r, m)
+        halves("psA", th)
+        listed(nu("sc"), Ps, -1023.0)
+        listed(nu("ai"), Ps, -1022.0)
+        scatter(nb("OB", 0, 417), nu("sc"), io)
+        listed(nu("bi"), Ps, -1024.0)
+        vcopy(nb("OB", 417, 418), nb("OB", 1, 2))
+        act(nb("OB", 0, 1), nb("OB", 416, 417))
         if r < 3:
-            send_lists(L, "LN%d" % (r + 1), "aN%d" % (r + 1), MASKS[r])
-            act(nf("of"), nb("OB", 1, 417), bias=1232.0)
-            rr = nb("rR")
-            tt(rr, ind(nb("PB"), nu("x")), nb("l", 0, C), SUB)
-            ts(nf("rH"), rG, -2.0, ADD)
-            settle_max(("rf", "of_%d" % r, "os_%d" % r, nu("og"), -1024.0))
-            order = nu("og")
+            listed(lane("fe_%d" % (r + 1), 1), Ps, -1024.0)
+        tt(nb("am"), ind(nb("OB", 0, 418), nu("ai")), mask, MUL)
+        act(N("rf", "bf_%d" % r), ind(nb("OB", 0, 418), nu("bi")), bias=1232.0)
+        scan(nb("as"), hm, nb("am"), 0.0, MUL, ADD)
+        ts(A(L, 0, K), ends("rb", "as_%d" % r), 208.0, ADD)
+        send_list(L, 0, K, LA, "aA%d" % r, m)
+        hold("bf_%d" % r, "bs_%d" % r)
+        listed(A(L, K, 2 * K), "bs_%d" % r, -1024.0)
+        send_list(L, K, 2 * K, LB, "aB%d" % r, m)
+        if r < 3:
+            send_list(L, 0, 2 * K, "LN%d" % (r + 1), "aN%d" % (r + 1), MASKS[r])
+            act(N("rf", "of_%d" % r), nb("OB", 1, 417), bias=1232.0)
+            hold("of_%d" % r, "os_%d" % r)
         if r == 1:
             quant("qv", "sv", "vin", 0, 128, 0)
         else:
             unpack("psB", "lq%d" % r, "lp%d" % r)
-            halves("psB", "tp%d" % r)
-        th, tp, tb, za, zt, hh, xt = ["%s%d" % (k, r) for k in ("th", "tp", "tb", "za", "zt", "hh", "xt")]
-        zq, zs, xq, xs = ["%s%d" % (k, r) for k in ("zq", "zs", "xq", "xs")]
-
+        if r < 3:
+            listed(nu("og"), "os_%d" % r, -1024.0)
+        halves("psB", tp)
         for b in range(4):
-            if b in ((3,), (1, 2), (1, 2, 3))[r - 1]:
-                vcopy(plane(tb, b), ind(plane(th, b), A(L, K, 2 * K)))
-            elif (r, b) != (2, 3):
-                act(plane(tb, b), ind(plane(th, b), A(L, K, 2 * K)))
+            if b in OWN_TB[r]:
+                vcopy(plane("tb", b), ind(plane(th, b), A(L, K, 2 * K)))
+            elif b not in LATE_TB[r]:
+                act(plane("tb", b), ind(plane(th, b), A(L, K, 2 * K)))
+
         def pack_z(i):
             a, e = HALF[i]
             quant(zq, zs, zt, a, e)
@@ -442,32 +507,32 @@ def rank_program(g, core, T, topo):
 
         for i, (a, e) in enumerate(HALF):
             for b in range(4):
-                for a1, e1 in ((a, a + 96), (a + 96, e)) if (i, b) == (0, 0) else ((a, e),):
-                    act(plane(za, b, a1, e1), ind(plane(tp, b), A(LZ, a1 // 16, e1 // 16)))
-                    tt(strip(zt, b, a1, e1), ind(plane(tp, b), A(LZ, K + a1 // 16, K + e1 // 16)), plane(za, b, a1, e1), ADD)
+                act(plane("za", b, a, e), ind(plane(tp, b), A(LA, a // 16, e // 16)))
+                tt(strip(zt, b, a, e), ind(plane(tp, b), A(LB, a // 16, e // 16)), plane("za", b, a, e), ADD)
                 if (i, b) == (1, 0):
                     pack_z(0)
         pack_z(1)
-        if r < 3:
-            tt(N("rb", "hm_%d" % (r + 1), 0, C), ind(rr, A("LN%d" % (r + 1), K, 2 * K)), mask, MUL)
         a, e = HALF[0]
         for b in range(4):
-            act(plane(hh, b, a, e), P("psA", b, e - a), scale=0.015625)
+            act(plane("hh", b, a, e), P("psA", b, e - a), scale=0.015625)
         a, e = HALF[1]
-        for b in range(4):
-            if b % 2:
-                act(plane(hh, b, a, e), P("psB", b, e - a), scale=0.015625)
-            else:
-                ts(plane(hh, b, a, e), P("psB", b, e - a), 0.015625, MUL)
-        if r == 2:
-            act(plane(tb, 3), ind(plane(th, 3), A(L, K, 2 * K)))
-        if r == 3:
-            act(N("rf", "nr"), ind(nb("OB"), nu("ai")), bias=208.0)
+        ts(plane("hh", 0, a, e), P("psB", 0, e - a), 0.015625, MUL)
+        for b in (1, 2, 3):
+            act(plane("hh", b, a, e), P("psB", b, e - a), scale=0.015625)
+        for b in LATE_TB[r]:
+            act(plane("tb", b), ind(plane(th, b), A(L, K, 2 * K)))
+        if r < 3:
+            act(N("rf", "hf_%d" % r), ind(N("rf", PR), A("LN%d" % (r + 1), K, 2 * K)))
+        else:
+            act(N("rf", "nr"), ind(nb("OB", 0, 418), nu("ai")), bias=208.0)
             dma("y", "dout", T.nr[:, :], T.rf[0:128:16, RF["nr"][0]:RF["nr"][0] + C], N("rf", "nr")[1], [])
+
         def pack_x(i):
             a, e = HALF[i]
             quant(xq, xs, xt, a, e)
-            if r == 3:
+            if r < 3:
+                signs(r + 1, i)
+            else:
                 mm(P("psA", i, e - a), "qv", "sv", 0, xq, xs, a, e)
                 dma("y", "dout", T.oc[:, 4 * a:4 * e], T[xq][:, a:e].bitcast(dt.uint8), [(xq, a, e)], [])
                 for k in range(4):
@@ -478,19 +543,18 @@ def rank_program(g, core, T, topo):
                     act(A("yo", a, e), P("psA", i, e - a))
                 dma("s", "dout", T.y[:, a:e], T.yo[:, a:e], [("yo", a, e)], [])
 
+        late = [b for b in range(4) if b not in LATE_TB[r]] + list(LATE_TB[r])
         for i, (a, e) in enumerate(HALF):
-            for b in range(4):
-                tt(strip(xt, b, a, e), ind(plane(hh, b), A(L, a // 16, e // 16)), plane(tb, b, a, e), ADD)
-                if (i, b) == (1, 0):
+            for k, b in enumerate(late):
+                tt(strip(xt, b, a, e), ind(plane("hh", b), A(L, a // 16, e // 16)), plane("tb", b, a, e), ADD)
+                if (i, k) == (1, 0):
                     pack_x(0)
-        if r < 3:
-            settle("hm_%d" % (r + 1), "hs_%d" % (r + 1))
         pack_x(1)
         if r < 3:
             send_state(r + 1, MASKS[r])
-            scores(r + 1)
             unpack("psA", xq, xs)
-            tt(N("rf", "dG_%d" % (r + 1)), ends("rb", "hs_%d" % (r + 1)), nf("rH"), SUB)
+            hold("hf_%d" % r, "hs_%d" % r)
+            listed(N("rf", "hd_%d" % r), "hs_%d" % r, C - 1024.0)
 
     for sem in sorted(total):
         g.wait_ge(T.sem[sem], total[sem])

@@ -1,16 +1,17 @@
 from concourse.mybir import dt, AluOpType, AxisListType, ActivationFunctionType
 
 ADD, SUB, MUL, MAX = AluOpType.add, AluOpType.subtract, AluOpType.mult, AluOpType.max
-GT, LT, EQ = AluOpType.is_gt, AluOpType.is_lt, AluOpType.is_equal
+GT, LT, EQ, NE = AluOpType.is_gt, AluOpType.is_lt, AluOpType.is_equal, AluOpType.not_equal
 COPY, IDENT, SIGN = ActivationFunctionType.Copy, ActivationFunctionType.Identity, ActivationFunctionType.Sign
+SQUARE, RELU = ActivationFunctionType.Square, ActivationFunctionType.Relu
 C = 416
 K = C // 16
 MASKS = [1, 2, 3]
 HALF = [(0, 288), (288, 416)]
+PAIR = [(0, 256), (256, 416)]
 CUT = 160
 TINY = 2.0 ** -93
-OWN_TB = {1: (2, 3), 2: (2, 3), 3: (1, 2, 3)}
-LATE_TB = {1: (), 2: (1,), 3: ()}
+TB = {1: ("vvss", "vlll"), 2: ("vvvl", "vsll"), 3: ("vvvs", "vlll")}
 
 
 def layout(items):
@@ -21,21 +22,21 @@ def layout(items):
     return at, n
 
 
-_rb = [(k, C) for k in ("mask", "hm", "cx", "c4", "iota", "t16", "PE")] + [("cp", 16)]
+_rb = [(k, C) for k in ("mask", "cx", "c4", "iota", "t16", "PE")] + [("cp", 16)]
 _rb += [("%s%d" % (k, s), 16) for s in (1, 2, 3) for k in ("mb", "ds")]
-_rb += [("%s_%d" % (k, r), 432) for r in (1, 2, 3) for k in ("sg", "sh", "g", "l", "ls", "so", "go", "OB", "am", "as")]
-_rb += [("PW_%d" % r, 2 * C) for r in (1, 2, 3)]
+_rb += [("%s_%d" % (k, r), C) for r in (1, 2, 3) for k in ("sg", "sh", "g", "l", "ls", "so", "go", "am", "as")]
+_rb += [("OB_%d" % r, 448) for r in (1, 2, 3)] + [("PW_%d" % r, 2 * C) for r in (1, 2, 3)]
 RB, NRB = layout(_rb)
-_ru = [("G%d" % s, K) for s in (2, 8, 32)] + [("OG0", K), ("pick", 8)] + [("q%d" % s, 1) for s in (1, 2, 3)]
+_ru = [("G%d" % s, K) for s in (2, 8, 32)] + [("OG0", K), ("pick", 8)] + [("i0_%d" % r, 1) for r in (1, 2, 3)] + [("q%d" % s, 1) for s in (1, 2, 3)]
 _ru += [("%s_%d" % (k, r), K) for r in (1, 2, 3) for k in ("x", "sc", "ai", "bi", "og")]
 RU, NRU = layout(_ru)
-POWERS = (1, 2, 4, 6, 8, 16, 24, 32, 64, 96, 128, 160)
+POWERS = (1, 2, 4, 6, 8, 16, 24, 32, 64, 96, 128)
 _rf = [(k, C) for k in ("i1024", "w0", "w0s", "or", "os", "nr", "S2", "S8", "S32")] + [("W%d" % s, C) for s in POWERS]
-_rf += [("p16", 1), ("pw", 16), ("p4", 16), ("thr", 1), ("bit", 4), ("nb", 1), ("fo0", 1), ("h1", K), ("j16", K)]
+_rf += [("p16", 1), ("pw", 16), ("pw2", 1), ("npw", 1), ("bit", 4), ("nb", 1), ("fo0", 1), ("j16", K)] + [("i0_%d" % r, 1) for r in (1, 2, 3)]
 _rf += [("%s%d" % (k, s), 16) for s in (1, 2, 3) for k in ("fo", "og")]
 _rf += [("%s_%d" % (k, r), C) for r in (1, 2, 3) for k in ("PR", "Ps", "bf", "bs")]
 _rf += [("%s_%d" % (k, r), C) for r in (1, 2) for k in ("of", "os", "hf", "hs")]
-_rf += [("%s_%d" % (k, r), 2 * K) for r in (1, 2, 3) for k in ("fd", "fe", "fx")] + [("hd_%d" % r, K) for r in (1, 2)]
+_rf += [("%s_%d" % (k, r), 3 * K) for r in (1, 2, 3) for k in ("fd", "fe", "fx")]
 RF, NRF = layout(_rf)
 RI, NRI = layout([("nx", K), ("p", 1), ("p16", 1), ("bit", 4), ("pick", 8)])
 WHERE = {"rb": RB, "ru": RU, "rf": RF, "ri": RI}
@@ -65,7 +66,7 @@ for _r in (1, 2, 3):
         SCRATCH["%s%d" % (_n, _r)] = ("sbuf", [128, 2 * K], "uint16")
     for _n in ("LA", "LB"):
         SCRATCH["%s%d" % (_n, _r)] = ("sbuf", [128, K], "uint16")
-SEMAPHORES = ["cv", "cs", "ct", "cg", "dnx", "dx", "du", "dv", "dwc", "dws", "dout", "lsem"] + ["%s%d" % (k, r) for r in (1, 2, 3) for k in ("aN", "aA", "aB", "aQ")]
+SEMAPHORES = ["cv", "cs", "ct", "cg", "dnx", "dx", "du", "dv", "dwc", "dws", "dout", "lsem", "aN0"] + ["%s%d" % (k, r) for r in (1, 2, 3) for k in ("aN", "aA", "aB", "aQ")]
 
 
 def rank_program(g, core, T, topo):
@@ -75,6 +76,7 @@ def rank_program(g, core, T, topo):
     eng = {"v": g.vector, "s": g.scalar, "t": g.tensor, "g": g, "y": g.sync}
     known = {q: {} for q in eng}
     count = {q: 0 for q in eng}
+    long = {q: False for q in eng}
     clocks, wr, rd, total = {}, {}, {}, {}
 
     def over(a, b):
@@ -101,6 +103,8 @@ def rank_program(g, core, T, topo):
                     need[ev] = 1
         for sem, n in sorted(need, key=lambda e: -len(clocks.get(e, {})) * 100000 - e[1]):
             if known[q].get(sem, 0) < n:
+                if sem == "c" + q and long[q]:
+                    n = max(n, count[q] - 1)
                 eng[q].wait_ge(T.sem[sem], n)
                 learn(q, sem, n)
 
@@ -115,6 +119,7 @@ def rank_program(g, core, T, topo):
     def op(q, f, reads, writes):
         sync(q, reads, writes)
         count[q] += 1
+        long[q] = any(w[2] - w[1] >= 96 for w in writes) and not any(w[0] == "ru" or w[0][0] == "L" for w in writes)
         sem = "c" + q
         f().then_inc(T.sem[sem], 1)
         total[sem] = count[q]
@@ -139,10 +144,10 @@ def rank_program(g, core, T, topo):
 
     def lane(name, k):
         o = RF[name][0]
-        return (T.rf[:, o + k:o + 2 * K:2], [("%s#%d" % (name, k), 0, K)])
+        return (T.rf[:, o + k:o + 3 * K:3], [("%s#%d" % (name, k), 0, K)])
 
     def lanes(name):
-        return (N("rf", name)[0], lane(name, 0)[1] + lane(name, 1)[1])
+        return (N("rf", name)[0], lane(name, 0)[1] + lane(name, 1)[1] + lane(name, 2)[1])
 
     def ind(w, o):
         return (w[0].indirect(o[0]), w[1] + o[1])
@@ -156,17 +161,18 @@ def rank_program(g, core, T, topo):
     def strip(buf, b, a, e):
         return (T[buf][:, 4 * a + b:4 * e:4], [("%s#%d" % (buf, b), a, e)])
 
+    def split(regs, *numbers):
+        for s in numbers:
+            if isinstance(s, tuple):
+                regs += s[1]
+        return [s[0] if isinstance(s, tuple) else s for s in numbers]
+
     def tt(out, a, b, o):
         op("v", lambda: g.vector.tensor_tensor(out[0], a[0], b[0], o), a[1] + b[1], out[1])
 
     def ts(out, a, s1, o1, s2=None, o2=None):
         regs = list(a[1])
-        if isinstance(s1, tuple):
-            regs += s1[1]
-            s1 = s1[0]
-        if isinstance(s2, tuple):
-            regs += s2[1]
-            s2 = s2[0]
+        s1, s2 = split(regs, s1, s2)
         if o2 is None:
             op("v", lambda: g.vector.tensor_scalar(out[0], a[0], s1, None, o1), regs, out[1])
         else:
@@ -180,22 +186,18 @@ def rank_program(g, core, T, topo):
 
     def act(out, a, scale=1.0, bias=0.0, func=IDENT):
         regs = list(a[1])
-        if isinstance(scale, tuple):
-            regs += scale[1]
-            scale = scale[0]
-        elif bias == 0.0 and scale == 1.0 and func == IDENT:
+        if (scale, bias, func) == (1.0, 0.0, IDENT):
             return op("s", lambda: g.scalar.activation(out[0], a[0], COPY), regs, out[1])
+        scale, bias = split(regs, scale, bias)
         op("s", lambda: g.scalar.activation(out[0], a[0], func, bias=bias, scale=scale), regs, out[1])
+
+    def count_zero(out, junk, a):
+        op("s", lambda: g.scalar.activation(junk[0], a[0], RELU, bias=-207.0, scale=-1.0, accum_out=out[0]), a[1], junk[1] + out[1])
 
     def scan(out, a, b, init, o1, o2):
         regs = a[1] + b[1]
-        if isinstance(init, tuple):
-            regs = regs + init[1]
-            init = init[0]
+        init = split(regs, init)[0]
         op("v", lambda: g.vector.tensor_tensor_scan(out[0], a[0], b[0], init, o1, o2), regs, out[1])
-
-    def memset(out, v):
-        op("v", lambda: g.vector.memset(out[0], v), [], out[1])
 
     def iota(out, pattern, base, cm):
         op("g", lambda: g.iota(out[0], pattern, base, cm, allow_small_or_imprecise_dtypes=True), [], out[1])
@@ -226,9 +228,9 @@ def rank_program(g, core, T, topo):
         total[sem] = n
         mark((sem, n), None, [], regs)
 
-    def send_list(src, a, e, dst, sem, m):
-        send(peer(m), sem, [(T[dst][:, 0:e - a], T[src][:, a:e])], [(src, a, e)])
-        arrives(peer(m), sem, 1, [(dst, 0, e - a)])
+    def send_list(src, a, e, dst, sem, m, at=0):
+        send(peer(m), sem, [(T[dst][:, at:at + e - a], T[src][:, a:e])], [(src, a, e)])
+        arrives(peer(m), sem, 1, [(dst, at, at + e - a)])
 
     def send_state(r, m):
         xq, xs, lq, lp = "xq%d" % (r - 1), "xs%d" % (r - 1), "lq%d" % r, "lp%d" % r
@@ -249,7 +251,7 @@ def rank_program(g, core, T, topo):
         for b in planes:
             act(plane(dst, b), P(ps, b, C), scale=0.5)
 
-    mask, hm, io, pw = N("rb", "mask"), N("rb", "hm"), N("rb", "iota"), N("rf", "pw", 15, 16)
+    cx, io, pw = N("rb", "cx"), N("rb", "iota"), N("rf", "pw", 15, 16)
 
     def hold(src, dst, a=0, e=C):
         scan(N("rf", dst, a, e), N("rb", "cx", 0, e - a), N("rf", src, a, e), 0.0, MUL, MAX)
@@ -267,66 +269,65 @@ def rank_program(g, core, T, topo):
         act(N("rf", dst, cut, C), ind(win, A(buf, at + cut // 16, at + K)), bias=bias)
 
     dma("y", "dnx", N("ri", "nx")[0], T.nx[:], [], N("ri", "nx")[1])
-    dma("y", "dx", T.xt0[:], T.x[:], [], [("xt0", 0, 4 * C)])
     dma("y", "du", T.uin[:], T.u[:], [], [("uin", 0, 512)])
+    dma("y", "dx", T.xt0[:], T.x[:], [], [("xt0", 0, 4 * C)])
     dma("y", "dwc", T.wq[:].bitcast(dt.uint8), T.wc[:], [], [("wq", 0, 512)])
     dma("y", "dws", T.wp[:], T.ws[:], [], [("wp", 0, 512)])
     dma("y", "dv", T.vin[:], T.v[:], [], [("vin", 0, 512)])
 
     one = lambda n: A("one", 0, n)
-    memset(one(528), 1.0)
+    op("v", lambda: g.vector.memset(one(528)[0], 1.0), [], one(528)[1])
     op("g", lambda: g.iota(N("ri", "p")[0], [[0, 1]], 0, 1), [], N("ri", "p")[1])
     iota(N("rb", "t16"), [[0, K], [1, 16]], 0, 0)
-    op("g", lambda: g.iota(N("ri", "pick")[0], [[16, 8]], 0, 0), [], N("ri", "pick")[1])
-    iota(N("rf", "j16"), [[16, K]], 0, 0)
-    op("g", lambda: g.affine_select(T.et[:, 0:515], one(515)[0], [[1, 515]], EQ, 0.0, -3, -4), one(515)[1], [("et", 0, 515)])
-    scan(N("rf", "i1024"), one(C), one(C), 1023.0, MUL, ADD)
-    act(io, N("rf", "i1024"), bias=-1232.0)
     ts(N("ri", "p16"), N("ri", "p"), 15, AluOpType.bitwise_and)
+    scan(N("rf", "i1024"), one(C), one(C), 1023.0, MUL, ADD)
+    vcopy(N("rf", "p16"), N("ri", "p16"))
     for s in range(4):
         ts(N("ri", "bit", s, s + 1), N("ri", "p"), s, AluOpType.logical_shift_right, 1, AluOpType.bitwise_and)
-    vcopy(N("rf", "p16"), N("ri", "p16"))
-    vcopy(N("rf", "bit"), N("ri", "bit"))
     for r in (1, 2, 3):
-        memset(lane("fd_%d" % r, 0), 0.0)
-    memset(N("rb", "PE", 0, 1), -208.0)
-    for r in (2, 3):
-        memset(N("rb", "PW_%d" % r, 0, 1), -208.0)
-        memset(N("rb", "PW_%d" % r, C, C + 1), -207.0)
-    ts(mask, N("rb", "t16"), N("rf", "p16"), EQ)
-    vcopy(N("ru", "pick"), N("ri", "pick"))
-    act(N("rb", "cx"), mask, scale=-2.0, bias=2.0)
-    act(N("rb", "cp"), N("rb", "mask", 0, 16), scale=-0.5, bias=0.5)
-    act(N("rf", "nb"), N("rf", "bit", 0, 1), scale=-1024.0, bias=1024.0)
-    ts(lane("fe_1", 1), N("rf", "j16"), N("rf", "p16"), ADD)
-    scan(N("rf", "pw"), N("rb", "cp"), N("rb", "mask", 0, 16), 0.0, MUL, ADD)
+        act(N("rb", "ds%d" % r, 1, 16), one(15))
+        for k in (0, 1):
+            act(lane("fd_%d" % r, k), one(K), scale=float(k))
+            if r > 1:
+                act(N("rb", "PW_%d" % r, k * C, k * C + 1), one(1), scale=k - 208.0)
+    act(N("rb", "PE", 0, 1), one(1), scale=-208.0)
 
     W = lambda s, a=0, e=C: N("rf", "W%d" % s, a, e)
+    m16 = N("rb", "mask", 0, 16)
     vcopy(A("L0", 0, K), N("ri", "nx"))
+    send_list("L0", 0, K, "LN1", "aN0", MASKS[0])
+    op("g", lambda: g.affine_select(T.et[:, 0:515], one(515)[0], [[1, 515]], EQ, 0.0, -3, -4), one(515)[1], [("et", 0, 515)])
+    op("g", lambda: g.iota(N("ri", "pick")[0], [[16, 8]], 0, 0), [], N("ri", "pick")[1])
+    iota(N("rf", "j16"), [[16, K]], 0, 0)
+    ts(cx, N("rb", "t16"), N("rf", "p16"), NE, 2.0, MUL)
     shared("W1", N("rf", "i1024"), "L0", 0, 0)
     shared("W2", W(1), "L0", 0, 0)
     scatter(N("rf", "w0"), A("L0", 0, K), N("rf", "i1024"))
+    vcopy(N("rf", "bit"), N("ri", "bit"))
+    act(N("rb", "cp"), N("rb", "cx", 0, 16), scale=0.25)
+    act(m16, N("rb", "cx", 0, 16), scale=-0.5, bias=1.0)
+    act(N("rf", "nb"), N("rf", "bit", 0, 1), scale=-1024.0, bias=1024.0)
     for s in (1, 2, 3):
-        act(N("rb", "mb%d" % s), N("rb", "mask", 0, 16), scale=N("rf", "bit", s, s + 1))
-        act(N("rb", "ds%d" % s, 1, 16), one(15))
+        act(N("rb", "mb%d" % s), m16, scale=N("rf", "bit", s, s + 1))
         act(N("rb", "ds%d" % s, 0, 1), N("rf", "bit", s, s + 1), scale=-1.0, bias=1.0)
-    hold("w0", "w0s")
+    act(N("rf", "fo0"), W(1, 0, 1), scale=N("rf", "bit", 0, 1), bias=N("rf", "nb"))
+    act(io, N("rf", "i1024"), bias=-1232.0)
+    hold("w0", "w0s", 0, 288)
     hold("W2", "S2")
-    listed(A("L0", K, 2 * K), "w0s", -1024.0)
+    scan(N("rf", "pw"), N("rb", "cp"), m16, 0.0, MUL, ADD)
+    hold("w0", "w0s", 288, C)
     listed(N("ru", "G2"), "S2", -1024.0)
-    send_list("L0", 0, 2 * K, "LN1", "aN1", MASKS[0])
+    listed(A("L0", K, 2 * K), "w0s", -1024.0)
     ts(N("ru", "q1"), W(1, 0, 1), -1024.0, ADD, N("rf", "bit", 0, 1), MUL)
-    ts(N("rf", "fo0"), W(1, 0, 1), N("rf", "bit", 0, 1), MUL, N("rf", "nb"), ADD)
+    send_list("L0", K, 2 * K, "LN1", "aN1", MASKS[0], K)
 
     def power(s, k, cut=CUT):
         shared("W%d" % s, W(s - k), "ru", RU["G%d" % k][0], cut)
 
-    def as_list(s, *between, cut=CUT):
-        if cut:
-            hold("W%d" % s, "S%d" % s, 0, cut)
-        hold("W%d" % s, "S%d" % s, cut, C)
-        for f in between:
-            f()
+    def as_list(s, between):
+        hold("W%d" % s, "S%d" % s, 0, CUT)
+        hold("W%d" % s, "S%d" % s, CUT, C)
+        between()
         listed(N("ru", "G%d" % s), "S%d" % s, -1024.0)
 
     def bit(s, part):
@@ -337,9 +338,9 @@ def rank_program(g, core, T, topo):
         if part == 2:
             ts(N("ru", "q%d" % (s + 1)) if s < 3 else N("ru", "OG0", 0, 1), N("rf", "fo%d" % s, 15, 16), -1024.0, ADD)
 
-    def more(s, a, e, part):
+    def more(s, a, e, part, by=vcopy):
         if part == 0:
-            vcopy(N("rf", "or", a + s, e + s), ind(W(s), N("ru", "OG0", a // 16, e // 16)))
+            by(N("rf", "or", a + s, e + s), ind(W(s), N("ru", "OG0", a // 16, e // 16)))
         if part == 1:
             hold("or", "os", a + s, e + s)
         if part == 2:
@@ -348,156 +349,185 @@ def rank_program(g, core, T, topo):
     def constant(b):
         op("v", lambda: g.vector.quantize_mx(T.qe[:, 128 * b:128 * b + 128], T.se[:, 128 * b:128 * b + 128], T.et[:, 3 - b:515 - b]), [("et", 0, 515)], [("qe", 128 * b, 128 * b + 128), ("se", 128 * b, 128 * b + 128)])
 
-    def pick_u():
+    def pick_u(scales):
         pk = N("ru", "pick")
-        op("v", lambda: g.vector.tensor_copy(T.u2[:, 0:128].bitcast(dt.uint32), T.qu[:, 0:128].bitcast(dt.uint32).indirect(pk[0])), [("qu", 0, 128)] + pk[1], [("u2", 0, 128)])
-        op("s", lambda: g.scalar.activation(T.s2[:, 0:128], T.su[:, 0:128].indirect(pk[0]), COPY), [("su", 0, 128)] + pk[1], [("s2", 0, 128)])
+        if scales:
+            op("s", lambda: g.scalar.activation(T.s2[:, 0:128], T.su[:, 0:128].indirect(pk[0]), COPY), [("su", 0, 128)] + pk[1], [("s2", 0, 128)])
+        else:
+            op("v", lambda: g.vector.tensor_copy(T.u2[:, 0:128].bitcast(dt.uint32), T.qu[:, 0:128].bitcast(dt.uint32).indirect(pk[0])), [("qu", 0, 128)] + pk[1], [("u2", 0, 128)])
 
     def guests(r):
-        tt(N("rb", "g_%d" % r, 0, C), ind(N("rb", "sg_%d" % r, 0, C), A("LN%d" % r, 0, K)), N("rb", "sh_%d" % r, 0, C), GT)
+        tt(N("rb", "g_%d" % r), ind(N("rb", "sg_%d" % r), A("LN%d" % r, 0, K)), N("rb", "sh_%d" % r), GT)
 
-    def leavers(r):
-        tt(N("rb", "l_%d" % r, 0, C), ind(N("rb", "sg_%d" % r, 0, C), A("LN%d" % r, K, 2 * K)), N("rb", "sh_%d" % r, 0, C), LT)
+    def leavers(r, a=0, e=C):
+        tt(N("rb", "l_%d" % r, a, e), ind(N("rb", "sg_%d" % r), A("LN%d" % r, K + a // 16, K + e // 16)), N("rb", "sh_%d" % r, a, e), LT)
 
     def slots(r, part):
         if part == 0:
-            scan(N("rb", "ls_%d" % r, 0, C), N("rb", "c4"), N("rb", "l_%d" % r, 0, C), 0.0, MUL, ADD)
+            scan(N("rb", "ls_%d" % r), N("rb", "c4"), N("rb", "l_%d" % r), 0.0, MUL, ADD)
         if part == 1:
-            ts(lane("fe_%d" % r, 0), ends("rb", "ls_%d" % r), N("rf", "thr"), GT)
+            ts(lane("fd_%d" % r, 2), ends("rb", "ls_%d" % r), N("rf", "pw2"), MUL, 0.5, GT)
         if part == 2:
             scan(N("rf", "fx_%d" % r), lanes("fd_%d" % r), lanes("fe_%d" % r), 0.0, MUL, ADD)
         if part == 3:
             o = RF["fx_%d" % r][0]
-            vcopy(N("ru", "x_%d" % r), A("rf", o + 1, o + 2 * K, 2))
+            vcopy(N("ru", "x_%d" % r), A("rf", o + 2, o + 3 * K, 3))
 
     power(4, 2)
     bit(1, 0)
-    power(6, 2)
+    vcopy(N("ru", "pick"), N("ri", "pick"))
     bit(1, 1)
-    act(hm, mask, scale=-1.0, bias=1.0)
-    power(8, 2)
+    power(6, 2)
     bit(1, 2)
-    as_list(8, lambda: bit(2, 0))
+    quant("qu", "su", "uin", 0, 128, 0)
+    bit(2, 0)
+    power(8, 2)
     bit(2, 1)
+    as_list(8, lambda: bit(2, 2))
+    pick_u(1)
+    act(N("rb", "c4"), cx, scale=2.0)
+    bit(3, 0)
     power(16, 8, 0)
-    bit(2, 2)
     quant("xq0", "xs0", "xt0", 0, C, 0)
     send_state(1, MASKS[0])
-    bit(3, 0)
-    power(24, 8, 0)
-    quant("qu", "su", "uin", 0, 128, 0)
     bit(3, 1)
-    pick_u()
+    pick_u(0)
     bit(3, 2)
-    power(32, 8)
+    power(24, 8)
     more(16, 0, 16, 0)
-    signs(1, 0)
-    signs(1, 1)
-    as_list(32, lambda: more(16, 0, 16, 1))
+    more(16, 0, 16, 1)
+    power(32, 8)
     more(16, 0, 16, 2)
-    power(64, 32, 0)
-    more(32, 0, 32, 0)
-    guests(1)
+    signs(1, 0)
+    as_list(32, lambda: more(32, 0, 32, 0))
     more(32, 0, 32, 1)
-    power(96, 32, 0)
-    act(N("rb", "c4"), mask, scale=-4.0, bias=4.0)
+    signs(1, 1)
+    power(64, 32, 0)
+    constant(0)
     more(32, 0, 32, 2)
     leavers(1)
-    more(64, 0, 64, 0)
-    power(128, 32)
-    more(64, 0, 64, 1)
-    vcopy(N("rf", "h1"), A("LN1", K, 2 * K))
-    more(64, 0, 64, 2)
-    scan(N("rf", "p4"), N("rb", "c4", 0, 16), N("rb", "mask", 0, 16), 0.0, MUL, ADD)
-    power(160, 32, 0)
-    more(128, 0, 128, 0)
-    ts(N("rf", "thr"), N("rf", "p4", 15, 16), 0.5, MUL)
-    more(128, 0, 128, 1)
-    tt(N("rf", "hd_1"), N("rf", "h1"), lane("fe_1", 1), SUB)
-    more(128, 0, 128, 2)
-    slots(1, 0)
-    more(160, 96, 256, 0)
-    l1, g1 = N("rb", "l_1", 0, C), N("rb", "g_1", 0, C)
-    so1, go1 = lambda a, e: N("rb", "so_1", a, e), lambda a, e: N("rb", "go_1", a, e)
-    act(so1(0, 256), ind(l1, N("ru", "OG0", 0, 16)), scale=-1.0, bias=1.0)
-    act(go1(0, 256), ind(g1, N("ru", "OG0", 0, 16)))
-    ts(lane("fd_1", 1), N("rf", "hd_1"), float(C), ADD)
-    more(160, 96, 256, 1)
-    slots(1, 1)
-    more(160, 96, 256, 2)
-    slots(1, 2)
-    vcopy(go1(256, C), ind(g1, N("ru", "OG0", 16, K)))
-    act(so1(256, C), ind(l1, N("ru", "OG0", 16, K)), scale=-1.0, bias=1.0)
-    scan(N("rb", "PE", 1, 257), so1(0, 256), go1(0, 256), -208.0, ADD, ADD)
-    scan(N("rb", "PE", 257, C), so1(256, C - 1), go1(256, C - 1), N("rb", "PE", 256, 257), ADD, ADD)
-    slots(1, 3)
-    scatter(N("rb", "PW_1", 0, C), N("ru", "OG0"), N("rb", "PE"))
-    constant(0)
-    ts(N("rb", "PW_1", C, 2 * C), N("rb", "PW_1", 0, C), 1.0, ADD)
+    power(96, 32, 0)
+    more(64, 0, 64, 0, act)
+    guests(1)
+    power(128, 32, 0)
+    more(96, 32, 64, 0)
+    act(N("rf", "pw2"), pw, func=SQUARE)
+    act(N("rf", "npw"), pw, scale=-1.0)
+    act(lane("fe_1", 2), N("rf", "j16"), bias=N("rf", "p16"))
+    act(lane("fe_1", 1), lane("fe_1", 2), scale=-1.0)
+    ts(lane("fe_1", 0), A("LN1", K, 2 * K), float(C), ADD)
+    more(64, 0, 96, 1)
     constant(1)
+    more(64, 0, 96, 2)
+    slots(1, 0)
+    so1, go1 = lambda a, e: N("rb", "so_1", a, e), lambda a, e: N("rb", "go_1", a, e)
+
+    def weights(a, e, by=act):
+        by(go1(a, e), ind(N("rb", "g_1"), N("ru", "OG0", a // 16, e // 16)))
+        act(so1(a, e), ind(N("rb", "l_1"), N("ru", "OG0", a // 16, e // 16)), scale=-1.0, bias=1.0)
+
+    def before(a, e):
+        scan(N("rb", "PE", a + 1, e + 1), so1(a, e), go1(a, e), N("rb", "PE", a, a + 1) if a else -208.0, ADD, ADD)
+
+    more(128, 32, 160, 0)
+    weights(0, 160)
+    slots(1, 1)
+    more(128, 32, 160, 1)
+    constant(2)
+    more(128, 32, 160, 2)
+    slots(1, 2)
+    more(128, 160, 288, 0)
+    weights(160, 288)
+    constant(3)
+    more(128, 160, 288, 1)
+    slots(1, 3)
+    more(128, 160, 288, 2)
+    before(0, 288)
+    weights(288, C, vcopy)
+    before(288, C - 1)
+    count_zero(N("rf", "i0_1"), N("rb", "am_1", 0, 208), N("rb", "PE", 1, 209))
+    act(N("rf", "or", 0, 16), ind(N("rf", "i1024"), N("ru", "OG0", 0, 1)))
+    unpack("psA", "xq0", "xs0")
+    halves("psA", "th1")
+    scatter(N("rb", "PW_1", 0, C), N("ru", "OG0"), N("rb", "PE"))
+    ts(N("rb", "PW_1", C, 2 * C), N("rb", "PW_1", 0, C), 1.0, ADD)
 
     for r in (1, 2, 3):
         m = MASKS[r - 1]
-        L, LN, LA, LB = "L%d" % r, "LN%d" % r, "LA%d" % r, "LB%d" % r
+        L, LA, LB = "L%d" % r, "LA%d" % r, "LB%d" % r
         nb = lambda k, a=0, b=C: N("rb", "%s_%d" % (k, r), a, b)
-        nu = lambda k: N("ru", "%s_%d" % (k, r))
+        nu = lambda k, a=0, b=C: N("ru", "%s_%d" % (k, r), a // 16, b // 16)
         th, tp, zt, xt = ["%s%d" % (k, r) for k in ("th", "tp", "zt", "xt")]
         zq, zs, xq, xs = ["%s%d" % (k, r) for k in ("zq", "zs", "xq", "xs")]
         PR, Ps = "PR_%d" % r, "Ps_%d" % r
         if r > 1:
-            leavers(r)
-            act(nb("so"), ind(nb("l"), N("ru", "og_%d" % (r - 1))), scale=-1.0, bias=1.0)
+            og = lambda a, e: N("ru", "og_%d" % (r - 1), a // 16, e // 16)
+            leavers(r, *HALF[0])
+            leavers(r, *HALF[1])
+            act(lane("fe_%d" % r, 0), ends("rf", "hs_%d" % (r - 1)), scale=pw, bias=C - 1024.0)
+            halves("psA", th, (0,))
+            act(nb("so"), ind(nb("l"), og(0, C)), scale=-1.0, bias=1.0)
             guests(r)
-            act(nb("go"), ind(nb("g"), N("ru", "og_%d" % (r - 1))))
-            slots(r, 0)
-            tt(lane("fd_%d" % r, 1), N("rf", "hd_%d" % (r - 1)), lane("fe_%d" % r, 1), SUB)
-            slots(r, 1)
-            slots(r, 2)
-            slots(r, 3)
-            scan(nb("PW", 1, C), nb("so", 0, C - 1), nb("go", 0, C - 1), -208.0, ADD, ADD)
-            scan(nb("PW", C + 1, 2 * C), nb("so", 0, C - 1), nb("go", 0, C - 1), -207.0, ADD, ADD)
+            for a, e in PAIR:
+                act(nb("go", a, e), ind(nb("g"), og(a, e)))
+            for part in range(3):
+                slots(r, part)
+            for a, e in PAIR:
+                e = min(e, C - 1)
+                for k in (0, 1):
+                    scan(nb("PW", k * C + a + 1, k * C + e + 1), nb("so", a, e), nb("go", a, e), nb("PW", k * C + a, k * C + a + 1) if a else k - 208.0, ADD, ADD)
+                if not a:
+                    count_zero(N("rf", "i0_%d" % r), nb("am", 0, 208), nb("PW", 1, 209))
+                    slots(r, 3)
         shared(PR, nb("PW", 0, 2 * C), "ru", RU["x_%d" % r][0], bias=1232.0)
+        vcopy(N("ru", "i0_%d" % r), N("rf", "i0_%d" % r))
         if r == 1:
-            constant(2)
+            act(nb("OB", 16 + C, 32 + C), ind(N("rf", "or"), N("ru", "i0_1")), bias=-1232.0)
+        else:
+            act(nb("OB", 16 + C, 32 + C), ind(N("rb", "OB_%d" % (r - 1), 16, 16 + C), N("ru", "i0_%d" % r)))
         hold(PR, Ps, 0, CUT)
         hold(PR, Ps, CUT, C)
         if r == 1:
-            constant(3)
-            unpack("psA", "xq0", "xs0")
+            act(N("rb", "mask", 16, C), N("rb", "cx", 16, C), scale=-0.5, bias=1.0)
             unpack("psB", "lq1", "lp1")
-        halves("psA", th)
-        listed(nu("sc"), Ps, -1023.0)
-        listed(nu("ai"), Ps, -1022.0)
-        scatter(nb("OB", 0, 417), nu("sc"), io)
-        listed(nu("bi"), Ps, -1024.0)
-        vcopy(nb("OB", 417, 418), nb("OB", 1, 2))
-        act(nb("OB", 0, 1), nb("OB", 416, 417))
+            halves("psB", tp, (0, 1))
+        else:
+            halves("psA", th, (1, 2, 3))
         if r < 3:
-            listed(lane("fe_%d" % (r + 1), 1), Ps, -1024.0)
-        tt(nb("am"), ind(nb("OB", 0, 418), nu("ai")), mask, MUL)
-        act(N("rf", "bf_%d" % r), ind(nb("OB", 0, 418), nu("bi")), bias=1232.0)
-        scan(nb("as"), hm, nb("am"), 0.0, MUL, ADD)
-        ts(A(L, 0, K), ends("rb", "as_%d" % r), 208.0, ADD)
+            act(lane("fe_%d" % (r + 1), 2), ends("rf", Ps), scale=pw, bias=-1024.0)
+            act(lane("fe_%d" % (r + 1), 1), ends("rf", Ps), scale=N("rf", "npw"), bias=1024.0)
+        listed(nu("sc"), Ps, -1024.0)
+        listed(nu("ai"), Ps, -1023.0)
+        scatter(nb("OB", 16, 16 + C), nu("sc"), io)
+        listed(nu("bi"), Ps, -1009.0)
+        act(nb("OB", 15, 16), nb("OB", 15 + C, 16 + C))
+        for a, e in HALF:
+            tt(nb("am", a, e), ind(nb("OB", 16, 17 + C), nu("ai", a, e)), N("rb", "mask", 0, e - a), MUL)
+        act(N("rf", "bf_%d" % r), ind(nb("OB", 0, 16 + C), nu("bi")), bias=1232.0)
+        for a, e in HALF:
+            scan(nb("as", a, e), N("rb", "cx", 0, e - a), nb("am", a, e), 0.0, MUL, ADD)
+        hold("bf_%d" % r, "bs_%d" % r, 0, 96)
+        ts(A(L, 0, K), ends("rb", "as_%d" % r), pw, MUL, 208.0, ADD)
         send_list(L, 0, K, LA, "aA%d" % r, m)
-        hold("bf_%d" % r, "bs_%d" % r)
+        hold("bf_%d" % r, "bs_%d" % r, 96, C)
         listed(A(L, K, 2 * K), "bs_%d" % r, -1024.0)
         send_list(L, K, 2 * K, LB, "aB%d" % r, m)
         if r < 3:
             send_list(L, 0, 2 * K, "LN%d" % (r + 1), "aN%d" % (r + 1), MASKS[r])
-            act(N("rf", "of_%d" % r), nb("OB", 1, 417), bias=1232.0)
-            hold("of_%d" % r, "os_%d" % r)
+        if r > 1:
+            unpack("psB", "lq%d" % r, "lp%d" % r)
+        halves("psB", tp, (2, 3) if r == 1 else range(4))
+
+        def predecessors(by, b, a, e):
+            by(plane("tb", b, a, e), ind(plane(th, b), A(L, K + a // 16, K + e // 16)))
+
+        for b in range(4):
+            who = [TB[r][i][b] for i in (0, 1)]
+            for w, (a, e) in ([(who[0], (0, C))] if who[0] == who[1] else zip(who, HALF)):
+                if w != "l":
+                    predecessors(vcopy if w == "v" else act, b, a, e)
         if r == 1:
             quant("qv", "sv", "vin", 0, 128, 0)
-        else:
-            unpack("psB", "lq%d" % r, "lp%d" % r)
-        if r < 3:
-            listed(nu("og"), "os_%d" % r, -1024.0)
-        halves("psB", tp)
-        for b in range(4):
-            if b in OWN_TB[r]:
-                vcopy(plane("tb", b), ind(plane(th, b), A(L, K, 2 * K)))
-            elif b not in LATE_TB[r]:
-                act(plane("tb", b), ind(plane(th, b), A(L, K, 2 * K)))
 
         def pack_z(i):
             a, e = HALF[i]
@@ -511,20 +541,28 @@ def rank_program(g, core, T, topo):
                 tt(strip(zt, b, a, e), ind(plane(tp, b), A(LB, a // 16, e // 16)), plane("za", b, a, e), ADD)
                 if (i, b) == (1, 0):
                     pack_z(0)
+        if r < 3:
+            act(N("rf", "of_%d" % r), nb("OB", 16, 16 + C), bias=1232.0)
         pack_z(1)
-        a, e = HALF[0]
+        if r < 3:
+            hold("of_%d" % r, "os_%d" % r, 0, 256)
         for b in range(4):
-            act(plane("hh", b, a, e), P("psA", b, e - a), scale=0.015625)
-        a, e = HALF[1]
-        ts(plane("hh", 0, a, e), P("psB", 0, e - a), 0.015625, MUL)
-        for b in (1, 2, 3):
-            act(plane("hh", b, a, e), P("psB", b, e - a), scale=0.015625)
-        for b in LATE_TB[r]:
-            act(plane("tb", b), ind(plane(th, b), A(L, K, 2 * K)))
+            for i, (a, e) in enumerate(HALF):
+                if (b, i) == (0, 1):
+                    ts(plane("hh", b, a, e), P("psB", b, e - a), 0.015625, MUL)
+                else:
+                    act(plane("hh", b, a, e), P("psB" if i else "psA", b, e - a), scale=0.015625)
+            if TB[r][0][b] == "l":
+                predecessors(act, b, *HALF[0])
+        if r < 3:
+            hold("of_%d" % r, "os_%d" % r, 256, C)
+        for b in range(4):
+            if TB[r][1][b] == "l":
+                predecessors(act, b, *HALF[1])
         if r < 3:
             act(N("rf", "hf_%d" % r), ind(N("rf", PR), A("LN%d" % (r + 1), K, 2 * K)))
         else:
-            act(N("rf", "nr"), ind(nb("OB", 0, 418), nu("ai")), bias=208.0)
+            act(N("rf", "nr"), ind(nb("OB", 16, 17 + C), nu("ai")), bias=208.0)
             dma("y", "dout", T.nr[:, :], T.rf[0:128:16, RF["nr"][0]:RF["nr"][0] + C], N("rf", "nr")[1], [])
 
         def pack_x(i):
@@ -535,26 +573,23 @@ def rank_program(g, core, T, topo):
             else:
                 mm(P("psA", i, e - a), "qv", "sv", 0, xq, xs, a, e)
                 dma("y", "dout", T.oc[:, 4 * a:4 * e], T[xq][:, a:e].bitcast(dt.uint8), [(xq, a, e)], [])
-                for k in range(4):
-                    dma("s" if i and k > 1 else "y", "dout", T.osc[4 * k:4 * k + 4, a:e], T[xs][32 * k:32 * k + 4, a:e], [(xs, a, e)], [])
-                if i:
-                    vcopy(A("yo", a, e), P("psA", i, e - a))
-                else:
-                    act(A("yo", a, e), P("psA", i, e - a))
+                for k in range(4 * i):
+                    dma("s" if k > 1 else "y", "dout", T.osc[4 * k:4 * k + 4, 0:C], T[xs][32 * k:32 * k + 4, 0:C], [(xs, 0, C)], [])
+                (vcopy if i else act)(A("yo", a, e), P("psA", i, e - a))
                 dma("s", "dout", T.y[:, a:e], T.yo[:, a:e], [("yo", a, e)], [])
 
-        late = [b for b in range(4) if b not in LATE_TB[r]] + list(LATE_TB[r])
         for i, (a, e) in enumerate(HALF):
-            for k, b in enumerate(late):
+            for b in range(4):
                 tt(strip(xt, b, a, e), ind(plane("hh", b), A(L, a // 16, e // 16)), plane("tb", b, a, e), ADD)
-                if (i, k) == (1, 0):
+                if (i, b) == (1, 0):
                     pack_x(0)
+        if r < 3:
+            listed(nu("og"), "os_%d" % r, -1024.0)
         pack_x(1)
         if r < 3:
             send_state(r + 1, MASKS[r])
             unpack("psA", xq, xs)
             hold("hf_%d" % r, "hs_%d" % r)
-            listed(N("rf", "hd_%d" % r), "hs_%d" % r, C - 1024.0)
 
-    for sem in sorted(total):
+    for sem in sorted(total, key=lambda k: (k == "dout", k in ("cv", "cs", "ct"), k)):
         g.wait_ge(T.sem[sem], total[sem])

@@ -1,17 +1,20 @@
-from concourse.mybir import dt, AluOpType, AxisListType, ActivationFunctionType
+from concourse.mybir import dt, AluOpType, ActivationFunctionType
 
-ADD, SUB, MUL, MAX = AluOpType.add, AluOpType.subtract, AluOpType.mult, AluOpType.max
-GT, LT, EQ, NE = AluOpType.is_gt, AluOpType.is_lt, AluOpType.is_equal, AluOpType.not_equal
+ADD, SUB, MUL, MIN = AluOpType.add, AluOpType.subtract, AluOpType.mult, AluOpType.min
+GT, EQ, NE = AluOpType.is_gt, AluOpType.is_equal, AluOpType.not_equal
 COPY, IDENT, SIGN = ActivationFunctionType.Copy, ActivationFunctionType.Identity, ActivationFunctionType.Sign
-SQUARE, RELU = ActivationFunctionType.Square, ActivationFunctionType.Relu
 C = 416
 K = C // 16
+S = 2 * C
 MASKS = [1, 2, 3]
-HALF = [(0, 288), (288, 416)]
-PAIR = [(0, 256), (256, 416)]
-CUT = 160
+ZRUN = [(0, 288), (288, 416)]
+XRUN = [(0, 256), (256, 416)]
+TB = {1: ("vsss", "vsmm"), 2: ("vsmm", "vlll"), 3: ("vvvs", "vvmm")}
 TINY = 2.0 ** -93
-TB = {1: ("vvss", "vlll"), 2: ("vvvl", "vsll"), 3: ("vvvs", "vlll")}
+SPREAD = [(0, 32, 4, 515), (32, 160, 2, 257), (160, 416, 1, 0)]
+EARLY = 160
+WIDE = 640
+FW0 = 432
 
 
 def layout(items):
@@ -22,21 +25,22 @@ def layout(items):
     return at, n
 
 
-_rb = [(k, C) for k in ("mask", "cx", "c4", "iota", "t16", "PE")] + [("cp", 16)]
-_rb += [("%s%d" % (k, s), 16) for s in (1, 2, 3) for k in ("mb", "ds")]
-_rb += [("%s_%d" % (k, r), C) for r in (1, 2, 3) for k in ("sg", "sh", "g", "l", "ls", "so", "go", "am", "as")]
-_rb += [("OB_%d" % r, 448) for r in (1, 2, 3)] + [("PW_%d" % r, 2 * C) for r in (1, 2, 3)]
-RB, NRB = layout(_rb)
-_ru = [("G%d" % s, K) for s in (2, 8, 32)] + [("OG0", K), ("pick", 8)] + [("i0_%d" % r, 1) for r in (1, 2, 3)] + [("q%d" % s, 1) for s in (1, 2, 3)]
-_ru += [("%s_%d" % (k, r), K) for r in (1, 2, 3) for k in ("x", "sc", "ai", "bi", "og")]
-RU, NRU = layout(_ru)
 POWERS = (1, 2, 4, 6, 8, 16, 24, 32, 64, 96, 128)
-_rf = [(k, C) for k in ("i1024", "w0", "w0s", "or", "os", "nr", "S2", "S8", "S32")] + [("W%d" % s, C) for s in POWERS]
-_rf += [("p16", 1), ("pw", 16), ("pw2", 1), ("npw", 1), ("bit", 4), ("nb", 1), ("fo0", 1), ("j16", K)] + [("i0_%d" % r, 1) for r in (1, 2, 3)]
+_rb = [(k, C) for k in ("cb", "name")] + [(k, 16) for k in ("m16", "tab", "i16", "i15")] + [("ones", S), ("free", 3 * S), ("fd", 3 * C + 16)]
+_rb += [("%s%d" % (k, s), 16) for s in (1, 2, 3) for k in ("mb", "ds")]
+_rb += [("%s_%d" % (k, r), C) for r in (1, 2, 3) for k in ("uh", "du", "ar", "br", "as", "bs")]
+_rb += [("sg_%d" % r, WIDE) for r in (1, 2, 3)] + [("FW_%d" % r, FW0 + S) for r in (1, 2, 3)] + [("BW_%d" % r, S + 224) for r in (1, 2, 3)]
+_rb += [("%s_%d" % (k, r), S) for r in (1, 2) for k in ("full", "CN")]
+_rb += [(k, C) for k in ("own", "i2", "w0", "w0s", "or", "os", "S2", "S8", "S32", "P1", "PY", "PYs")] + [("W%d" % s, C) for s in POWERS]
+_rb += [("%s_%d" % (k, r), C) for r in (1, 2) for k in ("Ps", "hf", "hs")] + [("PR_%d" % r, WIDE) for r in (1, 2)]
+RB, NRB = layout(_rb)
+_ru = [("G%d" % s, K) for s in (2, 8, 32)] + [("OG0", K), ("pick", 8), ("same", K), ("y", K)] + [("q%d" % s, 1) for s in (1, 2, 3)]
+_ru += [("x_%d" % r, K) for r in (1, 2, 3)]
+RU, NRU = layout(_ru)
+_rf = [("nr", C), ("plain", WIDE + 16), ("tabb", 16), ("bit", 4)] + [(k, 1) for k in ("p16", "p15", "pq", "npq", "npq2", "nq", "nb", "fo0")]
+_rf += [(k, K) for k in ("j16", "h", "d", "xl")]
 _rf += [("%s%d" % (k, s), 16) for s in (1, 2, 3) for k in ("fo", "og")]
-_rf += [("%s_%d" % (k, r), C) for r in (1, 2, 3) for k in ("PR", "Ps", "bf", "bs")]
-_rf += [("%s_%d" % (k, r), C) for r in (1, 2) for k in ("of", "os", "hf", "hs")]
-_rf += [("%s_%d" % (k, r), 3 * K) for r in (1, 2, 3) for k in ("fd", "fe", "fx")]
+_rf += [(k, 3 * K) for k in ("fe", "fx", "fl", "fy")]
 RF, NRF = layout(_rf)
 RI, NRI = layout([("nx", K), ("p", 1), ("p16", 1), ("bit", 4), ("pick", 8)])
 WHERE = {"rb": RB, "ru": RU, "rf": RF, "ri": RI}
@@ -53,20 +57,20 @@ SCRATCH = {
     "psA": ("psum", [128, 2048], "float32"), "psB": ("psum", [128, 2048], "float32"),
     "L0": ("sbuf", [128, 2 * K], "uint16"),
     "xt0": ("sbuf", [128, 4 * C], BF), "xq0": ("sbuf", [128, C], X4), "xs0": ("sbuf", [128, C], U8),
-    "za": ("sbuf", [128, 4 * C], BF), "hh": ("sbuf", [128, 4 * C], BF), "tb": ("sbuf", [128, 4 * C], BF),
+    "th": ("sbuf", [128, 4 * WIDE], BF), "hh": ("sbuf", [128, 4 * WIDE], BF), "tb": ("sbuf", [128, 4 * C], BF),
+    "tp": ("sbuf", [128, 4 * WIDE], BF), "za": ("sbuf", [128, 4 * C], BF),
 }
 for _r in (1, 2, 3):
-    for _n in ("th", "tp", "zt", "xt"):
+    for _n in ("zt", "xt"):
         SCRATCH["%s%d" % (_n, _r)] = ("sbuf", [128, 4 * C], BF)
     for _n in ("xq", "lq", "zq"):
         SCRATCH["%s%d" % (_n, _r)] = ("sbuf", [128, C], X4)
     for _n in ("xs", "lp", "zs"):
         SCRATCH["%s%d" % (_n, _r)] = ("sbuf", [128, C], U8)
-    for _n in ("L", "LN"):
-        SCRATCH["%s%d" % (_n, _r)] = ("sbuf", [128, 2 * K], "uint16")
-    for _n in ("LA", "LB"):
+    for _n in ("LA", "LB", "LN", "RA", "RB"):
         SCRATCH["%s%d" % (_n, _r)] = ("sbuf", [128, K], "uint16")
-SEMAPHORES = ["cv", "cs", "ct", "cg", "dnx", "dx", "du", "dv", "dwc", "dws", "dout", "lsem", "aN0"] + ["%s%d" % (k, r) for r in (1, 2, 3) for k in ("aN", "aA", "aB", "aQ")]
+SEMAPHORES = ["cv", "cs", "ct", "cg", "dnx", "dx", "du", "dv", "dwc", "dws", "dout", "lsem"] + ["a%s%d" % (k, r) for r in (1, 2, 3) for k in "NAB"]
+SEMAPHORES += ["aQ%d_%d" % (r, i) for r in (1, 2, 3) for i in (0, 1, 2)]
 
 
 def rank_program(g, core, T, topo):
@@ -134,29 +138,55 @@ def rank_program(g, core, T, topo):
     def A(buf, a, b, step=1):
         return (T[buf][:, a:b] if step == 1 else T[buf][:, a:b:step], [(buf, a, b)])
 
-    def N(buf, name, a=0, b=None):
+    def N(buf, name, a=0, b=None, step=1):
         o, w = WHERE[buf][name]
-        return A(buf, o + a, o + (w if b is None else b))
+        return A(buf, o + a, o + (w if b is None else b), step)
 
-    def ends(buf, name, a=0, e=C):
-        o = WHERE[buf][name][0]
-        return A(buf, o + a + 15, o + e, 16)
+    def back(name, hi, lo, step=1):
+        o = RB[name][0]
+        return (T.rb[:, o + hi:o + lo - 1:-step], [("rb", o + lo, o + hi + 1)])
+
+    def ends(name, a=0, e=C):
+        o = RB[name][0]
+        return A("rb", o + a + 15, o + e, 16)
 
     def lane(name, k):
         o = RF[name][0]
         return (T.rf[:, o + k:o + 3 * K:3], [("%s#%d" % (name, k), 0, K)])
 
     def lanes(name):
-        return (N("rf", name)[0], lane(name, 0)[1] + lane(name, 1)[1] + lane(name, 2)[1])
+        return (N("rf", name)[0], [r for k in range(3) for r in lane(name, k)[1]])
+
+    def factor(k):
+        o = RB["fd"][0]
+        if k == "row":
+            return (T.rb[:, o:o + 3 * C:3], [("fd#1", 0, C)])
+        if k is None:
+            return (T.rb[:, o + 29:o + 3 * C + 16:16], [("fd#%d" % i, 0, C) for i in range(3)])
+        return (T.rb[:, o + 29 + 16 * k:o + 3 * C + 16:48], [("fd#%d" % k, 0, C)])
+
+    def spread(buf, at, a, e):
+        out = []
+        for p, q, step, o in SPREAD:
+            lo, hi = max(a, p), min(e, q)
+            if lo < hi:
+                out.append((lo, hi, A(buf, at + o + step * (lo - p), at + o + step * (hi - 1 - p) + 1, step)))
+        return out
 
     def ind(w, o):
         return (w[0].indirect(o[0]), w[1] + o[1])
 
-    def P(buf, bank, n):
-        return (T[buf][:, 512 * bank:512 * bank + n], [(buf, 512 * bank, 512 * bank + 512)])
+    def P(buf, bank, a, e):
+        return (T[buf][:, 512 * bank + a:512 * bank + e], [(buf, 512 * bank, 512 * bank + 512)])
 
     def plane(buf, b, a=0, e=C):
         return A(buf, C * b + a, C * b + e)
+
+    def wide(buf, b):
+        return A(buf, WIDE * b, WIDE * b + WIDE)
+
+    def part(buf, a, e, at=0):
+        return A(buf, at + a // 16, at + e // 16)
 
     def strip(buf, b, a, e):
         return (T[buf][:, 4 * a + b:4 * e:4], [("%s#%d" % (buf, b), a, e)])
@@ -191,15 +221,12 @@ def rank_program(g, core, T, topo):
         scale, bias = split(regs, scale, bias)
         op("s", lambda: g.scalar.activation(out[0], a[0], func, bias=bias, scale=scale), regs, out[1])
 
-    def count_zero(out, junk, a):
-        op("s", lambda: g.scalar.activation(junk[0], a[0], RELU, bias=-207.0, scale=-1.0, accum_out=out[0]), a[1], junk[1] + out[1])
-
     def scan(out, a, b, init, o1, o2):
         regs = a[1] + b[1]
         init = split(regs, init)[0]
         op("v", lambda: g.vector.tensor_tensor_scan(out[0], a[0], b[0], init, o1, o2), regs, out[1])
 
-    def iota(out, pattern, base, cm):
+    def iota(out, pattern, base, cm=0):
         op("g", lambda: g.iota(out[0], pattern, base, cm, allow_small_or_imprecise_dtypes=True), [], out[1])
 
     def quant(q, s, tile, a, e, t0=None):
@@ -211,62 +238,62 @@ def rank_program(g, core, T, topo):
         op("t", lambda: g.tensor.matmul_mx(out[0], T[lq][:, la:la + 128], T[ls][:, la:la + 128], T[rq][:, a:e], T[rs][:, a:e], True, True),
            [(lq, la, la + 128), (ls, la, la + 128), (rq, a, e), (rs, a, e)], out[1])
 
-    def peer(m):
-        return T.cores[rank ^ m]
-
-    def send(dst, sem, pairs, regs):
+    def send(m, sem, pairs, reads, lands):
+        dst = T.cores[rank ^ m]
         rid, pid = topo.addr(dst)[:2]
-        mask = topo.mask(core, dst)
-        n = len(topo.engines(core, dst))
-        sync("g", regs, [])
+        sync("g", reads, [])
         for out, in_ in pairs:
-            g.remote_dma(out, in_, T.sem[sem], T.sem.lsem, pid, rid, mask)
-            total["lsem"] = total.get("lsem", 0) + n
+            g.remote_dma(out, in_, T.sem[sem], T.sem.lsem, pid, rid, topo.mask(core, dst))
+            total["lsem"] = total.get("lsem", 0) + len(topo.engines(core, dst))
+        total[sem] = len(pairs) * len(topo.engines(dst, core))
+        mark((sem, total[sem]), None, [], lands)
 
-    def arrives(src, sem, k, regs):
-        n = k * len(topo.engines(src, core))
-        total[sem] = n
-        mark((sem, n), None, [], regs)
+    def send_hosts(src, at, r):
+        send(MASKS[r - 1], "aN%d" % r, [(T["LN%d" % r][:, 0:K], T[src][:, at:at + K])], [(src, at, at + K)], [("LN%d" % r, 0, K)])
 
-    def send_list(src, a, e, dst, sem, m, at=0):
-        send(peer(m), sem, [(T[dst][:, at:at + e - a], T[src][:, a:e])], [(src, a, e)])
-        arrives(peer(m), sem, 1, [(dst, at, at + e - a)])
+    def send_ring(k, r):
+        src, dst = "L%s%d" % (k, r), "R%s%d" % (k, r)
+        send(MASKS[r - 1], "a%s%d" % (k, r), [(T[dst][:, 0:K], T[src][:, 0:K])], [(src, 0, K)], [(dst, 0, K)])
 
-    def send_state(r, m):
+    def send_state(r, i, a, e):
         xq, xs, lq, lp = "xq%d" % (r - 1), "xs%d" % (r - 1), "lq%d" % r, "lp%d" % r
-        send(peer(m), "aQ%d" % r, [(T[lq][:, 0:C].bitcast(dt.uint8), T[xq][:, 0:C].bitcast(dt.uint8)), (T[lp][:, 0:C], T[xs][:, 0:C])], [(xq, 0, C), (xs, 0, C)])
-        arrives(peer(m), "aQ%d" % r, 2, [(lq, 0, C), (lp, 0, C)])
+        send(MASKS[r - 1], "aQ%d_%d" % (r, i), [(T[lq][:, a:e].bitcast(dt.uint8), T[xq][:, a:e].bitcast(dt.uint8)), (T[lp][:, a:e], T[xs][:, a:e])],
+             [(xq, a, e), (xs, a, e)], [(lq, a, e), (lp, a, e)])
+
+    def sign_row(r, a, e):
+        o = RB["sg_%d" % r][0]
+        return spread("rb", o, a, e) if r > 1 else [(a, e, A("rb", o + a, o + e))]
 
     def signs(r, i):
-        a, e = HALF[i]
-        mm(P("psB", i, e - a), "u2", "s2", 0, "xq%d" % (r - 1), "xs%d" % (r - 1), a, e)
-        for k in ("sg", "sh"):
-            act(N("rb", "%s_%d" % (k, r), a, e), P("psB", i, e - a), bias=-TINY, func=SIGN)
+        a, e = XRUN[i]
+        mm(P("psA", i, 0, e - a), "u2", "s2", 0, "xq%d" % (r - 1), "xs%d" % (r - 1), a, e)
+        for lo, hi, out in sign_row(r, a, e):
+            act(out, P("psA", i, lo - a, hi - a), bias=-TINY, func=SIGN)
 
-    def unpack(ps, q, s):
+    def unpack(ps, q, s, a=0, e=C):
         for b in range(4):
-            mm(P(ps, b, C), "qe", "se", 128 * b, q, s, 0, C)
+            mm(P(ps, b, 0, e - a), "qe", "se", 128 * b, q, s, a, e)
 
-    def halves(ps, dst, planes=range(4)):
+    def halves(ps, dst, planes=range(4), a=0, e=C):
         for b in planes:
-            act(plane(dst, b), P(ps, b, C), scale=0.5)
+            for lo, hi, out in spread(dst, WIDE * b, a, e):
+                act(out, P(ps, b, lo - a, hi - a), scale=0.5)
 
-    cx, io, pw = N("rb", "cx"), N("rb", "iota"), N("rf", "pw", 15, 16)
+    pq, npq = N("rf", "pq"), N("rf", "npq")
 
-    def hold(src, dst, a=0, e=C):
-        scan(N("rf", dst, a, e), N("rb", "cx", 0, e - a), N("rf", src, a, e), 0.0, MUL, MAX)
+    def hold(dst, src, n, o=ADD):
+        scan(dst, N("rb", "cb", 0, n), src, 0.0, MUL, o)
 
-    def listed(out, held, shift, a=0, e=C):
-        ts(out, ends("rf", held, a, e), pw, MUL, shift, ADD)
+    def held(src, dst, a=0, e=C):
+        hold(N("rb", dst, a, e), N("rb", src, a, e), e - a)
 
-    def shared(dst, win, buf, at, cut=CUT, bias=0.0):
+    def listed(out, name, a=0, e=C):
+        ts(out, ends(name, a, e), pq, MUL, 208.25, ADD)
+
+    def shared(dst, win, lst, at, cut, scale=1.0, bias=0.0):
         if cut:
-            o = ind(win, A(buf, at, at + cut // 16))
-            if bias:
-                ts(N("rf", dst, 0, cut), o, bias, ADD)
-            else:
-                vcopy(N("rf", dst, 0, cut), o)
-        act(N("rf", dst, cut, C), ind(win, A(buf, at + cut // 16, at + K)), bias=bias)
+            ts(N("rb", dst, 0, cut), ind(win, part(lst, 0, cut, at)), scale, MUL, bias, ADD)
+        act(N("rb", dst, cut, C), ind(win, part(lst, cut, C, at)), scale=scale, bias=bias)
 
     dma("y", "dnx", N("ri", "nx")[0], T.nx[:], [], N("ri", "nx")[1])
     dma("y", "du", T.uin[:], T.u[:], [], [("uin", 0, 512)])
@@ -276,78 +303,85 @@ def rank_program(g, core, T, topo):
     dma("y", "dv", T.vin[:], T.v[:], [], [("vin", 0, 512)])
 
     one = lambda n: A("one", 0, n)
+    p16, m16 = N("rf", "p16"), N("rb", "m16")
+
+    def constant(b):
+        op("v", lambda: g.vector.quantize_mx(T.qe[:, 128 * b:128 * b + 128], T.se[:, 128 * b:128 * b + 128], T.et[:, 3 - b:515 - b]), [("et", 0, 515)], [("qe", 128 * b, 128 * b + 128), ("se", 128 * b, 128 * b + 128)])
+
+    def bit_of_p(s):
+        ts(N("ri", "bit", s, s + 1), N("ri", "p"), s, AluOpType.logical_shift_right, 1, AluOpType.bitwise_and)
+
     op("v", lambda: g.vector.memset(one(528)[0], 1.0), [], one(528)[1])
     op("g", lambda: g.iota(N("ri", "p")[0], [[0, 1]], 0, 1), [], N("ri", "p")[1])
-    iota(N("rb", "t16"), [[0, K], [1, 16]], 0, 0)
-    ts(N("ri", "p16"), N("ri", "p"), 15, AluOpType.bitwise_and)
-    scan(N("rf", "i1024"), one(C), one(C), 1023.0, MUL, ADD)
-    vcopy(N("rf", "p16"), N("ri", "p16"))
-    for s in range(4):
-        ts(N("ri", "bit", s, s + 1), N("ri", "p"), s, AluOpType.logical_shift_right, 1, AluOpType.bitwise_and)
-    for r in (1, 2, 3):
-        act(N("rb", "ds%d" % r, 1, 16), one(15))
-        for k in (0, 1):
-            act(lane("fd_%d" % r, k), one(K), scale=float(k))
-            if r > 1:
-                act(N("rb", "PW_%d" % r, k * C, k * C + 1), one(1), scale=k - 208.0)
-    act(N("rb", "PE", 0, 1), one(1), scale=-208.0)
-
-    W = lambda s, a=0, e=C: N("rf", "W%d" % s, a, e)
-    m16 = N("rb", "mask", 0, 16)
-    vcopy(A("L0", 0, K), N("ri", "nx"))
-    send_list("L0", 0, K, "LN1", "aN0", MASKS[0])
+    iota(N("rb", "i16"), [[1, 16]], 0)
+    iota(N("rb", "i15"), [[1, 16]], -1)
     op("g", lambda: g.affine_select(T.et[:, 0:515], one(515)[0], [[1, 515]], EQ, 0.0, -3, -4), one(515)[1], [("et", 0, 515)])
     op("g", lambda: g.iota(N("ri", "pick")[0], [[16, 8]], 0, 0), [], N("ri", "pick")[1])
-    iota(N("rf", "j16"), [[16, K]], 0, 0)
-    ts(cx, N("rb", "t16"), N("rf", "p16"), NE, 2.0, MUL)
-    shared("W1", N("rf", "i1024"), "L0", 0, 0)
-    shared("W2", W(1), "L0", 0, 0)
-    scatter(N("rf", "w0"), A("L0", 0, K), N("rf", "i1024"))
+    iota(N("rf", "j16"), [[16, K]], 0)
+    iota(N("rb", "i2"), [[2, C]], -C)
+    ts(N("ri", "p16"), N("ri", "p"), 15, AluOpType.bitwise_and)
+    scan(N("rb", "own"), one(C), one(C), -209.0, MUL, ADD)
+    vcopy(p16, N("ri", "p16"))
+    bit_of_p(0)
+    bit_of_p(1)
+    ts(N("rb", "tab"), N("rb", "i16"), p16, NE)
+    ts(N("rf", "tabb"), N("rb", "i15"), p16, EQ, 65535.0, MUL)
+    ts(N("ru", "same"), one(K), p16, MUL)
+    bit_of_p(2)
+    tt(N("rf", "tabb"), N("rf", "tabb"), N("rb", "tab"), ADD)
+    bit_of_p(3)
+    ts(N("rf", "p15"), p16, 15.0, EQ, 1.0 - 2.0 ** -16, MUL)
     vcopy(N("rf", "bit"), N("ri", "bit"))
-    act(N("rb", "cp"), N("rb", "cx", 0, 16), scale=0.25)
-    act(m16, N("rb", "cx", 0, 16), scale=-0.5, bias=1.0)
-    act(N("rf", "nb"), N("rf", "bit", 0, 1), scale=-1024.0, bias=1024.0)
+    for s in (1, 2, 3):
+        act(N("rb", "ds%d" % s, 1, 16), one(15))
+    act(factor(0), one(K), scale=0.0)
+    act(lane("fl", 0), one(K), scale=-1.0)
+    act(lane("fl", 2), one(K), scale=0.0)
+    act(m16, N("rb", "tab"), scale=-1.0, bias=1.0)
+    act(N("rb", "cb"), ind(N("rf", "tabb"), N("ru", "same")))
+    act(pq, N("rf", "p15"), bias=2.0 ** -16)
+    constant(0)
+    constant(1)
+
+    W = lambda s, a=0, e=C: N("rb", "W%d" % s, a, e)
+    vcopy(A("L0", 0, K), N("ri", "nx"))
+    constant(2)
+    shared("W1", N("rb", "own"), "L0", 0, 192)
+    constant(3)
+    shared("W2", W(1), "L0", 0, 192)
+    ts(N("ru", "q1"), W(1, 0, 1), 208.0, ADD, N("rf", "bit", 0, 1), MUL)
+    act(N("rf", "nb"), N("rf", "bit", 0, 1), scale=208.0, bias=-208.0)
     for s in (1, 2, 3):
         act(N("rb", "mb%d" % s), m16, scale=N("rf", "bit", s, s + 1))
         act(N("rb", "ds%d" % s, 0, 1), N("rf", "bit", s, s + 1), scale=-1.0, bias=1.0)
     act(N("rf", "fo0"), W(1, 0, 1), scale=N("rf", "bit", 0, 1), bias=N("rf", "nb"))
-    act(io, N("rf", "i1024"), bias=-1232.0)
-    hold("w0", "w0s", 0, 288)
-    hold("W2", "S2")
-    scan(N("rf", "pw"), N("rb", "cp"), m16, 0.0, MUL, ADD)
-    hold("w0", "w0s", 288, C)
-    listed(N("ru", "G2"), "S2", -1024.0)
-    listed(A("L0", K, 2 * K), "w0s", -1024.0)
-    ts(N("ru", "q1"), W(1, 0, 1), -1024.0, ADD, N("rf", "bit", 0, 1), MUL)
-    send_list("L0", K, 2 * K, "LN1", "aN1", MASKS[0], K)
+    for p, q, step, o in SPREAD:
+        iota(N("rb", "name", p, q), [[-step, q - p]], -o - 1)
 
-    def power(s, k, cut=CUT):
+    def power(s, k, cut):
         shared("W%d" % s, W(s - k), "ru", RU["G%d" % k][0], cut)
 
-    def as_list(s, between):
-        hold("W%d" % s, "S%d" % s, 0, CUT)
-        hold("W%d" % s, "S%d" % s, CUT, C)
-        between()
-        listed(N("ru", "G%d" % s), "S%d" % s, -1024.0)
+    def as_list(s, step):
+        if step == 0:
+            held("W%d" % s, "S%d" % s)
+        else:
+            listed(N("ru", "G%d" % s), "S%d" % s)
 
-    def bit(s, part):
-        if part == 0:
+    def bit(s, step):
+        if step == 0:
             tt(N("rf", "og%d" % s), ind(W(2 ** s), N("ru", "q%d" % s)), N("rb", "mb%d" % s), MUL)
-        if part == 1:
+        if step == 1:
             scan(N("rf", "fo%d" % s), N("rb", "ds%d" % s), N("rf", "og%d" % s), N("rf", "fo%d" % (s - 1), 15, 16) if s > 1 else N("rf", "fo0"), MUL, ADD)
-        if part == 2:
-            ts(N("ru", "q%d" % (s + 1)) if s < 3 else N("ru", "OG0", 0, 1), N("rf", "fo%d" % s, 15, 16), -1024.0, ADD)
+        if step == 2:
+            ts(N("ru", "q%d" % (s + 1)) if s < 3 else N("ru", "OG0", 0, 1), N("rf", "fo%d" % s, 15, 16), 208.0, ADD)
 
-    def more(s, a, e, part, by=vcopy):
-        if part == 0:
-            by(N("rf", "or", a + s, e + s), ind(W(s), N("ru", "OG0", a // 16, e // 16)))
-        if part == 1:
-            hold("or", "os", a + s, e + s)
-        if part == 2:
-            listed(N("ru", "OG0", (a + s) // 16, (e + s) // 16), "os", -1024.0, a + s, e + s)
-
-    def constant(b):
-        op("v", lambda: g.vector.quantize_mx(T.qe[:, 128 * b:128 * b + 128], T.se[:, 128 * b:128 * b + 128], T.et[:, 3 - b:515 - b]), [("et", 0, 515)], [("qe", 128 * b, 128 * b + 128), ("se", 128 * b, 128 * b + 128)])
+    def more(s, a, e, step, by=vcopy):
+        if step == 0:
+            by(N("rb", "or", a + s, e + s), ind(W(s), N("ru", "OG0", a // 16, e // 16)))
+        if step == 1:
+            held("or", "os", a + s, e + s)
+        if step == 2:
+            listed(N("ru", "OG0", (a + s) // 16, (e + s) // 16), "os", a + s, e + s)
 
     def pick_u(scales):
         pk = N("ru", "pick")
@@ -356,240 +390,251 @@ def rank_program(g, core, T, topo):
         else:
             op("v", lambda: g.vector.tensor_copy(T.u2[:, 0:128].bitcast(dt.uint32), T.qu[:, 0:128].bitcast(dt.uint32).indirect(pk[0])), [("qu", 0, 128)] + pk[1], [("u2", 0, 128)])
 
-    def guests(r):
-        tt(N("rb", "g_%d" % r), ind(N("rb", "sg_%d" % r), A("LN%d" % r, 0, K)), N("rb", "sh_%d" % r), GT)
+    def up_signs(r, a, e):
+        for lo, hi, src in sign_row(r, a, e):
+            hold(N("rb", "du_%d" % r, lo, hi), src, hi - lo)
 
-    def leavers(r, a=0, e=C):
-        tt(N("rb", "l_%d" % r, a, e), ind(N("rb", "sg_%d" % r), A("LN%d" % r, K + a // 16, K + e // 16)), N("rb", "sh_%d" % r, a, e), LT)
+    def leavers(r, step, out=None, cut=192):
+        if step == 0:
+            shared("uh_%d" % r, N("rb", "sg_%d" % r), "LN%d" % r, 0, cut, 0.5, -1.5)
+        if step == 1:
+            ts(factor(2), ends("du_%d" % r), 0.0, GT)
+        if step == 2:
+            hold(factor("row"), N("rb", "uh_%d" % r), C, MIN)
+        if step == 3:
+            scan(N("rf", "fx"), factor(None), lanes("fe"), 0.0, MUL, ADD)
+        if step == 4:
+            vcopy(out, N("rf", "fx", 2, 3 * K, 3))
 
-    def slots(r, part):
-        if part == 0:
-            scan(N("rb", "ls_%d" % r), N("rb", "c4"), N("rb", "l_%d" % r), 0.0, MUL, ADD)
-        if part == 1:
-            ts(lane("fd_%d" % r, 2), ends("rb", "ls_%d" % r), N("rf", "pw2"), MUL, 0.5, GT)
-        if part == 2:
-            scan(N("rf", "fx_%d" % r), lanes("fd_%d" % r), lanes("fe_%d" % r), 0.0, MUL, ADD)
-        if part == 3:
-            o = RF["fx_%d" % r][0]
-            vcopy(N("ru", "x_%d" % r), A("rf", o + 2, o + 3 * K, 3))
+    def places(a, e):
+        scatter(N("rb", "P1"), N("ru", "OG0", a // 16, e // 16), N("rb", "i2", a, e))
 
-    power(4, 2)
+    def plain():
+        for p, q, step, o in SPREAD:
+            iota(N("rf", "plain", o, o + step * (q - p)), [[1, q - p], [0, step]], p)
+
+    as_list(2, 0)
     bit(1, 0)
-    vcopy(N("ru", "pick"), N("ri", "pick"))
+    as_list(2, 1)
+    power(4, 2, 0)
+    power(6, 2, 0)
+    scatter(N("rb", "w0"), A("L0", 0, K), N("rb", "own"))
     bit(1, 1)
-    power(6, 2)
+    held("w0", "w0s")
     bit(1, 2)
-    quant("qu", "su", "uin", 0, 128, 0)
+    listed(A("L0", K, 2 * K), "w0s")
+    send_hosts("L0", K, 1)
+    power(8, 2, 128)
+    act(npq, pq, scale=-1.0)
+    act(N("rf", "nq"), N("rf", "p15"), scale=65536.0, bias=-65536.0)
+    act(N("rf", "npq2"), pq, scale=npq)
+    act(lane("fe", 2), N("rf", "j16"), bias=p16)
+    act(lane("fl", 1), one(K), scale=N("rf", "nq"))
     bit(2, 0)
-    power(8, 2)
+    as_list(8, 0)
     bit(2, 1)
-    as_list(8, lambda: bit(2, 2))
-    pick_u(1)
-    act(N("rb", "c4"), cx, scale=2.0)
-    bit(3, 0)
+    as_list(8, 1)
     power(16, 8, 0)
+    vcopy(N("ru", "pick"), N("ri", "pick"))
+    bit(2, 2)
     quant("xq0", "xs0", "xt0", 0, C, 0)
-    send_state(1, MASKS[0])
+    send_state(1, 0, 0, C)
+    iota(N("rb", "free"), [[0, 3 * S]], 1)
+    iota(N("rb", "ones"), [[0, S]], 1)
+    plain()
+    unpack("psB", "xq0", "xs0")
+    bit(3, 0)
+    quant("qu", "su", "uin", 0, 128, 0)
     bit(3, 1)
-    pick_u(0)
+    power(24, 8, 128)
     bit(3, 2)
-    power(24, 8)
-    more(16, 0, 16, 0)
+    pick_u(0)
+    more(16, 0, 16, 0, act)
+    power(32, 8, 192)
     more(16, 0, 16, 1)
-    power(32, 8)
+    as_list(32, 0)
     more(16, 0, 16, 2)
-    signs(1, 0)
-    as_list(32, lambda: more(32, 0, 32, 0))
+    as_list(32, 1)
+    more(32, 0, 32, 0, vcopy)
+    pick_u(1)
+    power(64, 32, 160)
     more(32, 0, 32, 1)
-    signs(1, 1)
-    power(64, 32, 0)
-    constant(0)
+    places(0, 32)
     more(32, 0, 32, 2)
-    leavers(1)
-    power(96, 32, 0)
-    more(64, 0, 64, 0, act)
-    guests(1)
-    power(128, 32, 0)
-    more(96, 32, 64, 0)
-    act(N("rf", "pw2"), pw, func=SQUARE)
-    act(N("rf", "npw"), pw, scale=-1.0)
-    act(lane("fe_1", 2), N("rf", "j16"), bias=N("rf", "p16"))
-    act(lane("fe_1", 1), lane("fe_1", 2), scale=-1.0)
-    ts(lane("fe_1", 0), A("LN1", K, 2 * K), float(C), ADD)
+    signs(1, 1)
+    power(96, 32, 192)
+    signs(1, 0)
+    vcopy(N("rf", "h"), A("LN1", 0, K))
+    more(64, 0, 64, 0, vcopy)
+    more(96, 32, 64, 0, act)
+    power(128, 32, 96)
     more(64, 0, 96, 1)
-    constant(1)
+    up_signs(1, 0, C)
     more(64, 0, 96, 2)
-    slots(1, 0)
-    so1, go1 = lambda a, e: N("rb", "so_1", a, e), lambda a, e: N("rb", "go_1", a, e)
-
-    def weights(a, e, by=act):
-        by(go1(a, e), ind(N("rb", "g_1"), N("ru", "OG0", a // 16, e // 16)))
-        act(so1(a, e), ind(N("rb", "l_1"), N("ru", "OG0", a // 16, e // 16)), scale=-1.0, bias=1.0)
-
-    def before(a, e):
-        scan(N("rb", "PE", a + 1, e + 1), so1(a, e), go1(a, e), N("rb", "PE", a, a + 1) if a else -208.0, ADD, ADD)
-
-    more(128, 32, 160, 0)
-    weights(0, 160)
-    slots(1, 1)
+    places(32, 64)
+    more(128, 32, 160, 0, vcopy)
+    leavers(1, 1)
+    leavers(1, 0, cut=0)
+    tt(N("rf", "d"), N("rf", "h"), lane("fe", 2), SUB)
     more(128, 32, 160, 1)
-    constant(2)
+    places(64, 160)
+    halves("psB", "th", (0,))
+    act(lane("fe", 0), N("rf", "d"), scale=npq)
     more(128, 32, 160, 2)
-    slots(1, 2)
-    more(128, 160, 288, 0)
-    weights(160, 288)
-    constant(3)
+    leavers(1, 2)
+    act(lane("fe", 1), N("rf", "d"), scale=-1.0)
+    more(128, 160, 288, 0, act)
+    places(160, 288)
     more(128, 160, 288, 1)
-    slots(1, 3)
+    halves("psB", "th", (1, 2))
+    leavers(1, 3)
     more(128, 160, 288, 2)
-    before(0, 288)
-    weights(288, C, vcopy)
-    before(288, C - 1)
-    count_zero(N("rf", "i0_1"), N("rb", "am_1", 0, 208), N("rb", "PE", 1, 209))
-    act(N("rf", "or", 0, 16), ind(N("rf", "i1024"), N("ru", "OG0", 0, 1)))
-    unpack("psA", "xq0", "xs0")
-    halves("psA", "th1")
-    scatter(N("rb", "PW_1", 0, C), N("ru", "OG0"), N("rb", "PE"))
-    ts(N("rb", "PW_1", C, 2 * C), N("rb", "PW_1", 0, C), 1.0, ADD)
+    leavers(1, 4, N("ru", "y"))
+    places(288, C)
+    shared("PY", N("rb", "P1"), "ru", RU["y"][0], 192)
+    scan(N("rf", "fy"), factor(None), lanes("fl"), 0.0, MUL, ADD)
+    halves("psB", "th", (3,))
+    held("PY", "PYs")
+    tt(N("rf", "xl"), ends("PYs"), N("rf", "fy", 2, 3 * K, 3), ADD)
+    ts(N("ru", "x_1"), N("rf", "xl"), pq, MUL, C + 0.25, ADD)
 
     for r in (1, 2, 3):
-        m = MASKS[r - 1]
-        L, LA, LB = "L%d" % r, "LA%d" % r, "LB%d" % r
+        LA, LB = "LA%d" % r, "LB%d" % r
         nb = lambda k, a=0, b=C: N("rb", "%s_%d" % (k, r), a, b)
-        nu = lambda k, a=0, b=C: N("ru", "%s_%d" % (k, r), a // 16, b // 16)
-        th, tp, zt, xt = ["%s%d" % (k, r) for k in ("th", "tp", "zt", "xt")]
-        zq, zs, xq, xs = ["%s%d" % (k, r) for k in ("zq", "zs", "xq", "xs")]
-        PR, Ps = "PR_%d" % r, "Ps_%d" % r
+        zt, xt, zq, zs, xq, xs, lq, lp = ["%s%d" % (k, r) for k in ("zt", "xt", "zq", "zs", "xq", "xs", "lq", "lp")]
+        xat = RU["x_%d" % r][0]
+        slot = lambda a, e, step=1: N("rb", "free", S * (r - 1) + a, S * (r - 1) + e, step)
+        down = lambda hi, lo, step=1: back("free", S * (r - 1) + hi, S * (r - 1) + lo, step)
         if r > 1:
-            og = lambda a, e: N("ru", "og_%d" % (r - 1), a // 16, e // 16)
-            leavers(r, *HALF[0])
-            leavers(r, *HALF[1])
-            act(lane("fe_%d" % r, 0), ends("rf", "hs_%d" % (r - 1)), scale=pw, bias=C - 1024.0)
-            halves("psA", th, (0,))
-            act(nb("so"), ind(nb("l"), og(0, C)), scale=-1.0, bias=1.0)
-            guests(r)
-            for a, e in PAIR:
-                act(nb("go", a, e), ind(nb("g"), og(a, e)))
-            for part in range(3):
-                slots(r, part)
-            for a, e in PAIR:
-                e = min(e, C - 1)
-                for k in (0, 1):
-                    scan(nb("PW", k * C + a + 1, k * C + e + 1), nb("so", a, e), nb("go", a, e), nb("PW", k * C + a, k * C + a + 1) if a else k - 208.0, ADD, ADD)
-                if not a:
-                    count_zero(N("rf", "i0_%d" % r), nb("am", 0, 208), nb("PW", 1, 209))
-                    slots(r, 3)
-        shared(PR, nb("PW", 0, 2 * C), "ru", RU["x_%d" % r][0], bias=1232.0)
-        vcopy(N("ru", "i0_%d" % r), N("rf", "i0_%d" % r))
-        if r == 1:
-            act(nb("OB", 16 + C, 32 + C), ind(N("rf", "or"), N("ru", "i0_1")), bias=-1232.0)
+            leavers(r, 0)
+            act(lane("fe", 0), N("rf", "d"), scale=N("rf", "npq2"), bias=npq)
+            act(lane("fe", 1), N("rf", "d"), scale=npq, bias=-1.0)
+            up_signs(r, SPREAD[2][0], C)
+            leavers(r, 2)
+            leavers(r, 1)
+            halves("psB", "th", range(r + 1))
+            for step in (3, 4):
+                leavers(r, step, N("ru", "x_%d" % r))
+            unpack("psA", lq, lp, 0, EARLY)
+            halves("psA", "tp", range(4), 0, EARLY)
         else:
-            act(nb("OB", 16 + C, 32 + C), ind(N("rb", "OB_%d" % (r - 1), 16, 16 + C), N("ru", "i0_%d" % r)))
-        hold(PR, Ps, 0, CUT)
-        hold(PR, Ps, CUT, C)
-        if r == 1:
-            act(N("rb", "mask", 16, C), N("rb", "cx", 16, C), scale=-0.5, bias=1.0)
-            unpack("psB", "lq1", "lp1")
-            halves("psB", tp, (0, 1))
-        else:
-            halves("psA", th, (1, 2, 3))
+            unpack("psA", lq, lp)
+            halves("psA", "tp")
+        scatter(slot(0, S), N("ru", "x_%d" % r), N("rb", "name"))
+        FW, BW = "FW_%d" % r, "BW_%d" % r
+        scan(nb("FW", FW0 - C - 1, FW0 + 1), slot(C - 2, S), slot(C - 2, S), -1.0, MUL, MIN)
+        scan(back(BW, S + C // 2 - 1, S - 1), down(C, 0, 2), down(C, 0, 2), -1.0, MUL, MIN)
+        scan(nb("FW", FW0 + 1, FW0 + S), slot(0, S - 1), slot(0, S - 1), nb("FW", FW0, FW0 + 1), MUL, MIN)
+        scan(back(BW, S - 2, 0), down(S - 1, 1), down(S - 1, 1), nb("BW", S - 1, S), MUL, MIN)
         if r < 3:
-            act(lane("fe_%d" % (r + 1), 2), ends("rf", Ps), scale=pw, bias=-1024.0)
-            act(lane("fe_%d" % (r + 1), 1), ends("rf", Ps), scale=N("rf", "npw"), bias=1024.0)
-        listed(nu("sc"), Ps, -1024.0)
-        listed(nu("ai"), Ps, -1023.0)
-        scatter(nb("OB", 16, 16 + C), nu("sc"), io)
-        listed(nu("bi"), Ps, -1009.0)
-        act(nb("OB", 15, 16), nb("OB", 15 + C, 16 + C))
-        for a, e in HALF:
-            tt(nb("am", a, e), ind(nb("OB", 16, 17 + C), nu("ai", a, e)), N("rb", "mask", 0, e - a), MUL)
-        act(N("rf", "bf_%d" % r), ind(nb("OB", 0, 16 + C), nu("bi")), bias=1232.0)
-        for a, e in HALF:
-            scan(nb("as", a, e), N("rb", "cx", 0, e - a), nb("am", a, e), 0.0, MUL, ADD)
-        hold("bf_%d" % r, "bs_%d" % r, 0, 96)
-        ts(A(L, 0, K), ends("rb", "as_%d" % r), pw, MUL, 208.0, ADD)
-        send_list(L, 0, K, LA, "aA%d" % r, m)
-        hold("bf_%d" % r, "bs_%d" % r, 96, C)
-        listed(A(L, K, 2 * K), "bs_%d" % r, -1024.0)
-        send_list(L, K, 2 * K, LB, "aB%d" % r, m)
-        if r < 3:
-            send_list(L, 0, 2 * K, "LN%d" % (r + 1), "aN%d" % (r + 1), MASKS[r])
-        if r > 1:
-            unpack("psB", "lq%d" % r, "lp%d" % r)
-        halves("psB", tp, (2, 3) if r == 1 else range(4))
+            act(nb("full", 0, S), slot(0, S), scale=-1.0, func=SIGN)
+        act(nb("br"), ind(nb("FW", FW0, FW0 + S), N("ru", "x_%d" % r)))
 
-        def predecessors(by, b, a, e):
-            by(plane("tb", b, a, e), ind(plane(th, b), A(L, K + a // 16, K + e // 16)))
+        def named(k, out, step):
+            if step == 0:
+                hold(nb(k + "s"), nb(k + "r"), C, MIN)
+            else:
+                ts(A(out, 0, K), ends("%ss_%d" % (k, r)), npq, MUL, -1.0, ADD)
+
+        vcopy(nb("ar", 0, 192), ind(nb("BW", 0, S), part("ru", 0, 192, xat)))
+        act(nb("ar", 256, C), ind(nb("BW", 0, S), part("ru", 256, C, xat)))
+        named("b", LB, 0)
+        vcopy(nb("ar", 192, 256), ind(nb("BW", 0, S), part("ru", 192, 256, xat)))
+        named("b", LB, 1)
+        send_ring("B", r)
+        named("a", LA, 0)
+        named("a", LA, 1)
+        send_ring("A", r)
+        if r < 3:
+            send_hosts(LB, 0, r + 1)
+
+        PR, Ps, hf, hs = ["%s_%d" % (k, r) for k in ("PR", "Ps", "hf", "hs")]
+        if r == 2:
+            halves("psB", "th", (3,))
+        if r > 1:
+            unpack("psB", lq, lp, EARLY, C)
+            halves("psB", "tp", range(4), EARLY, C)
+
+        def predecessors(by, b, a=0, e=C):
+            by(plane("tb", b, a, e), ind(wide("th", b), part(LB, a, e)))
 
         for b in range(4):
             who = [TB[r][i][b] for i in (0, 1)]
-            for w, (a, e) in ([(who[0], (0, C))] if who[0] == who[1] else zip(who, HALF)):
-                if w != "l":
+            for w, (a, e) in ([(who[0], (0, C))] if who[0] == who[1] else zip(who, XRUN)):
+                if w in "vs":
                     predecessors(vcopy if w == "v" else act, b, a, e)
-        if r == 1:
-            quant("qv", "sv", "vin", 0, 128, 0)
+            if r < 3 and b == 0:
+                scan(nb("CN", 0, S), nb("full", 0, S), N("rb", "ones"), -2.0 - C, ADD, ADD)
+        pieces = spread("rb", RB[PR][0], 0, C) if r < 3 else []
+        for lo, hi, out in pieces:
+            vcopy(out, ind(nb("CN", 0, S), part("ru", lo, hi, xat)))
+
+        def behind(w):
+            for i in (0, 1):
+                for b in range(4):
+                    if TB[r][i][b] == w:
+                        predecessors(act, b, *XRUN[i])
 
         def pack_z(i):
-            a, e = HALF[i]
+            a, e = ZRUN[i]
             quant(zq, zs, zt, a, e)
             for b in range(4):
-                mm(P("psB" if i else "psA", b, e - a), "wq", "wp", 128 * b, zq, zs, a, e)
+                mm(P("psB" if i else "psA", b, 0, e - a), "wq", "wp", 128 * b, zq, zs, a, e)
 
-        for i, (a, e) in enumerate(HALF):
+        def layer(i, b):
+            a, e = ZRUN[i]
+            for lo, hi, out in spread("hh", WIDE * b, a, e):
+                act(out, P("psB" if i else "psA", b, lo - a, hi - a), scale=0.015625)
+
+        for i, (a, e) in enumerate(ZRUN):
             for b in range(4):
-                act(plane("za", b, a, e), ind(plane(tp, b), A(LA, a // 16, e // 16)))
-                tt(strip(zt, b, a, e), ind(plane(tp, b), A(LB, a // 16, e // 16)), plane("za", b, a, e), ADD)
-                if (i, b) == (1, 0):
-                    pack_z(0)
-        if r < 3:
-            act(N("rf", "of_%d" % r), nb("OB", 16, 16 + C), bias=1232.0)
+                act(plane("za", b, a, e), ind(wide("tp", b), part("RB%d" % r, a, e)))
+                tt(strip(zt, b, a, e), ind(wide("tp", b), part("RA%d" % r, a, e)), plane("za", b, a, e), ADD)
+                if i and not b:
+                    pack_z(i - 1)
+        behind("m")
+        layer(0, 0)
         pack_z(1)
+        for lo, hi, out in pieces:
+            hold(N("rb", Ps, lo, hi), out, hi - lo)
+        if r == 3:
+            quant("qv", "sv", "vin", 0, 128, 0)
+        for i, b in ((1, 0), (0, 1), (1, 1), (0, 2), (1, 2), (0, 3), (1, 3)):
+            layer(i, b)
+        behind("l")
         if r < 3:
-            hold("of_%d" % r, "os_%d" % r, 0, 256)
-        for b in range(4):
-            for i, (a, e) in enumerate(HALF):
-                if (b, i) == (0, 1):
-                    ts(plane("hh", b, a, e), P("psB", b, e - a), 0.015625, MUL)
-                else:
-                    act(plane("hh", b, a, e), P("psB" if i else "psA", b, e - a), scale=0.015625)
-            if TB[r][0][b] == "l":
-                predecessors(act, b, *HALF[0])
-        if r < 3:
-            hold("of_%d" % r, "os_%d" % r, 256, C)
-        for b in range(4):
-            if TB[r][1][b] == "l":
-                predecessors(act, b, *HALF[1])
-        if r < 3:
-            act(N("rf", "hf_%d" % r), ind(N("rf", PR), A("LN%d" % (r + 1), K, 2 * K)))
+            act(N("rb", hf), ind(N("rb", PR), A("LN%d" % (r + 1), 0, K)))
+            act(lane("fe", 2), ends(Ps), scale=pq, bias=C + 0.25)
         else:
-            act(N("rf", "nr"), ind(nb("OB", 16, 17 + C), nu("ai")), bias=208.0)
+            act(N("rf", "nr"), ind(N("rf", "plain", 0, WIDE), A(LA, 0, K)))
             dma("y", "dout", T.nr[:, :], T.rf[0:128:16, RF["nr"][0]:RF["nr"][0] + C], N("rf", "nr")[1], [])
 
         def pack_x(i):
-            a, e = HALF[i]
+            a, e = XRUN[i]
             quant(xq, xs, xt, a, e)
             if r < 3:
+                for k, (lo, hi) in enumerate([(a, e)] if i else [(a, EARLY), (EARLY, e)]):
+                    send_state(r + 1, 2 * i + k, lo, hi)
                 signs(r + 1, i)
             else:
-                mm(P("psA", i, e - a), "qv", "sv", 0, xq, xs, a, e)
+                mm(P("psA", i, 0, e - a), "qv", "sv", 0, xq, xs, a, e)
                 dma("y", "dout", T.oc[:, 4 * a:4 * e], T[xq][:, a:e].bitcast(dt.uint8), [(xq, a, e)], [])
                 for k in range(4 * i):
                     dma("s" if k > 1 else "y", "dout", T.osc[4 * k:4 * k + 4, 0:C], T[xs][32 * k:32 * k + 4, 0:C], [(xs, 0, C)], [])
-                (vcopy if i else act)(A("yo", a, e), P("psA", i, e - a))
+                (vcopy if i else act)(A("yo", a, e), P("psA", i, 0, e - a))
                 dma("s", "dout", T.y[:, a:e], T.yo[:, a:e], [("yo", a, e)], [])
 
-        for i, (a, e) in enumerate(HALF):
+        for i, (a, e) in enumerate(XRUN):
             for b in range(4):
-                tt(strip(xt, b, a, e), ind(plane("hh", b), A(L, a // 16, e // 16)), plane("tb", b, a, e), ADD)
+                tt(strip(xt, b, a, e), ind(wide("hh", b), part(LA, a, e)), plane("tb", b, a, e), ADD)
                 if (i, b) == (1, 0):
                     pack_x(0)
-        if r < 3:
-            listed(nu("og"), "os_%d" % r, -1024.0)
         pack_x(1)
         if r < 3:
-            send_state(r + 1, MASKS[r])
-            unpack("psA", xq, xs)
-            hold("hf_%d" % r, "hs_%d" % r)
+            unpack("psB", xq, xs)
+            held(hf, hs)
+            up_signs(r + 1, 0, SPREAD[2][0])
+            tt(N("rf", "d"), ends(hs), ends(Ps), SUB)
 
     for sem in sorted(total, key=lambda k: (k == "dout", k in ("cv", "cs", "ct"), k)):
         g.wait_ge(T.sem[sem], total[sem])

from concourse.mybir import dt, AluOpType, ActivationFunctionType

ADD, SUB, MUL, MIN = AluOpType.add, AluOpType.subtract, AluOpType.mult, AluOpType.min
GT, EQ, NE = AluOpType.is_gt, AluOpType.is_equal, AluOpType.not_equal
COPY, IDENT, SIGN = ActivationFunctionType.Copy, ActivationFunctionType.Identity, ActivationFunctionType.Sign
C = 416
K = C // 16
S = 2 * C
MASKS = [1, 2, 3]
ZRUN = [(0, 288), (288, 416)]
XRUN = [(0, 256), (256, 416)]
TB = {1: ("vsss", "vsmm"), 2: ("vsmm", "vlll"), 3: ("vvvs", "vvmm")}
TINY = 2.0 ** -93
SPREAD = [(0, 32, 4, 515), (32, 160, 2, 257), (160, 416, 1, 0)]
EARLY = 160
WIDE = 640
FW0 = 432


def layout(items):
    at, n = {}, 0
    for name, w in items:
        at[name] = (n, w)
        n += (w + 15) // 16 * 16
    return at, n


POWERS = (1, 2, 4, 6, 8, 16, 24, 32, 64, 96, 128)
_rb = [(k, C) for k in ("cb", "name")] + [(k, 16) for k in ("m16", "tab", "i16", "i15")] + [("ones", S), ("free", 3 * S), ("fd", 3 * C + 16)]
_rb += [("%s%d" % (k, s), 16) for s in (1, 2, 3) for k in ("mb", "ds")]
_rb += [("%s_%d" % (k, r), C) for r in (1, 2, 3) for k in ("uh", "du", "ar", "br", "as", "bs")]
_rb += [("sg_%d" % r, WIDE) for r in (1, 2, 3)] + [("FW_%d" % r, FW0 + S) for r in (1, 2, 3)] + [("BW_%d" % r, S + 224) for r in (1, 2, 3)]
_rb += [("%s_%d" % (k, r), S) for r in (1, 2) for k in ("full", "CN")]
_rb += [(k, C) for k in ("own", "i2", "w0", "w0s", "or", "os", "S2", "S8", "S32", "P1", "PY", "PYs")] + [("W%d" % s, C) for s in POWERS]
_rb += [("%s_%d" % (k, r), C) for r in (1, 2) for k in ("Ps", "hf", "hs")] + [("PR_%d" % r, WIDE) for r in (1, 2)]
RB, NRB = layout(_rb)
_ru = [("G%d" % s, K) for s in (2, 8, 32)] + [("OG0", K), ("pick", 8), ("same", K), ("y", K)] + [("q%d" % s, 1) for s in (1, 2, 3)]
_ru += [("x_%d" % r, K) for r in (1, 2, 3)]
RU, NRU = layout(_ru)
_rf = [("nr", C), ("plain", WIDE + 16), ("tabb", 16), ("bit", 4)] + [(k, 1) for k in ("p16", "p15", "pq", "npq", "npq2", "nq", "nb", "fo0")]
_rf += [(k, K) for k in ("j16", "h", "d", "xl")]
_rf += [("%s%d" % (k, s), 16) for s in (1, 2, 3) for k in ("fo", "og")]
_rf += [(k, 3 * K) for k in ("fe", "fx", "fl", "fy")]
RF, NRF = layout(_rf)
RI, NRI = layout([("nx", K), ("p", 1), ("p16", 1), ("bit", 4), ("pick", 8)])
WHERE = {"rb": RB, "ru": RU, "rf": RF, "ri": RI}

X4, U8, BF = "float8_e4m3fn_x4", "uint8", "bfloat16"
SCRATCH = {
    "rb": ("sbuf", [128, NRB], BF), "ru": ("sbuf", [128, NRU], "uint16"), "rf": ("sbuf", [128, NRF], "float32"), "ri": ("sbuf", [128, NRI], "int32"),
    "one": ("sbuf", [128, 528], BF), "et": ("sbuf", [128, 528], BF), "qe": ("sbuf", [128, 512], X4), "se": ("sbuf", [128, 512], U8),
    "uin": ("sbuf", [128, 512], BF), "qu": ("sbuf", [128, 128], X4), "su": ("sbuf", [128, 128], U8),
    "u2": ("sbuf", [128, 128], X4), "s2": ("sbuf", [128, 128], U8),
    "vin": ("sbuf", [128, 512], BF), "qv": ("sbuf", [128, 128], X4), "sv": ("sbuf", [128, 128], U8),
    "wq": ("sbuf", [128, 512], X4), "wp": ("sbuf", [128, 512], U8),
    "yo": ("sbuf", [128, C], "float32"),
    "psA": ("psum", [128, 2048], "float32"), "psB": ("psum", [128, 2048], "float32"),
    "L0": ("sbuf", [128, 2 * K], "uint16"),
    "xt0": ("sbuf", [128, 4 * C], BF), "xq0": ("sbuf", [128, C], X4), "xs0": ("sbuf", [128, C], U8),
    "th": ("sbuf", [128, 4 * WIDE], BF), "hh": ("sbuf", [128, 4 * WIDE], BF), "tb": ("sbuf", [128, 4 * C], BF),
    "tp": ("sbuf", [128, 4 * WIDE], BF), "za": ("sbuf", [128, 4 * C], BF),
}
for _r in (1, 2, 3):
    for _n in ("zt", "xt"):
        SCRATCH["%s%d" % (_n, _r)] = ("sbuf", [128, 4 * C], BF)
    for _n in ("xq", "lq", "zq"):
        SCRATCH["%s%d" % (_n, _r)] = ("sbuf", [128, C], X4)
    for _n in ("xs", "lp", "zs"):
        SCRATCH["%s%d" % (_n, _r)] = ("sbuf", [128, C], U8)
    for _n in ("LA", "LB", "LN", "RA", "RB"):
        SCRATCH["%s%d" % (_n, _r)] = ("sbuf", [128, K], "uint16")
SEMAPHORES = ["cv", "cs", "ct", "cg", "dnx", "dx", "du", "dv", "dwc", "dws", "dout", "lsem"] + ["a%s%d" % (k, r) for r in (1, 2, 3) for k in "NAB"]
SEMAPHORES += ["aQ%d_%d" % (r, i) for r in (1, 2, 3) for i in (0, 1, 2)]


def rank_program(g, core, T, topo):
    rank = T.rank_of(core)
    if rank is None:
        return
    eng = {"v": g.vector, "s": g.scalar, "t": g.tensor, "g": g, "y": g.sync}
    known = {q: {} for q in eng}
    count = {q: 0 for q in eng}
    long = {q: False for q in eng}
    clocks, wr, rd, total = {}, {}, {}, {}

    def over(a, b):
        return a[1] < b[2] and b[1] < a[2]

    def learn(q, sem, n):
        for k, v in list(clocks.get((sem, n), {}).items()) + [(sem, n)]:
            if known[q].get(k, 0) < v:
                known[q][k] = v

    def sync(q, reads, writes):
        need = {}
        for r in reads:
            for reg, ev in wr.get(r[0], []):
                if over(reg, r):
                    need[ev] = 1
            if r[0][:2] == "ps":
                for reg, ev in rd.get(r[0], []):
                    if over(reg, r) and ev[0] != "c" + q:
                        need[ev] = 1
        for w in writes:
            for reg, ev in wr.get(w[0], []) + rd.get(w[0], []):
                if over(reg, w):
                    need[ev] = 1
        for sem, n in sorted(need, key=lambda e: -len(clocks.get(e, {})) * 100000 - e[1]):
            if known[q].get(sem, 0) < n:
                if sem == "c" + q and long[q]:
                    n = max(n, count[q] - 1)
                eng[q].wait_ge(T.sem[sem], n)
                learn(q, sem, n)

    def mark(ev, q, reads, writes):
        clocks[ev] = dict(known[q]) if q else {}
        for w in writes:
            wr[w[0]] = [e for e in wr.get(w[0], []) if not (w[1] <= e[0][1] and e[0][2] <= w[2])] + [(w, ev)]
            rd[w[0]] = [e for e in rd.get(w[0], []) if not (w[1] <= e[0][1] and e[0][2] <= w[2])]
        for r in reads:
            rd.setdefault(r[0], []).append((r, ev))

    def op(q, f, reads, writes):
        sync(q, reads, writes)
        count[q] += 1
        long[q] = any(w[2] - w[1] >= 96 for w in writes) and not any(w[0] == "ru" or w[0][0] == "L" for w in writes)
        sem = "c" + q
        f().then_inc(T.sem[sem], 1)
        total[sem] = count[q]
        mark((sem, count[q]), q, reads, writes)

    def dma(q, sem, out, in_, reads, writes):
        sync(q, reads, writes)
        eng[q].dma_start(out, in_).then_inc(T.sem[sem], 16)
        total[sem] = total.get(sem, 0) + 16
        mark((sem, total[sem]), q, reads, writes)

    def A(buf, a, b, step=1):
        return (T[buf][:, a:b] if step == 1 else T[buf][:, a:b:step], [(buf, a, b)])

    def N(buf, name, a=0, b=None, step=1):
        o, w = WHERE[buf][name]
        return A(buf, o + a, o + (w if b is None else b), step)

    def back(name, hi, lo, step=1):
        o = RB[name][0]
        return (T.rb[:, o + hi:o + lo - 1:-step], [("rb", o + lo, o + hi + 1)])

    def ends(name, a=0, e=C):
        o = RB[name][0]
        return A("rb", o + a + 15, o + e, 16)

    def lane(name, k):
        o = RF[name][0]
        return (T.rf[:, o + k:o + 3 * K:3], [("%s#%d" % (name, k), 0, K)])

    def lanes(name):
        return (N("rf", name)[0], [r for k in range(3) for r in lane(name, k)[1]])

    def factor(k):
        o = RB["fd"][0]
        if k == "row":
            return (T.rb[:, o:o + 3 * C:3], [("fd#1", 0, C)])
        if k is None:
            return (T.rb[:, o + 29:o + 3 * C + 16:16], [("fd#%d" % i, 0, C) for i in range(3)])
        return (T.rb[:, o + 29 + 16 * k:o + 3 * C + 16:48], [("fd#%d" % k, 0, C)])

    def spread(buf, at, a, e):
        out = []
        for p, q, step, o in SPREAD:
            lo, hi = max(a, p), min(e, q)
            if lo < hi:
                out.append((lo, hi, A(buf, at + o + step * (lo - p), at + o + step * (hi - 1 - p) + 1, step)))
        return out

    def ind(w, o):
        return (w[0].indirect(o[0]), w[1] + o[1])

    def P(buf, bank, a, e):
        return (T[buf][:, 512 * bank + a:512 * bank + e], [(buf, 512 * bank, 512 * bank + 512)])

    def plane(buf, b, a=0, e=C):
        return A(buf, C * b + a, C * b + e)

    def wide(buf, b):
        return A(buf, WIDE * b, WIDE * b + WIDE)

    def part(buf, a, e, at=0):
        return A(buf, at + a // 16, at + e // 16)

    def strip(buf, b, a, e):
        return (T[buf][:, 4 * a + b:4 * e:4], [("%s#%d" % (buf, b), a, e)])

    def split(regs, *numbers):
        for s in numbers:
            if isinstance(s, tuple):
                regs += s[1]
        return [s[0] if isinstance(s, tuple) else s for s in numbers]

    def tt(out, a, b, o):
        op("v", lambda: g.vector.tensor_tensor(out[0], a[0], b[0], o), a[1] + b[1], out[1])

    def ts(out, a, s1, o1, s2=None, o2=None):
        regs = list(a[1])
        s1, s2 = split(regs, s1, s2)
        if o2 is None:
            op("v", lambda: g.vector.tensor_scalar(out[0], a[0], s1, None, o1), regs, out[1])
        else:
            op("v", lambda: g.vector.tensor_scalar(out[0], a[0], s1, s2, o1, o2), regs, out[1])

    def vcopy(out, a):
        op("v", lambda: g.vector.tensor_copy(out[0], a[0]), a[1], out[1])

    def scatter(win, o, a):
        op("v", lambda: g.vector.tensor_copy(win[0].indirect(o[0]), a[0]), a[1] + o[1], win[1])

    def act(out, a, scale=1.0, bias=0.0, func=IDENT):
        regs = list(a[1])
        if (scale, bias, func) == (1.0, 0.0, IDENT):
            return op("s", lambda: g.scalar.activation(out[0], a[0], COPY), regs, out[1])
        scale, bias = split(regs, scale, bias)
        op("s", lambda: g.scalar.activation(out[0], a[0], func, bias=bias, scale=scale), regs, out[1])

    def scan(out, a, b, init, o1, o2):
        regs = a[1] + b[1]
        init = split(regs, init)[0]
        op("v", lambda: g.vector.tensor_tensor_scan(out[0], a[0], b[0], init, o1, o2), regs, out[1])

    def iota(out, pattern, base, cm=0):
        op("g", lambda: g.iota(out[0], pattern, base, cm, allow_small_or_imprecise_dtypes=True), [], out[1])

    def quant(q, s, tile, a, e, t0=None):
        regs = [("%s#%d" % (tile, b), a, e) for b in range(4)] if t0 is None else [(tile, t0, t0 + 4 * (e - a))]
        i0 = 4 * a if t0 is None else t0
        op("v", lambda: g.vector.quantize_mx(T[q][:, a:e], T[s][:, a:e], T[tile][:, i0:i0 + 4 * (e - a)]), regs, [(q, a, e), (s, a, e)])

    def mm(out, lq, ls, la, rq, rs, a, e):
        op("t", lambda: g.tensor.matmul_mx(out[0], T[lq][:, la:la + 128], T[ls][:, la:la + 128], T[rq][:, a:e], T[rs][:, a:e], True, True),
           [(lq, la, la + 128), (ls, la, la + 128), (rq, a, e), (rs, a, e)], out[1])

    def send(m, sem, pairs, reads, lands):
        dst = T.cores[rank ^ m]
        rid, pid = topo.addr(dst)[:2]
        sync("g", reads, [])
        for out, in_ in pairs:
            g.remote_dma(out, in_, T.sem[sem], T.sem.lsem, pid, rid, topo.mask(core, dst))
            total["lsem"] = total.get("lsem", 0) + len(topo.engines(core, dst))
        total[sem] = len(pairs) * len(topo.engines(dst, core))
        mark((sem, total[sem]), None, [], lands)

    def send_hosts(src, at, r):
        send(MASKS[r - 1], "aN%d" % r, [(T["LN%d" % r][:, 0:K], T[src][:, at:at + K])], [(src, at, at + K)], [("LN%d" % r, 0, K)])

    def send_ring(k, r):
        src, dst = "L%s%d" % (k, r), "R%s%d" % (k, r)
        send(MASKS[r - 1], "a%s%d" % (k, r), [(T[dst][:, 0:K], T[src][:, 0:K])], [(src, 0, K)], [(dst, 0, K)])

    def send_state(r, i, a, e):
        xq, xs, lq, lp = "xq%d" % (r - 1), "xs%d" % (r - 1), "lq%d" % r, "lp%d" % r
        send(MASKS[r - 1], "aQ%d_%d" % (r, i), [(T[lq][:, a:e].bitcast(dt.uint8), T[xq][:, a:e].bitcast(dt.uint8)), (T[lp][:, a:e], T[xs][:, a:e])],
             [(xq, a, e), (xs, a, e)], [(lq, a, e), (lp, a, e)])

    def sign_row(r, a, e):
        o = RB["sg_%d" % r][0]
        return spread("rb", o, a, e) if r > 1 else [(a, e, A("rb", o + a, o + e))]

    def signs(r, i):
        a, e = XRUN[i]
        mm(P("psA", i, 0, e - a), "u2", "s2", 0, "xq%d" % (r - 1), "xs%d" % (r - 1), a, e)
        for lo, hi, out in sign_row(r, a, e):
            act(out, P("psA", i, lo - a, hi - a), bias=-TINY, func=SIGN)

    def unpack(ps, q, s, a=0, e=C):
        for b in range(4):
            mm(P(ps, b, 0, e - a), "qe", "se", 128 * b, q, s, a, e)

    def halves(ps, dst, planes=range(4), a=0, e=C):
        for b in planes:
            for lo, hi, out in spread(dst, WIDE * b, a, e):
                act(out, P(ps, b, lo - a, hi - a), scale=0.5)

    pq, npq = N("rf", "pq"), N("rf", "npq")

    def hold(dst, src, n, o=ADD):
        scan(dst, N("rb", "cb", 0, n), src, 0.0, MUL, o)

    def held(src, dst, a=0, e=C):
        hold(N("rb", dst, a, e), N("rb", src, a, e), e - a)

    def listed(out, name, a=0, e=C):
        ts(out, ends(name, a, e), pq, MUL, 208.25, ADD)

    def shared(dst, win, lst, at, cut, scale=1.0, bias=0.0):
        if cut:
            ts(N("rb", dst, 0, cut), ind(win, part(lst, 0, cut, at)), scale, MUL, bias, ADD)
        act(N("rb", dst, cut, C), ind(win, part(lst, cut, C, at)), scale=scale, bias=bias)

    dma("y", "dnx", N("ri", "nx")[0], T.nx[:], [], N("ri", "nx")[1])
    dma("y", "du", T.uin[:], T.u[:], [], [("uin", 0, 512)])
    dma("y", "dx", T.xt0[:], T.x[:], [], [("xt0", 0, 4 * C)])
    dma("y", "dwc", T.wq[:].bitcast(dt.uint8), T.wc[:], [], [("wq", 0, 512)])
    dma("y", "dws", T.wp[:], T.ws[:], [], [("wp", 0, 512)])
    dma("y", "dv", T.vin[:], T.v[:], [], [("vin", 0, 512)])

    one = lambda n: A("one", 0, n)
    p16, m16 = N("rf", "p16"), N("rb", "m16")

    def constant(b):
        op("v", lambda: g.vector.quantize_mx(T.qe[:, 128 * b:128 * b + 128], T.se[:, 128 * b:128 * b + 128], T.et[:, 3 - b:515 - b]), [("et", 0, 515)], [("qe", 128 * b, 128 * b + 128), ("se", 128 * b, 128 * b + 128)])

    def bit_of_p(s):
        ts(N("ri", "bit", s, s + 1), N("ri", "p"), s, AluOpType.logical_shift_right, 1, AluOpType.bitwise_and)

    op("v", lambda: g.vector.memset(one(528)[0], 1.0), [], one(528)[1])
    op("g", lambda: g.iota(N("ri", "p")[0], [[0, 1]], 0, 1), [], N("ri", "p")[1])
    iota(N("rb", "i16"), [[1, 16]], 0)
    iota(N("rb", "i15"), [[1, 16]], -1)
    op("g", lambda: g.affine_select(T.et[:, 0:515], one(515)[0], [[1, 515]], EQ, 0.0, -3, -4), one(515)[1], [("et", 0, 515)])
    op("g", lambda: g.iota(N("ri", "pick")[0], [[16, 8]], 0, 0), [], N("ri", "pick")[1])
    iota(N("rf", "j16"), [[16, K]], 0)
    iota(N("rb", "i2"), [[2, C]], -C)
    ts(N("ri", "p16"), N("ri", "p"), 15, AluOpType.bitwise_and)
    scan(N("rb", "own"), one(C), one(C), -209.0, MUL, ADD)
    vcopy(p16, N("ri", "p16"))
    bit_of_p(0)
    bit_of_p(1)
    ts(N("rb", "tab"), N("rb", "i16"), p16, NE)
    ts(N("rf", "tabb"), N("rb", "i15"), p16, EQ, 65535.0, MUL)
    ts(N("ru", "same"), one(K), p16, MUL)
    bit_of_p(2)
    tt(N("rf", "tabb"), N("rf", "tabb"), N("rb", "tab"), ADD)
    bit_of_p(3)
    ts(N("rf", "p15"), p16, 15.0, EQ, 1.0 - 2.0 ** -16, MUL)
    vcopy(N("rf", "bit"), N("ri", "bit"))
    for s in (1, 2, 3):
        act(N("rb", "ds%d" % s, 1, 16), one(15))
    act(factor(0), one(K), scale=0.0)
    act(lane("fl", 0), one(K), scale=-1.0)
    act(lane("fl", 2), one(K), scale=0.0)
    act(m16, N("rb", "tab"), scale=-1.0, bias=1.0)
    act(N("rb", "cb"), ind(N("rf", "tabb"), N("ru", "same")))
    act(pq, N("rf", "p15"), bias=2.0 ** -16)
    constant(0)
    constant(1)

    W = lambda s, a=0, e=C: N("rb", "W%d" % s, a, e)
    vcopy(A("L0", 0, K), N("ri", "nx"))
    constant(2)
    shared("W1", N("rb", "own"), "L0", 0, 192)
    constant(3)
    shared("W2", W(1), "L0", 0, 192)
    ts(N("ru", "q1"), W(1, 0, 1), 208.0, ADD, N("rf", "bit", 0, 1), MUL)
    act(N("rf", "nb"), N("rf", "bit", 0, 1), scale=208.0, bias=-208.0)
    for s in (1, 2, 3):
        act(N("rb", "mb%d" % s), m16, scale=N("rf", "bit", s, s + 1))
        act(N("rb", "ds%d" % s, 0, 1), N("rf", "bit", s, s + 1), scale=-1.0, bias=1.0)
    act(N("rf", "fo0"), W(1, 0, 1), scale=N("rf", "bit", 0, 1), bias=N("rf", "nb"))
    for p, q, step, o in SPREAD:
        iota(N("rb", "name", p, q), [[-step, q - p]], -o - 1)

    def power(s, k, cut):
        shared("W%d" % s, W(s - k), "ru", RU["G%d" % k][0], cut)

    def as_list(s, step):
        if step == 0:
            held("W%d" % s, "S%d" % s)
        else:
            listed(N("ru", "G%d" % s), "S%d" % s)

    def bit(s, step):
        if step == 0:
            tt(N("rf", "og%d" % s), ind(W(2 ** s), N("ru", "q%d" % s)), N("rb", "mb%d" % s), MUL)
        if step == 1:
            scan(N("rf", "fo%d" % s), N("rb", "ds%d" % s), N("rf", "og%d" % s), N("rf", "fo%d" % (s - 1), 15, 16) if s > 1 else N("rf", "fo0"), MUL, ADD)
        if step == 2:
            ts(N("ru", "q%d" % (s + 1)) if s < 3 else N("ru", "OG0", 0, 1), N("rf", "fo%d" % s, 15, 16), 208.0, ADD)

    def more(s, a, e, step, by=vcopy):
        if step == 0:
            by(N("rb", "or", a + s, e + s), ind(W(s), N("ru", "OG0", a // 16, e // 16)))
        if step == 1:
            held("or", "os", a + s, e + s)
        if step == 2:
            listed(N("ru", "OG0", (a + s) // 16, (e + s) // 16), "os", a + s, e + s)

    def pick_u(scales):
        pk = N("ru", "pick")
        if scales:
            op("s", lambda: g.scalar.activation(T.s2[:, 0:128], T.su[:, 0:128].indirect(pk[0]), COPY), [("su", 0, 128)] + pk[1], [("s2", 0, 128)])
        else:
            op("v", lambda: g.vector.tensor_copy(T.u2[:, 0:128].bitcast(dt.uint32), T.qu[:, 0:128].bitcast(dt.uint32).indirect(pk[0])), [("qu", 0, 128)] + pk[1], [("u2", 0, 128)])

    def up_signs(r, a, e):
        for lo, hi, src in sign_row(r, a, e):
            hold(N("rb", "du_%d" % r, lo, hi), src, hi - lo)

    def leavers(r, step, out=None, cut=192):
        if step == 0:
            shared("uh_%d" % r, N("rb", "sg_%d" % r), "LN%d" % r, 0, cut, 0.5, -1.5)
        if step == 1:
            ts(factor(2), ends("du_%d" % r), 0.0, GT)
        if step == 2:
            hold(factor("row"), N("rb", "uh_%d" % r), C, MIN)
        if step == 3:
            scan(N("rf", "fx"), factor(None), lanes("fe"), 0.0, MUL, ADD)
        if step == 4:
            vcopy(out, N("rf", "fx", 2, 3 * K, 3))

    def places(a, e):
        scatter(N("rb", "P1"), N("ru", "OG0", a // 16, e // 16), N("rb", "i2", a, e))

    def plain():
        for p, q, step, o in SPREAD:
            iota(N("rf", "plain", o, o + step * (q - p)), [[1, q - p], [0, step]], p)

    as_list(2, 0)
    bit(1, 0)
    as_list(2, 1)
    power(4, 2, 0)
    power(6, 2, 0)
    scatter(N("rb", "w0"), A("L0", 0, K), N("rb", "own"))
    bit(1, 1)
    held("w0", "w0s")
    bit(1, 2)
    listed(A("L0", K, 2 * K), "w0s")
    send_hosts("L0", K, 1)
    power(8, 2, 128)
    act(npq, pq, scale=-1.0)
    act(N("rf", "nq"), N("rf", "p15"), scale=65536.0, bias=-65536.0)
    act(N("rf", "npq2"), pq, scale=npq)
    act(lane("fe", 2), N("rf", "j16"), bias=p16)
    act(lane("fl", 1), one(K), scale=N("rf", "nq"))
    bit(2, 0)
    as_list(8, 0)
    bit(2, 1)
    as_list(8, 1)
    power(16, 8, 0)
    vcopy(N("ru", "pick"), N("ri", "pick"))
    bit(2, 2)
    quant("xq0", "xs0", "xt0", 0, C, 0)
    send_state(1, 0, 0, C)
    iota(N("rb", "free"), [[0, 3 * S]], 1)
    iota(N("rb", "ones"), [[0, S]], 1)
    plain()
    unpack("psB", "xq0", "xs0")
    bit(3, 0)
    quant("qu", "su", "uin", 0, 128, 0)
    bit(3, 1)
    power(24, 8, 128)
    bit(3, 2)
    pick_u(0)
    more(16, 0, 16, 0, act)
    power(32, 8, 192)
    more(16, 0, 16, 1)
    as_list(32, 0)
    more(16, 0, 16, 2)
    as_list(32, 1)
    more(32, 0, 32, 0, vcopy)
    pick_u(1)
    power(64, 32, 160)
    more(32, 0, 32, 1)
    places(0, 32)
    more(32, 0, 32, 2)
    signs(1, 1)
    power(96, 32, 192)
    signs(1, 0)
    vcopy(N("rf", "h"), A("LN1", 0, K))
    more(64, 0, 64, 0, vcopy)
    more(96, 32, 64, 0, act)
    power(128, 32, 96)
    more(64, 0, 96, 1)
    up_signs(1, 0, C)
    more(64, 0, 96, 2)
    places(32, 64)
    more(128, 32, 160, 0, vcopy)
    leavers(1, 1)
    leavers(1, 0, cut=0)
    tt(N("rf", "d"), N("rf", "h"), lane("fe", 2), SUB)
    more(128, 32, 160, 1)
    places(64, 160)
    halves("psB", "th", (0,))
    act(lane("fe", 0), N("rf", "d"), scale=npq)
    more(128, 32, 160, 2)
    leavers(1, 2)
    act(lane("fe", 1), N("rf", "d"), scale=-1.0)
    more(128, 160, 288, 0, act)
    places(160, 288)
    more(128, 160, 288, 1)
    halves("psB", "th", (1, 2))
    leavers(1, 3)
    more(128, 160, 288, 2)
    leavers(1, 4, N("ru", "y"))
    places(288, C)
    shared("PY", N("rb", "P1"), "ru", RU["y"][0], 192)
    scan(N("rf", "fy"), factor(None), lanes("fl"), 0.0, MUL, ADD)
    halves("psB", "th", (3,))
    held("PY", "PYs")
    tt(N("rf", "xl"), ends("PYs"), N("rf", "fy", 2, 3 * K, 3), ADD)
    ts(N("ru", "x_1"), N("rf", "xl"), pq, MUL, C + 0.25, ADD)

    for r in (1, 2, 3):
        LA, LB = "LA%d" % r, "LB%d" % r
        nb = lambda k, a=0, b=C: N("rb", "%s_%d" % (k, r), a, b)
        zt, xt, zq, zs, xq, xs, lq, lp = ["%s%d" % (k, r) for k in ("zt", "xt", "zq", "zs", "xq", "xs", "lq", "lp")]
        xat = RU["x_%d" % r][0]
        slot = lambda a, e, step=1: N("rb", "free", S * (r - 1) + a, S * (r - 1) + e, step)
        down = lambda hi, lo, step=1: back("free", S * (r - 1) + hi, S * (r - 1) + lo, step)
        if r > 1:
            leavers(r, 0)
            act(lane("fe", 0), N("rf", "d"), scale=N("rf", "npq2"), bias=npq)
            act(lane("fe", 1), N("rf", "d"), scale=npq, bias=-1.0)
            up_signs(r, SPREAD[2][0], C)
            leavers(r, 2)
            leavers(r, 1)
            halves("psB", "th", range(r + 1))
            for step in (3, 4):
                leavers(r, step, N("ru", "x_%d" % r))
            unpack("psA", lq, lp, 0, EARLY)
            halves("psA", "tp", range(4), 0, EARLY)
        else:
            unpack("psA", lq, lp)
            halves("psA", "tp")
        scatter(slot(0, S), N("ru", "x_%d" % r), N("rb", "name"))
        FW, BW = "FW_%d" % r, "BW_%d" % r
        scan(nb("FW", FW0 - C - 1, FW0 + 1), slot(C - 2, S), slot(C - 2, S), -1.0, MUL, MIN)
        scan(back(BW, S + C // 2 - 1, S - 1), down(C, 0, 2), down(C, 0, 2), -1.0, MUL, MIN)
        scan(nb("FW", FW0 + 1, FW0 + S), slot(0, S - 1), slot(0, S - 1), nb("FW", FW0, FW0 + 1), MUL, MIN)
        scan(back(BW, S - 2, 0), down(S - 1, 1), down(S - 1, 1), nb("BW", S - 1, S), MUL, MIN)
        if r < 3:
            act(nb("full", 0, S), slot(0, S), scale=-1.0, func=SIGN)
        act(nb("br"), ind(nb("FW", FW0, FW0 + S), N("ru", "x_%d" % r)))

        def named(k, out, step):
            if step == 0:
                hold(nb(k + "s"), nb(k + "r"), C, MIN)
            else:
                ts(A(out, 0, K), ends("%ss_%d" % (k, r)), npq, MUL, -1.0, ADD)

        vcopy(nb("ar", 0, 192), ind(nb("BW", 0, S), part("ru", 0, 192, xat)))
        act(nb("ar", 256, C), ind(nb("BW", 0, S), part("ru", 256, C, xat)))
        named("b", LB, 0)
        vcopy(nb("ar", 192, 256), ind(nb("BW", 0, S), part("ru", 192, 256, xat)))
        named("b", LB, 1)
        send_ring("B", r)
        named("a", LA, 0)
        named("a", LA, 1)
        send_ring("A", r)
        if r < 3:
            send_hosts(LB, 0, r + 1)

        PR, Ps, hf, hs = ["%s_%d" % (k, r) for k in ("PR", "Ps", "hf", "hs")]
        if r == 2:
            halves("psB", "th", (3,))
        if r > 1:
            unpack("psB", lq, lp, EARLY, C)
            halves("psB", "tp", range(4), EARLY, C)

        def predecessors(by, b, a=0, e=C):
            by(plane("tb", b, a, e), ind(wide("th", b), part(LB, a, e)))

        for b in range(4):
            who = [TB[r][i][b] for i in (0, 1)]
            for w, (a, e) in ([(who[0], (0, C))] if who[0] == who[1] else zip(who, XRUN)):
                if w in "vs":
                    predecessors(vcopy if w == "v" else act, b, a, e)
            if r < 3 and b == 0:
                scan(nb("CN", 0, S), nb("full", 0, S), N("rb", "ones"), -2.0 - C, ADD, ADD)
        pieces = spread("rb", RB[PR][0], 0, C) if r < 3 else []
        for lo, hi, out in pieces:
            vcopy(out, ind(nb("CN", 0, S), part("ru", lo, hi, xat)))

        def behind(w):
            for i in (0, 1):
                for b in range(4):
                    if TB[r][i][b] == w:
                        predecessors(act, b, *XRUN[i])

        def pack_z(i):
            a, e = ZRUN[i]
            quant(zq, zs, zt, a, e)
            for b in range(4):
                mm(P("psB" if i else "psA", b, 0, e - a), "wq", "wp", 128 * b, zq, zs, a, e)

        def layer(i, b):
            a, e = ZRUN[i]
            for lo, hi, out in spread("hh", WIDE * b, a, e):
                act(out, P("psB" if i else "psA", b, lo - a, hi - a), scale=0.015625)

        for i, (a, e) in enumerate(ZRUN):
            for b in range(4):
                act(plane("za", b, a, e), ind(wide("tp", b), part("RB%d" % r, a, e)))
                tt(strip(zt, b, a, e), ind(wide("tp", b), part("RA%d" % r, a, e)), plane("za", b, a, e), ADD)
                if i and not b:
                    pack_z(i - 1)
        behind("m")
        layer(0, 0)
        pack_z(1)
        for lo, hi, out in pieces:
            hold(N("rb", Ps, lo, hi), out, hi - lo)
        if r == 3:
            quant("qv", "sv", "vin", 0, 128, 0)
        for i, b in ((1, 0), (0, 1), (1, 1), (0, 2), (1, 2), (0, 3), (1, 3)):
            layer(i, b)
        behind("l")
        if r < 3:
            act(N("rb", hf), ind(N("rb", PR), A("LN%d" % (r + 1), 0, K)))
            act(lane("fe", 2), ends(Ps), scale=pq, bias=C + 0.25)
        else:
            act(N("rf", "nr"), ind(N("rf", "plain", 0, WIDE), A(LA, 0, K)))
            dma("y", "dout", T.nr[:, :], T.rf[0:128:16, RF["nr"][0]:RF["nr"][0] + C], N("rf", "nr")[1], [])

        def pack_x(i):
            a, e = XRUN[i]
            quant(xq, xs, xt, a, e)
            if r < 3:
                for k, (lo, hi) in enumerate([(a, e)] if i else [(a, EARLY), (EARLY, e)]):
                    send_state(r + 1, 2 * i + k, lo, hi)
                signs(r + 1, i)
            else:
                mm(P("psA", i, 0, e - a), "qv", "sv", 0, xq, xs, a, e)
                dma("y", "dout", T.oc[:, 4 * a:4 * e], T[xq][:, a:e].bitcast(dt.uint8), [(xq, a, e)], [])
                for k in range(4 * i):
                    dma("s" if k > 1 else "y", "dout", T.osc[4 * k:4 * k + 4, 0:C], T[xs][32 * k:32 * k + 4, 0:C], [(xs, 0, C)], [])
                (vcopy if i else act)(A("yo", a, e), P("psA", i, 0, e - a))
                dma("s", "dout", T.y[:, a:e], T.yo[:, a:e], [("yo", a, e)], [])

        for i, (a, e) in enumerate(XRUN):
            for b in range(4):
                tt(strip(xt, b, a, e), ind(wide("hh", b), part(LA, a, e)), plane("tb", b, a, e), ADD)
                if (i, b) == (1, 0):
                    pack_x(0)
        pack_x(1)
        if r < 3:
            unpack("psB", xq, xs)
            held(hf, hs)
            up_signs(r + 1, 0, SPREAD[2][0])
            tt(N("rf", "d"), ends(hs), ends(Ps), SUB)

    for sem in sorted(total, key=lambda k: (k == "dout", k in ("cv", "cs", "ct"), k)):
        g.wait_ge(T.sem[sem], total[sem])
